import numpy as np
import ml_dtypes


def mxq(x, axis, fmt="e4m3"):
    dtype, down = {"e4m3": (ml_dtypes.float8_e4m3fn, 7), "e5m2": (ml_dtypes.float8_e5m2, 14)}[fmt]
    v = np.moveaxis(np.asarray(x, np.float32).astype(ml_dtypes.bfloat16).astype(np.float64), axis, -1)
    blocks = v.reshape(v.shape[:-1] + (-1, 32))
    amax = np.abs(blocks).max(-1, keepdims=True)
    byte = np.maximum(np.where(amax > 0, np.frexp(amax)[1] - 1 + 127, 0) - down, 1)
    scale = np.exp2(byte - 127.0)
    codes = (blocks / scale).astype(np.float32).astype(dtype).astype(np.float64)
    return np.moveaxis((codes * scale).reshape(v.shape), -1, axis)


WIDE = False


def mx_kscale(k):
    if not WIDE:
        return np.ones(k)
    levels = np.array([30, -30])
    if k % 512:
        return np.exp2(np.random.permutation(np.resize(levels, k // 32))).repeat(32)
    a = np.empty((k // 512, 16))
    for p in range(k // 512):
        a[p, :8] = np.random.permutation(np.resize(levels, 8))
        for g in range(8):
            far = levels[np.abs(levels - a[p, g]) >= 10]
            a[p, g + 8] = far[np.random.randint(len(far))]
    return np.exp2(a.ravel()).repeat(32)


def f64(x):
    return np.asarray(x).astype(np.float64)


def striped(idx):
    return np.tile(idx.reshape(-1, 16).T, (8, 1)).astype(np.uint16)


def unstriped(offs):
    return offs[:16].T.reshape(-1).astype(np.int64)


def bf(x):
    return np.asarray(x, np.float32).astype(ml_dtypes.bfloat16)


E2M1 = np.array([0.0, 0.5, 1.0, 1.5, 2.0, 3.0, 4.0, 6.0, -0.0, -0.5, -1.0, -1.5, -2.0, -3.0, -4.0, -6.0])


def pack_weight(w, fmt):
    k, n = w.shape
    w = f64(bf(w)).reshape(k // 32, 32, n)
    amax = np.abs(w).max(1)
    if fmt in ("e4m3", "e5m2"):
        byte = np.frexp(amax)[1] - 1 + 127 - (7 if fmt == "e4m3" else 14)
    else:
        mant, ex = np.frexp(amax / 6.0)
        byte = np.where(mant > 0.5, ex, ex - 1) + 127
    byte = np.clip(np.where(amax > 0, byte, 1), 1, 254)
    scaled = (w * np.exp2(127.0 - byte)[:, None, :]).reshape(k, n).astype(np.float32)
    by_word = np.ascontiguousarray(scaled.reshape(k // 512, 128, 4, n).transpose(0, 1, 3, 2))
    if fmt in ("e4m3", "e5m2"):
        words = by_word.astype(ml_dtypes.float8_e4m3fn if fmt == "e4m3" else ml_dtypes.float8_e5m2).view(np.uint8)
    else:
        c = by_word.astype(ml_dtypes.float4_e2m1fn).view(np.uint8) & 0xF
        words = c[..., 0::2] | (c[..., 1::2] << 4)
    return np.ascontiguousarray(words), np.ascontiguousarray(byte.astype(np.uint8).reshape(k // 512, 16, n))


def unpack_weight(words, scales, fmt):
    g, p, n, _ = words.shape
    if fmt in ("e4m3", "e5m2"):
        vals = np.ascontiguousarray(words).view(ml_dtypes.float8_e4m3fn if fmt == "e4m3" else ml_dtypes.float8_e5m2).astype(np.float64)
    else:
        nib = np.empty((g, p, n, 4), np.uint8)
        nib[..., 0::2] = words & 0xF
        nib[..., 1::2] = words >> 4
        vals = E2M1[nib]
    vals = vals * np.repeat(np.exp2(scales.astype(np.float64) - 127.0), 8, axis=1)[..., None]
    return vals.transpose(0, 1, 3, 2).reshape(g * 512, n)


def planes(Y):
    n, m = Y.shape
    b = f64(bf(Y)).reshape(n // 32, 32, m)
    amax = np.abs(b).max(1)
    byte = np.clip(np.where(amax > 0, np.frexp(amax)[1] - 1 + 127 - 7, 1), 1, 254)
    codes = (b * np.exp2(127.0 - byte)[:, None, :]).reshape(n, m).astype(np.float32).astype(ml_dtypes.float8_e4m3fn).view(np.uint8)
    words = codes.reshape(n // 512, 128, 4, m).transpose(0, 1, 3, 2)
    return np.ascontiguousarray(words), np.ascontiguousarray(byte.astype(np.uint8).reshape(n // 512, 16, m))


K, H, N, T, S, T2 = 512, 1024, 512, 2048, 1024, 2048

def setup_inputs():
    n = np.random.standard_normal
    s = mx_kscale(K)[:, None]
    u = mx_kscale(H)[:, None]
    tab = n((K, T)) * np.exp(1.0 * n((1, T))) * s
    tab_words, tab_scales = pack_weight(tab, "e5m2")
    w1 = 4.0 * n((K, H)) / np.sqrt(K) / s * u.T
    wr = 3.0 * n((H, H)) / np.sqrt(H) / u * u.T
    wr_words, wr_scales = pack_weight(wr, "e4m3")
    wo = n((H, N)) * np.exp(0.8 * n((1, N))) / np.sqrt(H) / u
    sT = 1.0 / (1.0 + np.exp(-n((H, T))))
    wgo = np.exp(0.3 * n((128, S)))
    return {"tab_words": tab_words, "tab_scales": tab_scales,
            "offs": striped(np.random.permutation(T)[:S]),
            "offs2": striped(np.random.permutation(T2)[:S]),
            "sT": sT.astype(np.float32), "w1": w1.astype(np.float32),
            "wr_words": wr_words, "wr_scales": wr_scales,
            "wo": wo.astype(np.float32), "wgo": wgo.astype(np.float32)}

def reference(tab_words, tab_scales, offs, offs2, sT, w1, wr_words, wr_scales, wo, wgo):
    v = unpack_weight(tab_words, tab_scales, "e5m2")[:, unstriped(offs)]
    s_ = f64(sT)[:, unstriped(offs)]
    d = s_ * (1.0 - s_)
    h = mxq(f64(w1), 0, "e4m3").T @ v
    g = d * h
    wr = unpack_weight(wr_words, wr_scales, "e4m3")
    rec = wr.T @ mxq(g, 0, "e4m3")
    b = g + d * rec
    e = mxq(f64(wo), 0, "e4m3").T @ mxq(b, 0, "e4m3")
    y = np.zeros((N, T2))
    y[:, unstriped(offs2)] = np.tile(f64(wgo), (N // 128, 1)) * e
    words, scales = planes(y)
    return y, words, scales

@@ -1,0 +1,303 @@
+from contextlib import ExitStack
+
+import concourse.mybir as mybir
+
+K, H, N, T, S, T2 = 512, 1024, 512, 2048, 1024, 2048
+FLOPS = 2 * S * (K * H + H * H + H * N)
+
+F32 = mybir.dt.float32
+BF16 = mybir.dt.bfloat16
+I32 = mybir.dt.int32
+U32 = mybir.dt.uint32
+U16 = mybir.dt.uint16
+U8 = mybir.dt.uint8
+E4M3 = mybir.dt.float8_e4m3fn_x4
+E5M2 = mybir.dt.float8_e5m2_x4
+MULT = mybir.AluOpType.mult
+ADD = mybir.AluOpType.add
+SUBTRACT = mybir.AluOpType.subtract
+
+P = 128
+PACK = 4
+PASS = P * PACK
+HALF = 512
+HALVES = S // HALF
+GROUPS = H // PASS
+CHUNK = 256
+SCALAR_CHUNKS = (0, 2, 4, 6)
+
+
+def tile_list_dislocation_recurrent_backward_kernel(
+    tc, tab_words, tab_scales, offs, offs2, sT, w1, wr_words, wr_scales, wo, wgo, out_0, out_1, out_2
+):
+    nc = tc.nc
+    with ExitStack() as ctx:
+        keep = ctx.enter_context(tc.tile_pool(name="keep", bufs=1))
+        work = ctx.enter_context(tc.tile_pool(name="work", bufs=1))
+        psum = ctx.enter_context(tc.psum_pool(name="psum", bufs=1))
+
+        def stream(shape, dtype, name):
+            return work.tile(shape, dtype, name=name, tag="stream", bufs=5)
+
+        def staging(shape, dtype, name):
+            return work.tile(shape, dtype, name=name, tag="staging", bufs=2)
+
+        def woven(name):
+            return work.tile([P, PACK * HALF], BF16, name=name, tag="woven", bufs=4, align_bytes=64)
+
+        def operand(name, tag, bufs):
+            codes = work.tile([P, HALF], U32, name=name + "_codes", tag=tag + "_codes", bufs=bufs, align_bytes=64)
+            scales = work.tile([P, HALF], U8, name=name + "_scales", tag=tag + "_scales", bufs=bufs, align_bytes=64)
+            return codes, scales
+
+        def quantize(src, name, tag, bufs):
+            codes, scales = operand(name, tag, bufs)
+            nc.vector.quantize_mx(out=codes[:].bitcast(E4M3), scales=scales[:], in_=src[:])
+            return codes, scales
+
+        def weave_weight(raw, name):
+            dst = woven(name)
+            nc.scalar.copy(
+                out=dst[:].rearrange("p (t m i) -> p m i t", t=PACK, i=PACK),
+                in_=raw[:].rearrange("p i (m t) -> p m i t", t=PACK),
+            )
+            return dst
+
+        def weave(src, dst):
+            nc.scalar.copy(
+                out=dst[:].rearrange("p (c i t) -> p c t i", t=PACK, i=4),
+                in_=src[:].rearrange("p t (c i) -> p c t i", i=4),
+            )
+            return dst
+
+        gather_list = keep.tile([P, S // 16], U16, name="gather_list")
+        scatter_list = keep.tile([P, S // 16], U16, name="scatter_list")
+        tab_w = keep.tile([P, T], U32, name="tab_w", align_bytes=64)
+        tab_s = keep.tile([P, T], U8, name="tab_s", align_bytes=64)
+        wr_s_raw = keep.tile([P, H], U8, name="wr_s_raw", align_bytes=64)
+        wr_s = keep.tile([P, H], U8, name="wr_s", align_bytes=64)
+        wr_w = keep.tile([P, GROUPS * H], I32, name="wr_w", align_bytes=64)
+        pages = [keep.tile([P, T2], F32, name=f"page{t}") for t in range(PACK)]
+        y_codes = keep.tile([P, T2], U32, name="y_codes", align_bytes=64)
+        y_scales = keep.tile([P, T2], U8, name="y_scales", align_bytes=64)
+
+        nc.vector.memset(tab_s[:].bitcast(I32), 0)
+        nc.vector.memset(wr_s_raw[:].bitcast(I32), 0)
+        for page in pages:
+            nc.vector.memset(page[:], 0.0)
+
+        s_rows = sT.rearrange("(a p t) c -> a t p c", p=P, t=PACK)
+        s_tiles = {}
+
+        def load_state(a, t):
+            s_tiles[a, t] = stream([P, T], F32, f"s{a}{t}")
+            nc.sync.dma_start(out=s_tiles[a, t][:], in_=s_rows[a, t])
+
+        def load_weight(rows, name):
+            raw = staging([P, PACK, HALF], F32, name)
+            nc.sync.dma_start(out=raw[:], in_=rows.rearrange("(p i) c -> p i c", i=PACK))
+            return raw
+
+        nc.sync.dma_start(gather_list[:], offs)
+        load_state(0, 0)
+        nc.sync.dma_start(out=tab_w[:].bitcast(I32), in_=tab_words[0].rearrange("p t i -> p (t i)").bitcast(I32))
+        for q in range(4):
+            nc.sync.dma_start(
+                out=tab_s[32 * q : 32 * q + 4, :].bitcast(I32), in_=tab_scales[0, 4 * q : 4 * q + 4, :].bitcast(I32)
+            )
+        w1_raw = [load_weight(w1[:, 0:PASS], "w1_raw0")]
+        load_state(0, 1)
+        load_state(0, 2)
+        load_state(0, 3)
+        w1_raw.append(load_weight(w1[:, PASS : 2 * PASS], "w1_raw1"))
+        load_state(1, 0)
+        nc.sync.dma_start(scatter_list[:], offs2)
+        for q in range(4):
+            nc.sync.dma_start(
+                out=wr_s_raw[32 * q : 32 * q + 4 * GROUPS, :].bitcast(I32),
+                in_=wr_scales[:, 4 * q : 4 * q + 4, :].bitcast(I32),
+            )
+        wr_w_raw = stream([P, GROUPS, H], I32, "wr_w_raw")
+        nc.sync.dma_start(out=wr_w_raw[:], in_=wr_words.rearrange("a p c i -> p a (c i)").bitcast(I32))
+        load_state(1, 1)
+        load_state(1, 2)
+        load_state(1, 3)
+        wo_raw = [load_weight(wo[PASS * a : PASS * (a + 1), :], f"wo_raw{a}") for a in range(GROUPS)]
+        wgo_rows = wgo.rearrange("(q t) j -> q t j", t=PACK)
+        wgo_tiles = []
+        for u in range(2):
+            rows = stream([P, 2, S], F32, f"wgo{u}")
+            for c in range(4):
+                nc.sync.dma_start(out=rows[32 * c : 32 * c + 32], in_=wgo_rows[:, 2 * u : 2 * u + 2, :])
+            wgo_tiles.append(rows)
+
+        def entries(lst, j):
+            return lst[:, j * (HALF // 16) : (j + 1) * (HALF // 16)]
+
+        neg_d = {}
+        g32 = {}
+        g_woven = {}
+        v_w = {}
+        v_s = {}
+        w1_q = {}
+
+        def derivative(a, t, j):
+            d = work.tile([P, HALF], F32, name=f"d{a}{t}{j}", tag=f"d{j}", bufs=GROUPS * PACK)
+            nc.vector.tensor_copy(d[:], s_tiles[a, t][:].indirect(entries(gather_list, j)))
+            neg_d[a, t, j] = d
+
+        def finish_derivative(a, t, j):
+            d = neg_d[a, t, j]
+            nc.vector.scalar_tensor_tensor(out=d[:], in0=d[:], scalar=1.0, in1=d[:], op0=SUBTRACT, op1=MULT)
+
+        def first_product(bank, a, t, j, stop):
+            cols = slice(P * t, P * (t + 1))
+            nc.tensor.matmul_mx(
+                out=bank[:], lhsT=w1_q[a][0][:, cols].bitcast(E4M3), lhsT_scale=w1_q[a][1][:, cols],
+                rhs=v_w[j][:].bitcast(E5M2), rhs_scale=v_s[j][:], start=True, stop=stop,
+            )
+
+        def repeats_first_product(b, t):
+            return b == GROUPS - 1 and t > 0
+
+        def gate(a, t, j):
+            h = psum.tile([P, HALF], F32, name=f"h{a}{t}{j}", tag="h", bufs=3)
+            first_product(h, a, t, j, stop=True)
+            nc.vector.scalar_tensor_tensor(
+                out=g32[a, j][:, t, :], in0=h[:], scalar=-1.0, in1=neg_d[a, t, j][:], op0=MULT, op1=MULT
+            )
+
+        for a in range(GROUPS):
+            for j in range(HALVES):
+                g32[a, j] = keep.tile([P, PACK, HALF], F32, name=f"g{a}{j}")
+
+        for j in range(HALVES):
+            derivative(0, 0, j)
+        for j in range(HALVES):
+            finish_derivative(0, 0, j)
+        for j in range(HALVES):
+            v_w[j] = keep.tile([P, HALF], U32, name=f"v_w{j}", align_bytes=64)
+            v_s[j] = keep.tile([P, HALF], U8, name=f"v_s{j}", align_bytes=64)
+            nc.vector.tensor_copy(v_w[j][:], tab_w[:].indirect(entries(gather_list, j)))
+            nc.vector.tensor_copy(v_s[j][:], tab_s[:].indirect(entries(gather_list, j)))
+        for a in range(GROUPS):
+            w1_q[a] = quantize(weave_weight(w1_raw[a], f"w1_woven{a}"), f"w1_{a}", "w1", GROUPS)
+            for t in range(PACK):
+                if (a, t) != (0, 0):
+                    for j in range(HALVES):
+                        derivative(a, t, j)
+                    for j in range(HALVES):
+                        finish_derivative(a, t, j)
+                for j in range(HALVES):
+                    gate(a, t, j)
+            for j in range(HALVES):
+                g_woven[a, j] = weave(g32[a, j], woven(f"g_woven{a}{j}"))
+
+        g_q = {}
+        for j in range(HALVES):
+            for a in range(GROUPS):
+                g_q[a, j] = quantize(g_woven[a, j], f"g_{a}{j}", f"act{j}", GROUPS)
+
+        for a in range(GROUPS):
+            nc.vector.tensor_copy(
+                out=wr_w[:, H * a : H * (a + 1)].rearrange("p (b t q) -> p b q t", t=PACK, q=P),
+                in_=wr_w_raw[:, a, :].rearrange("p (b q t) -> p b q t", t=PACK, q=P),
+            )
+        nc.vector.tensor_copy(
+            out=wr_s[:].rearrange("p (b t q) -> p b q t", t=PACK, q=P),
+            in_=wr_s_raw[:].rearrange("p (b q t) -> p b q t", t=PACK, q=P),
+        )
+        wo_q = [quantize(weave_weight(wo_raw[a], f"wo_woven{a}"), f"wo_{a}", "wo", GROUPS) for a in range(GROUPS)]
+
+        def recurrent(b, j, dst):
+            for t in range(PACK):
+                rec = psum.tile([P, HALF], F32, name=f"rec{b}{t}{j}", tag="rec", bufs=3)
+                c0 = PASS * b + P * t
+                again = repeats_first_product(b, t)
+                if again:
+                    first_product(rec, b, t, j, stop=False)
+                for a in range(GROUPS):
+                    nc.tensor.matmul_mx(
+                        out=rec[:], lhsT=wr_w[:, H * a + c0 : H * a + c0 + P].bitcast(E4M3),
+                        lhsT_scale=wr_s[4 * a : P, c0 : c0 + P],
+                        rhs=g_q[a, j][0][:].bitcast(E4M3), rhs_scale=g_q[a, j][1][:],
+                        start=(a == 0 and not again), stop=(a == GROUPS - 1),
+                    )
+                d = neg_d[b, t, j]
+                dst32 = g32[b, j][:, t, :] if again else d[:]
+                nc.vector.scalar_tensor_tensor(out=dst32, in0=rec[:], scalar=-1.0, in1=d[:], op0=MULT, op1=MULT)
+            for t in range(PACK):
+                if not repeats_first_product(b, t):
+                    nc.vector.tensor_tensor(g32[b, j][:, t, :], g32[b, j][:, t, :], neg_d[b, t, j][:], ADD)
+            return weave(g32[b, j], dst)
+
+        b_q = {}
+        e32 = {}
+
+        def output_product(t, j, dst):
+            e = psum.tile([P, HALF], F32, name=f"e{t}{j}", tag="e", bufs=2)
+            cols = slice(P * t, P * (t + 1))
+            for b in range(GROUPS):
+                nc.tensor.matmul_mx(
+                    out=e[:], lhsT=wo_q[b][0][:, cols].bitcast(E4M3), lhsT_scale=wo_q[b][1][:, cols],
+                    rhs=b_q[b, j][0][:].bitcast(E4M3), rhs_scale=b_q[b, j][1][:],
+                    start=(b == 0), stop=(b == GROUPS - 1),
+                )
+            nc.scalar.copy(out=dst, in_=e[:])
+            e32[t, j] = dst
+
+        def e_tile(t, j):
+            return work.tile([P, HALF], F32, name=f"e32_{t}{j}", tag="d0", bufs=GROUPS * PACK)[:]
+
+        for b in range(GROUPS):
+            b_q[b, 0] = quantize(recurrent(b, 0, woven(f"b_woven{b}0")), f"b_{b}0", "act0", GROUPS)
+        for t in range(2):
+            output_product(t, 0, e_tile(t, 0))
+        b_q[0, 1] = quantize(recurrent(0, 1, woven("b_woven01")), "b_01", "act1", GROUPS)
+        last_woven = work.tile([P, PACK * HALF], BF16, name="b_woven11", tag="late", bufs=1, align_bytes=64)
+        b_q[1, 1] = quantize(recurrent(1, 1, last_woven), "b_11", "act1", GROUPS)
+        held = work.tile([P, 2, HALF], F32, name="e32_held", tag="late", bufs=1, align_bytes=64)
+        for t in range(2, PACK):
+            output_product(t, 0, held[:, t - 2, :])
+        for t in range(PACK):
+            output_product(t, 1, e_tile(t, 1))
+
+        y_rows = out_0.rearrange("(p t) m -> t p m", t=PACK)
+        y16 = [staging([P, PACK, T2 // 2], BF16, f"y16_{u}") for u in range(2)]
+        for j in range(HALVES):
+            for t in range(PACK):
+                nc.vector.tensor_tensor(
+                    pages[t][:].indirect(entries(scatter_list, j)), e32[t, j],
+                    wgo_tiles[t // 2][:, t % 2, HALF * j : HALF * (j + 1)], MULT,
+                )
+                if j == HALVES - 1:
+                    nc.sync.dma_start(out=y_rows[t], in_=pages[t][:])
+                    if t < PACK - 1:
+                        for u in range(2):
+                            nc.scalar.copy(out=y16[u][:, t, :], in_=pages[t][:, u * (T2 // 2) : (u + 1) * (T2 // 2)])
+
+        words_out = out_1[0].rearrange("p m t -> p (m t)").bitcast(I32)
+        per_half = T2 // 2 // CHUNK
+        y_woven = {}
+        for c in range(T2 // CHUNK):
+            u, c0 = c // per_half, (c % per_half) * CHUNK
+            copy = nc.scalar.copy if c in SCALAR_CHUNKS else nc.vector.tensor_copy
+            copy(out=y16[u][:, PACK - 1, c0 : c0 + CHUNK], in_=pages[PACK - 1][:, c * CHUNK : (c + 1) * CHUNK])
+            if c % 2 == 0:
+                pair = woven(f"y_woven{c}")
+            y_woven[c] = pair[:, (c % 2) * PACK * CHUNK : (c % 2 + 1) * PACK * CHUNK]
+            copy(
+                out=y_woven[c].rearrange("p (c i t) -> p c t i", t=PACK, i=4),
+                in_=y16[u][:, :, c0 : c0 + CHUNK].rearrange("p t (c i) -> p c t i", i=4),
+            )
+        for c in range(T2 // CHUNK):
+            cols = slice(c * CHUNK, (c + 1) * CHUNK)
+            nc.vector.quantize_mx(out=y_codes[:, cols].bitcast(E4M3), scales=y_scales[:, cols], in_=y_woven[c])
+            if c % 2 == 1:
+                both = slice((c - 1) * CHUNK, (c + 1) * CHUNK)
+                nc.sync.dma_start(out=words_out[:, both], in_=y_codes[:, both].bitcast(I32))
+        for q in range(4):
+            queue = nc.sync if q % 2 == 0 else nc.scalar
+            queue.dma_start(
+                out=out_2[0, 4 * q : 4 * q + 4, :].bitcast(I32), in_=y_scales[32 * q : 32 * q + 4, :].bitcast(I32)
+            )

@@ -24,7 +24,6 @@ HALF = 512
 HALVES = S // HALF
 GROUPS = H // PASS
 CHUNK = 256
-SCALAR_CHUNKS = (0, 2, 4, 6)
 
 
 def tile_list_dislocation_recurrent_backward_kernel(
@@ -36,8 +35,8 @@ def tile_list_dislocation_recurrent_backward_kernel(
         work = ctx.enter_context(tc.tile_pool(name="work", bufs=1))
         psum = ctx.enter_context(tc.psum_pool(name="psum", bufs=1))
 
-        def stream(shape, dtype, name):
-            return work.tile(shape, dtype, name=name, tag="stream", bufs=5)
+        def in_slot(slot, shape, dtype, name):
+            return work.tile(shape, dtype, name=name, tag=f"slot{slot[0]}{slot[1]}", bufs=1, align_bytes=64)
 
         def staging(shape, dtype, name):
             return work.tile(shape, dtype, name=name, tag="staging", bufs=2)
@@ -74,8 +73,8 @@ def tile_list_dislocation_recurrent_backward_kernel(
         scatter_list = keep.tile([P, S // 16], U16, name="scatter_list")
         tab_w = keep.tile([P, T], U32, name="tab_w", align_bytes=64)
         tab_s = keep.tile([P, T], U8, name="tab_s", align_bytes=64)
-        wr_s_raw = keep.tile([P, H], U8, name="wr_s_raw", align_bytes=64)
-        wr_s = keep.tile([P, H], U8, name="wr_s", align_bytes=64)
+        wr_s_raw = keep.tile([P, PASS], U8, name="wr_s_raw", align_bytes=64)
+        wr_s = keep.tile([P, PASS], U8, name="wr_s", align_bytes=64)
         wr_w = keep.tile([P, GROUPS * H], I32, name="wr_w", align_bytes=64)
         pages = [keep.tile([P, T2], F32, name=f"page{t}") for t in range(PACK)]
         y_codes = keep.tile([P, T2], U32, name="y_codes", align_bytes=64)
@@ -90,7 +89,7 @@ def tile_list_dislocation_recurrent_backward_kernel(
         s_tiles = {}
 
         def load_state(a, t):
-            s_tiles[a, t] = stream([P, T], F32, f"s{a}{t}")
+            s_tiles[a, t] = in_slot((a, t), [P, T], F32, f"s{a}{t}")
             nc.sync.dma_start(out=s_tiles[a, t][:], in_=s_rows[a, t])
 
         def load_weight(rows, name):
@@ -100,36 +99,30 @@ def tile_list_dislocation_recurrent_backward_kernel(
 
         nc.sync.dma_start(gather_list[:], offs)
         load_state(0, 0)
+        load_state(0, 1)
         nc.sync.dma_start(out=tab_w[:].bitcast(I32), in_=tab_words[0].rearrange("p t i -> p (t i)").bitcast(I32))
         for q in range(4):
             nc.sync.dma_start(
                 out=tab_s[32 * q : 32 * q + 4, :].bitcast(I32), in_=tab_scales[0, 4 * q : 4 * q + 4, :].bitcast(I32)
             )
         w1_raw = [load_weight(w1[:, 0:PASS], "w1_raw0")]
-        load_state(0, 1)
         load_state(0, 2)
         load_state(0, 3)
-        w1_raw.append(load_weight(w1[:, PASS : 2 * PASS], "w1_raw1"))
         load_state(1, 0)
-        nc.sync.dma_start(scatter_list[:], offs2)
-        for q in range(4):
-            nc.sync.dma_start(
-                out=wr_s_raw[32 * q : 32 * q + 4 * GROUPS, :].bitcast(I32),
-                in_=wr_scales[:, 4 * q : 4 * q + 4, :].bitcast(I32),
-            )
-        wr_w_raw = stream([P, GROUPS, H], I32, "wr_w_raw")
-        nc.sync.dma_start(out=wr_w_raw[:], in_=wr_words.rearrange("a p c i -> p a (c i)").bitcast(I32))
+        w1_raw.append(load_weight(w1[:, PASS : 2 * PASS], "w1_raw1"))
         load_state(1, 1)
         load_state(1, 2)
         load_state(1, 3)
+        nc.sync.dma_start(scatter_list[:], offs2)
+        for a in range(GROUPS):
+            for q in range(4):
+                nc.sync.dma_start(
+                    out=wr_s_raw[32 * q + 8 * a : 32 * q + 8 * a + 8, :].bitcast(I32),
+                    in_=wr_scales[a, 4 * q : 4 * q + 4, :].bitcast(I32).rearrange("r (b c) -> b r c", b=GROUPS),
+                )
+        wr_w_raw = keep.tile([P, GROUPS, H], I32, name="wr_w_raw")
+        nc.sync.dma_start(out=wr_w_raw[:], in_=wr_words.rearrange("a p c i -> p a (c i)").bitcast(I32))
         wo_raw = [load_weight(wo[PASS * a : PASS * (a + 1), :], f"wo_raw{a}") for a in range(GROUPS)]
-        wgo_rows = wgo.rearrange("(q t) j -> q t j", t=PACK)
-        wgo_tiles = []
-        for u in range(2):
-            rows = stream([P, 2, S], F32, f"wgo{u}")
-            for c in range(4):
-                nc.sync.dma_start(out=rows[32 * c : 32 * c + 32], in_=wgo_rows[:, 2 * u : 2 * u + 2, :])
-            wgo_tiles.append(rows)
 
         def entries(lst, j):
             return lst[:, j * (HALF // 16) : (j + 1) * (HALF // 16)]
@@ -142,7 +135,7 @@ def tile_list_dislocation_recurrent_backward_kernel(
         w1_q = {}
 
         def derivative(a, t, j):
-            d = work.tile([P, HALF], F32, name=f"d{a}{t}{j}", tag=f"d{j}", bufs=GROUPS * PACK)
+            d = work.tile([P, HALF], F32, name=f"d{a}{t}{j}", tag=f"d{a}{t}{j}", bufs=1, align_bytes=64)
             nc.vector.tensor_copy(d[:], s_tiles[a, t][:].indirect(entries(gather_list, j)))
             neg_d[a, t, j] = d
 
@@ -161,42 +154,44 @@ def tile_list_dislocation_recurrent_backward_kernel(
             return b == GROUPS - 1 and t > 0
 
         def gate(a, t, j):
-            h = psum.tile([P, HALF], F32, name=f"h{a}{t}{j}", tag="h", bufs=3)
+            h = psum.tile([P, HALF], F32, name=f"h{a}{t}{j}", tag="sum", bufs=6)
             first_product(h, a, t, j, stop=True)
             nc.vector.scalar_tensor_tensor(
                 out=g32[a, j][:, t, :], in0=h[:], scalar=-1.0, in1=neg_d[a, t, j][:], op0=MULT, op1=MULT
             )
 
-        for a in range(GROUPS):
-            for j in range(HALVES):
-                g32[a, j] = keep.tile([P, PACK, HALF], F32, name=f"g{a}{j}")
-
-        for j in range(HALVES):
-            derivative(0, 0, j)
-        for j in range(HALVES):
-            finish_derivative(0, 0, j)
-        for j in range(HALVES):
+        def table_gathers(j):
             v_w[j] = keep.tile([P, HALF], U32, name=f"v_w{j}", align_bytes=64)
             v_s[j] = keep.tile([P, HALF], U8, name=f"v_s{j}", align_bytes=64)
             nc.vector.tensor_copy(v_w[j][:], tab_w[:].indirect(entries(gather_list, j)))
             nc.vector.tensor_copy(v_s[j][:], tab_s[:].indirect(entries(gather_list, j)))
-        for a in range(GROUPS):
-            w1_q[a] = quantize(weave_weight(w1_raw[a], f"w1_woven{a}"), f"w1_{a}", "w1", GROUPS)
-            for t in range(PACK):
-                if (a, t) != (0, 0):
-                    for j in range(HALVES):
-                        derivative(a, t, j)
-                    for j in range(HALVES):
-                        finish_derivative(a, t, j)
-                for j in range(HALVES):
+
+        def gated_gradient(units):
+            for step in range(len(units) + 2):
+                if step < len(units):
+                    derivative(*units[step])
+                if 1 <= step <= len(units):
+                    finish_derivative(*units[step - 1])
+                if step >= 2:
+                    a, t, j = units[step - 2]
+                    if t == 0:
+                        g32[a, j] = in_slot((0, HALVES * a + j), [P, PACK, HALF], F32, f"g{a}{j}")
                     gate(a, t, j)
-            for j in range(HALVES):
-                g_woven[a, j] = weave(g32[a, j], woven(f"g_woven{a}{j}"))
+                    if t == PACK - 1:
+                        g_woven[a, j] = weave(g32[a, j], woven(f"g_woven{a}{j}"))
 
         g_q = {}
+
+        def quantize_gradient(a, j):
+            g_q[a, j] = quantize(g_woven[a, j], f"g_{a}{j}", f"act{j}", GROUPS)
+
         for j in range(HALVES):
-            for a in range(GROUPS):
-                g_q[a, j] = quantize(g_woven[a, j], f"g_{a}{j}", f"act{j}", GROUPS)
+            table_gathers(j)
+        for a in range(GROUPS):
+            w1_q[a] = quantize(weave_weight(w1_raw[a], f"w1_woven{a}"), f"w1_{a}", "w1", GROUPS)
+        gated_gradient(
+            [(0, t, j) for t in range(PACK) for j in range(HALVES)] + [(1, t, 0) for t in range(PACK)]
+        )
 
         for a in range(GROUPS):
             nc.vector.tensor_copy(
@@ -204,14 +199,29 @@ def tile_list_dislocation_recurrent_backward_kernel(
                 in_=wr_w_raw[:, a, :].rearrange("p (b q t) -> p b q t", t=PACK, q=P),
             )
         nc.vector.tensor_copy(
-            out=wr_s[:].rearrange("p (b t q) -> p b q t", t=PACK, q=P),
-            in_=wr_s_raw[:].rearrange("p (b q t) -> p b q t", t=PACK, q=P),
+            out=wr_s[:].rearrange("p (t q) -> p q t", t=PACK),
+            in_=wr_s_raw[:].rearrange("p (q t) -> p q t", t=PACK),
         )
+        quantize_gradient(0, 0)
+        quantize_gradient(0, 1)
+        quantize_gradient(1, 0)
+        gated_gradient([(1, t, 1) for t in range(PACK)])
+        wgo_rows = wgo.rearrange("(q t) j -> q t j", t=PACK)
+        wgo_tiles = []
+        for u in range(2):
+            rows = in_slot((1, u), [P, 2, S], F32, f"wgo{u}")
+            for c in range(4):
+                nc.sync.dma_start(out=rows[32 * c : 32 * c + 32], in_=wgo_rows[:, 2 * u : 2 * u + 2, :])
+            wgo_tiles.append(rows)
         wo_q = [quantize(weave_weight(wo_raw[a], f"wo_woven{a}"), f"wo_{a}", "wo", GROUPS) for a in range(GROUPS)]
+
+        def add_gradient(b, t, j):
+            if not repeats_first_product(b, t):
+                nc.vector.tensor_tensor(g32[b, j][:, t, :], g32[b, j][:, t, :], neg_d[b, t, j][:], ADD)
 
         def recurrent(b, j, dst):
             for t in range(PACK):
-                rec = psum.tile([P, HALF], F32, name=f"rec{b}{t}{j}", tag="rec", bufs=3)
+                rec = psum.tile([P, HALF], F32, name=f"rec{b}{t}{j}", tag="sum", bufs=6)
                 c0 = PASS * b + P * t
                 again = repeats_first_product(b, t)
                 if again:
@@ -219,23 +229,35 @@ def tile_list_dislocation_recurrent_backward_kernel(
                 for a in range(GROUPS):
                     nc.tensor.matmul_mx(
                         out=rec[:], lhsT=wr_w[:, H * a + c0 : H * a + c0 + P].bitcast(E4M3),
-                        lhsT_scale=wr_s[4 * a : P, c0 : c0 + P],
+                        lhsT_scale=wr_s[4 * (GROUPS * a + b) : P, P * t : P * (t + 1)],
                         rhs=g_q[a, j][0][:].bitcast(E4M3), rhs_scale=g_q[a, j][1][:],
                         start=(a == 0 and not again), stop=(a == GROUPS - 1),
                     )
                 d = neg_d[b, t, j]
                 dst32 = g32[b, j][:, t, :] if again else d[:]
                 nc.vector.scalar_tensor_tensor(out=dst32, in0=rec[:], scalar=-1.0, in1=d[:], op0=MULT, op1=MULT)
-            for t in range(PACK):
-                if not repeats_first_product(b, t):
-                    nc.vector.tensor_tensor(g32[b, j][:, t, :], g32[b, j][:, t, :], neg_d[b, t, j][:], ADD)
+                if t > 0:
+                    add_gradient(b, t - 1, j)
+            add_gradient(b, PACK - 1, j)
             return weave(g32[b, j], dst)
 
         b_q = {}
+
+        y_rows = out_0.rearrange("(p t) m -> t p m", t=PACK)
+        y_pairs = {}
+
+        def pair_up(t):
+            for c in range(T2 // CHUNK):
+                if t == 0:
+                    y_pairs[c] = work.tile(
+                        [P, 2, CHUNK, 2], BF16, name=f"y_pairs{c}", tag=f"d{c // PACK}{c % PACK}1", bufs=1, align_bytes=64
+                    )
+                nc.scalar.copy(out=y_pairs[c][:, t // 2, :, t % 2], in_=pages[t][:, c * CHUNK : (c + 1) * CHUNK])
+
         e32 = {}
 
-        def output_product(t, j, dst):
-            e = psum.tile([P, HALF], F32, name=f"e{t}{j}", tag="e", bufs=2)
+        def output_product(t, j, bank, tag):
+            e = psum.tile([P, HALF], F32, name=f"e{t}{j}", tag=f"e{bank}", bufs=1)
             cols = slice(P * t, P * (t + 1))
             for b in range(GROUPS):
                 nc.tensor.matmul_mx(
@@ -243,59 +265,54 @@ def tile_list_dislocation_recurrent_backward_kernel(
                     rhs=b_q[b, j][0][:].bitcast(E4M3), rhs_scale=b_q[b, j][1][:],
                     start=(b == 0), stop=(b == GROUPS - 1),
                 )
-            nc.scalar.copy(out=dst, in_=e[:])
-            e32[t, j] = dst
+            e32[t, j] = work.tile([P, HALF], F32, name=f"e32_{t}{j}", tag=tag, bufs=1, align_bytes=64)
+            nc.scalar.copy(out=e32[t, j][:], in_=e[:])
 
-        def e_tile(t, j):
-            return work.tile([P, HALF], F32, name=f"e32_{t}{j}", tag="d0", bufs=GROUPS * PACK)[:]
+        def place(t, j):
+            nc.vector.tensor_tensor(
+                pages[t][:].indirect(entries(scatter_list, j)), e32[t, j][:],
+                wgo_tiles[t // 2][:, t % 2, HALF * j : HALF * (j + 1)], MULT,
+            )
+            if j == HALVES - 1:
+                nc.sync.dma_start(out=y_rows[t], in_=pages[t][:])
 
+        b_woven = {b: recurrent(b, 0, woven(f"b_woven{b}0")) for b in range(GROUPS)}
+        quantize_gradient(1, 1)
+        first_woven = recurrent(0, 1, woven("b_woven01"))
         for b in range(GROUPS):
-            b_q[b, 0] = quantize(recurrent(b, 0, woven(f"b_woven{b}0")), f"b_{b}0", "act0", GROUPS)
-        for t in range(2):
-            output_product(t, 0, e_tile(t, 0))
-        b_q[0, 1] = quantize(recurrent(0, 1, woven("b_woven01")), "b_01", "act1", GROUPS)
-        last_woven = work.tile([P, PACK * HALF], BF16, name="b_woven11", tag="late", bufs=1, align_bytes=64)
-        b_q[1, 1] = quantize(recurrent(1, 1, last_woven), "b_11", "act1", GROUPS)
-        held = work.tile([P, 2, HALF], F32, name="e32_held", tag="late", bufs=1, align_bytes=64)
-        for t in range(2, PACK):
-            output_product(t, 0, held[:, t - 2, :])
-        for t in range(PACK):
-            output_product(t, 1, e_tile(t, 1))
-
-        y_rows = out_0.rearrange("(p t) m -> t p m", t=PACK)
-        y16 = [staging([P, PACK, T2 // 2], BF16, f"y16_{u}") for u in range(2)]
-        for j in range(HALVES):
-            for t in range(PACK):
-                nc.vector.tensor_tensor(
-                    pages[t][:].indirect(entries(scatter_list, j)), e32[t, j],
-                    wgo_tiles[t // 2][:, t % 2, HALF * j : HALF * (j + 1)], MULT,
-                )
-                if j == HALVES - 1:
-                    nc.sync.dma_start(out=y_rows[t], in_=pages[t][:])
-                    if t < PACK - 1:
-                        for u in range(2):
-                            nc.scalar.copy(out=y16[u][:, t, :], in_=pages[t][:, u * (T2 // 2) : (u + 1) * (T2 // 2)])
+            b_q[b, 0] = quantize(b_woven[b], f"b_{b}0", "act0", GROUPS)
+        output_product(0, 0, 0, "d031")
+        last_woven = recurrent(1, 1, woven("b_woven11"))
+        b_q[0, 1] = quantize(first_woven, "b_01", "act1", GROUPS)
+        b_q[1, 1] = quantize(last_woven, "b_11", "act1", GROUPS)
+        place(0, 0)
+        output_product(1, 0, 1, "slot03")
+        place(1, 0)
+        rest = [(0, 1), (1, 1), (2, 0), (2, 1), (3, 0), (3, 1)]
+        for i, (t, j) in enumerate(rest):
+            output_product(t, j, i % 2, f"d0{i % 2}0")
+            place(t, j)
+            if i >= 2 and rest[i - 2][1] == HALVES - 1:
+                pair_up(rest[i - 2][0])
+        pair_up(PACK - 1)
 
         words_out = out_1[0].rearrange("p m t -> p (m t)").bitcast(I32)
-        per_half = T2 // 2 // CHUNK
         y_woven = {}
-        for c in range(T2 // CHUNK):
-            u, c0 = c // per_half, (c % per_half) * CHUNK
-            copy = nc.scalar.copy if c in SCALAR_CHUNKS else nc.vector.tensor_copy
-            copy(out=y16[u][:, PACK - 1, c0 : c0 + CHUNK], in_=pages[PACK - 1][:, c * CHUNK : (c + 1) * CHUNK])
-            if c % 2 == 0:
-                pair = woven(f"y_woven{c}")
-            y_woven[c] = pair[:, (c % 2) * PACK * CHUNK : (c % 2 + 1) * PACK * CHUNK]
-            copy(
-                out=y_woven[c].rearrange("p (c i t) -> p c t i", t=PACK, i=4),
-                in_=y16[u][:, :, c0 : c0 + CHUNK].rearrange("p t (c i) -> p c t i", i=4),
-            )
-        for c in range(T2 // CHUNK):
-            cols = slice(c * CHUNK, (c + 1) * CHUNK)
-            nc.vector.quantize_mx(out=y_codes[:, cols].bitcast(E4M3), scales=y_scales[:, cols], in_=y_woven[c])
-            if c % 2 == 1:
-                both = slice((c - 1) * CHUNK, (c + 1) * CHUNK)
-                nc.sync.dma_start(out=words_out[:, both], in_=y_codes[:, both].bitcast(I32))
+        for c in range(T2 // CHUNK + 1):
+            if c < T2 // CHUNK:
+                if c % 2 == 0:
+                    both_chunks = woven(f"y_woven{c}")
+                y_woven[c] = both_chunks[:, (c % 2) * PACK * CHUNK : (c % 2 + 1) * PACK * CHUNK]
+                nc.vector.tensor_copy(
+                    out=y_woven[c].bitcast(F32).rearrange("p (m u) -> p m u", u=2),
+                    in_=y_pairs[c][:].rearrange("p u m e -> p u (m e)").bitcast(F32).rearrange("p u m -> p m u"),
+                )
+            if c > 0:
+                cols = slice((c - 1) * CHUNK, c * CHUNK)
+                nc.vector.quantize_mx(out=y_codes[:, cols].bitcast(E4M3), scales=y_scales[:, cols], in_=y_woven[c - 1])
+                if c % 2 == 0:
+                    both = slice((c - 2) * CHUNK, c * CHUNK)
+                    nc.sync.dma_start(out=words_out[:, both], in_=y_codes[:, both].bitcast(I32))
         for q in range(4):
             queue = nc.sync if q % 2 == 0 else nc.scalar
             queue.dma_start(

@@ -15,7 +15,7 @@ E4M3 = mybir.dt.float8_e4m3fn_x4
 E5M2 = mybir.dt.float8_e5m2_x4
 MULT = mybir.AluOpType.mult
 ADD = mybir.AluOpType.add
-SUBTRACT = mybir.AluOpType.subtract
+COPY = mybir.ActivationFunctionType.Copy
 
 P = 128
 PACK = 4
@@ -75,7 +75,6 @@ def tile_list_dislocation_recurrent_backward_kernel(
         tab_s = keep.tile([P, T], U8, name="tab_s", align_bytes=64)
         wr_s_raw = keep.tile([P, PASS], U8, name="wr_s_raw", align_bytes=64)
         wr_s = keep.tile([P, PASS], U8, name="wr_s", align_bytes=64)
-        wr_w = keep.tile([P, GROUPS * H], I32, name="wr_w", align_bytes=64)
         pages = [keep.tile([P, T2], F32, name=f"page{t}") for t in range(PACK)]
         y_codes = keep.tile([P, T2], U32, name="y_codes", align_bytes=64)
         y_scales = keep.tile([P, T2], U8, name="y_scales", align_bytes=64)
@@ -100,18 +99,18 @@ def tile_list_dislocation_recurrent_backward_kernel(
         nc.sync.dma_start(gather_list[:], offs)
         load_state(0, 0)
         load_state(0, 1)
+        load_state(0, 2)
         nc.sync.dma_start(out=tab_w[:].bitcast(I32), in_=tab_words[0].rearrange("p t i -> p (t i)").bitcast(I32))
         for q in range(4):
             nc.sync.dma_start(
                 out=tab_s[32 * q : 32 * q + 4, :].bitcast(I32), in_=tab_scales[0, 4 * q : 4 * q + 4, :].bitcast(I32)
             )
-        w1_raw = [load_weight(w1[:, 0:PASS], "w1_raw0")]
-        load_state(0, 2)
         load_state(0, 3)
         load_state(1, 0)
-        w1_raw.append(load_weight(w1[:, PASS : 2 * PASS], "w1_raw1"))
+        w1_raw = [load_weight(w1[:, 0:PASS], "w1_raw0")]
         load_state(1, 1)
         load_state(1, 2)
+        w1_raw.append(load_weight(w1[:, PASS : 2 * PASS], "w1_raw1"))
         load_state(1, 3)
         nc.sync.dma_start(scatter_list[:], offs2)
         for a in range(GROUPS):
@@ -127,7 +126,7 @@ def tile_list_dislocation_recurrent_backward_kernel(
         def entries(lst, j):
             return lst[:, j * (HALF // 16) : (j + 1) * (HALF // 16)]
 
-        neg_d = {}
+        deriv = {}
         g32 = {}
         g_woven = {}
         v_w = {}
@@ -137,11 +136,16 @@ def tile_list_dislocation_recurrent_backward_kernel(
         def derivative(a, t, j):
             d = work.tile([P, HALF], F32, name=f"d{a}{t}{j}", tag=f"d{a}{t}{j}", bufs=1, align_bytes=64)
             nc.vector.tensor_copy(d[:], s_tiles[a, t][:].indirect(entries(gather_list, j)))
-            neg_d[a, t, j] = d
+            deriv[a, t, j] = d
 
         def finish_derivative(a, t, j):
-            d = neg_d[a, t, j]
-            nc.vector.scalar_tensor_tensor(out=d[:], in0=d[:], scalar=1.0, in1=d[:], op0=SUBTRACT, op1=MULT)
+            d = deriv[a, t, j]
+            if (a, t, j) == (GROUPS - 1, PACK - 1, 0):
+                rest = in_slot((1, 2), [P, HALF], F32, f"rest{a}{t}{j}")
+            else:
+                rest = work.tile([P, HALF], F32, name=f"rest{a}{t}{j}", tag="rest", bufs=6)
+            nc.scalar.activation(out=rest[:], in_=d[:], func=COPY, scale=-1.0, bias=1.0)
+            nc.gpsimd.tensor_tensor(d[:], d[:], rest[:], MULT)
 
         def first_product(bank, a, t, j, stop):
             cols = slice(P * t, P * (t + 1))
@@ -156,9 +160,7 @@ def tile_list_dislocation_recurrent_backward_kernel(
         def gate(a, t, j):
             h = psum.tile([P, HALF], F32, name=f"h{a}{t}{j}", tag="sum", bufs=6)
             first_product(h, a, t, j, stop=True)
-            nc.vector.scalar_tensor_tensor(
-                out=g32[a, j][:, t, :], in0=h[:], scalar=-1.0, in1=neg_d[a, t, j][:], op0=MULT, op1=MULT
-            )
+            nc.vector.tensor_tensor(g32[a, j][:, t, :], h[:], deriv[a, t, j][:], MULT)
 
         def table_gathers(j):
             v_w[j] = keep.tile([P, HALF], U32, name=f"v_w{j}", align_bytes=64)
@@ -166,19 +168,17 @@ def tile_list_dislocation_recurrent_backward_kernel(
             nc.vector.tensor_copy(v_w[j][:], tab_w[:].indirect(entries(gather_list, j)))
             nc.vector.tensor_copy(v_s[j][:], tab_s[:].indirect(entries(gather_list, j)))
 
-        def gated_gradient(units):
-            for step in range(len(units) + 2):
-                if step < len(units):
-                    derivative(*units[step])
-                if 1 <= step <= len(units):
-                    finish_derivative(*units[step - 1])
-                if step >= 2:
-                    a, t, j = units[step - 2]
-                    if t == 0:
-                        g32[a, j] = in_slot((0, HALVES * a + j), [P, PACK, HALF], F32, f"g{a}{j}")
-                    gate(a, t, j)
-                    if t == PACK - 1:
-                        g_woven[a, j] = weave(g32[a, j], woven(f"g_woven{a}{j}"))
+        def gate_group(a, j):
+            g32[a, j] = in_slot((0, HALVES * a + j), [P, PACK, HALF], F32, f"g{a}{j}")
+            for t in range(PACK):
+                gate(a, t, j)
+            g_woven[a, j] = weave(g32[a, j], woven(f"g_woven{a}{j}"))
+
+        def derivatives(a):
+            for t in range(PACK):
+                for j in range(HALVES):
+                    derivative(a, t, j)
+                    finish_derivative(a, t, j)
 
         g_q = {}
 
@@ -189,10 +189,13 @@ def tile_list_dislocation_recurrent_backward_kernel(
             table_gathers(j)
         for a in range(GROUPS):
             w1_q[a] = quantize(weave_weight(w1_raw[a], f"w1_woven{a}"), f"w1_{a}", "w1", GROUPS)
-        gated_gradient(
-            [(0, t, j) for t in range(PACK) for j in range(HALVES)] + [(1, t, 0) for t in range(PACK)]
-        )
+        for a in range(GROUPS):
+            derivatives(a)
+        gate_group(0, 0)
+        gate_group(0, 1)
+        gate_group(1, 0)
 
+        wr_w = in_slot((1, 2), [P, GROUPS * H], I32, "wr_w")
         for a in range(GROUPS):
             nc.vector.tensor_copy(
                 out=wr_w[:, H * a : H * (a + 1)].rearrange("p (b t q) -> p b q t", t=PACK, q=P),
@@ -205,7 +208,7 @@ def tile_list_dislocation_recurrent_backward_kernel(
         quantize_gradient(0, 0)
         quantize_gradient(0, 1)
         quantize_gradient(1, 0)
-        gated_gradient([(1, t, 1) for t in range(PACK)])
+        gate_group(1, 1)
         wgo_rows = wgo.rearrange("(q t) j -> q t j", t=PACK)
         wgo_tiles = []
         for u in range(2):
@@ -217,7 +220,7 @@ def tile_list_dislocation_recurrent_backward_kernel(
 
         def add_gradient(b, t, j):
             if not repeats_first_product(b, t):
-                nc.vector.tensor_tensor(g32[b, j][:, t, :], g32[b, j][:, t, :], neg_d[b, t, j][:], ADD)
+                nc.vector.tensor_tensor(g32[b, j][:, t, :], g32[b, j][:, t, :], deriv[b, t, j][:], ADD)
 
         def recurrent(b, j, dst):
             for t in range(PACK):
@@ -233,9 +236,9 @@ def tile_list_dislocation_recurrent_backward_kernel(
                         rhs=g_q[a, j][0][:].bitcast(E4M3), rhs_scale=g_q[a, j][1][:],
                         start=(a == 0 and not again), stop=(a == GROUPS - 1),
                     )
-                d = neg_d[b, t, j]
+                d = deriv[b, t, j]
                 dst32 = g32[b, j][:, t, :] if again else d[:]
-                nc.vector.scalar_tensor_tensor(out=dst32, in0=rec[:], scalar=-1.0, in1=d[:], op0=MULT, op1=MULT)
+                nc.vector.tensor_tensor(dst32, rec[:], d[:], MULT)
                 if t > 0:
                     add_gradient(b, t - 1, j)
             add_gradient(b, PACK - 1, j)

@@ -101,18 +101,18 @@ def tile_list_dislocation_recurrent_backward_kernel(
         load_state(0, 1)
         load_state(0, 2)
         nc.sync.dma_start(out=tab_w[:].bitcast(I32), in_=tab_words[0].rearrange("p t i -> p (t i)").bitcast(I32))
+        load_state(0, 3)
+        load_state(1, 0)
+        nc.sync.dma_start(scatter_list[:], offs2)
         for q in range(4):
             nc.sync.dma_start(
                 out=tab_s[32 * q : 32 * q + 4, :].bitcast(I32), in_=tab_scales[0, 4 * q : 4 * q + 4, :].bitcast(I32)
             )
-        load_state(0, 3)
-        load_state(1, 0)
         w1_raw = [load_weight(w1[:, 0:PASS], "w1_raw0")]
         load_state(1, 1)
         load_state(1, 2)
         w1_raw.append(load_weight(w1[:, PASS : 2 * PASS], "w1_raw1"))
         load_state(1, 3)
-        nc.sync.dma_start(scatter_list[:], offs2)
         for a in range(GROUPS):
             for q in range(4):
                 nc.sync.dma_start(
@@ -154,8 +154,8 @@ def tile_list_dislocation_recurrent_backward_kernel(
                 rhs=v_w[j][:].bitcast(E5M2), rhs_scale=v_s[j][:], start=True, stop=stop,
             )
 
-        def repeats_first_product(b, t):
-            return b == GROUPS - 1 and t > 0
+        def repeats_first_product(b, t, j):
+            return t >= 2 and (b, j) != (0, 1)
 
         def gate(a, t, j):
             h = psum.tile([P, HALF], F32, name=f"h{a}{t}{j}", tag="sum", bufs=6)
@@ -187,10 +187,11 @@ def tile_list_dislocation_recurrent_backward_kernel(
 
         for j in range(HALVES):
             table_gathers(j)
-        for a in range(GROUPS):
-            w1_q[a] = quantize(weave_weight(w1_raw[a], f"w1_woven{a}"), f"w1_{a}", "w1", GROUPS)
+        w1_woven = [weave_weight(w1_raw[a], f"w1_woven{a}") for a in range(GROUPS)]
         for a in range(GROUPS):
             derivatives(a)
+        for a in range(GROUPS):
+            w1_q[a] = quantize(w1_woven[a], f"w1_{a}", "w1", GROUPS)
         gate_group(0, 0)
         gate_group(0, 1)
         gate_group(1, 0)
@@ -219,14 +220,15 @@ def tile_list_dislocation_recurrent_backward_kernel(
         wo_q = [quantize(weave_weight(wo_raw[a], f"wo_woven{a}"), f"wo_{a}", "wo", GROUPS) for a in range(GROUPS)]
 
         def add_gradient(b, t, j):
-            if not repeats_first_product(b, t):
-                nc.vector.tensor_tensor(g32[b, j][:, t, :], g32[b, j][:, t, :], deriv[b, t, j][:], ADD)
+            if not repeats_first_product(b, t, j):
+                engine = nc.vector if (b, j) == (1, 1) else nc.gpsimd
+                engine.tensor_tensor(g32[b, j][:, t, :], g32[b, j][:, t, :], deriv[b, t, j][:], ADD)
 
         def recurrent(b, j, dst):
             for t in range(PACK):
                 rec = psum.tile([P, HALF], F32, name=f"rec{b}{t}{j}", tag="sum", bufs=6)
                 c0 = PASS * b + P * t
-                again = repeats_first_product(b, t)
+                again = repeats_first_product(b, t, j)
                 if again:
                     first_product(rec, b, t, j, stop=False)
                 for a in range(GROUPS):

@@ -23,7 +23,7 @@ PASS = P * PACK
 HALF = 512
 HALVES = S // HALF
 GROUPS = H // PASS
-CHUNK = 256
+GRADIENT_SLOT = {(0, 0): (0, 3), (0, 1): (1, 0), (1, 0): (1, 3), (1, 1): (1, 2)}
 
 
 def tile_list_dislocation_recurrent_backward_kernel(
@@ -38,45 +38,56 @@ def tile_list_dislocation_recurrent_backward_kernel(
         def in_slot(slot, shape, dtype, name):
             return work.tile(shape, dtype, name=name, tag=f"slot{slot[0]}{slot[1]}", bufs=1, align_bytes=64)
 
-        def staging(shape, dtype, name):
-            return work.tile(shape, dtype, name=name, tag="staging", bufs=2)
+        def staging(u, shape, dtype, name):
+            return work.tile(shape, dtype, name=name, tag=f"staging{u}", bufs=1, align_bytes=64)
 
         def woven(name):
-            return work.tile([P, PACK * HALF], BF16, name=name, tag="woven", bufs=4, align_bytes=64)
+            return work.tile([P, PACK * HALF], BF16, name=name, tag="woven", bufs=3, align_bytes=64)
 
-        def operand(name, tag, bufs):
-            codes = work.tile([P, HALF], U32, name=name + "_codes", tag=tag + "_codes", bufs=bufs, align_bytes=64)
-            scales = work.tile([P, HALF], U8, name=name + "_scales", tag=tag + "_scales", bufs=bufs, align_bytes=64)
-            return codes, scales
+        def wide(name):
+            return work.tile([P, 2 * PACK * HALF], BF16, name=name, tag="wide", bufs=3, align_bytes=64)
 
-        def quantize(src, name, tag, bufs):
-            codes, scales = operand(name, tag, bufs)
-            nc.vector.quantize_mx(out=codes[:].bitcast(E4M3), scales=scales[:], in_=src[:])
-            return codes, scales
+        def side(tile, u):
+            return tile[:, PACK * HALF * u : PACK * HALF * (u + 1)]
 
-        def weave_weight(raw, name):
-            dst = woven(name)
+        def quantize(src, width, name, codes_tag):
+            codes = work.tile([P, width], U32, name=name + "_codes", tag=codes_tag, bufs=1, align_bytes=64)
+            scales = keep.tile([P, width], U8, name=name + "_scales", align_bytes=64)
+            nc.vector.quantize_mx(out=codes[:].bitcast(E4M3), scales=scales[:], in_=src)
+            return [(codes[:, half(u)], scales[:, half(u)]) for u in range(width // HALF)]
+
+        def half(j):
+            return slice(HALF * j, HALF * (j + 1))
+
+        def weave_weight(raw, dst):
             nc.scalar.copy(
-                out=dst[:].rearrange("p (t m i) -> p m i t", t=PACK, i=PACK),
+                out=dst.rearrange("p (t m i) -> p m i t", t=PACK, i=PACK),
                 in_=raw[:].rearrange("p i (m t) -> p m i t", t=PACK),
             )
             return dst
 
-        def weave(src, dst):
-            nc.scalar.copy(
-                out=dst[:].rearrange("p (c i t) -> p c t i", t=PACK, i=4),
-                in_=src[:].rearrange("p t (c i) -> p c t i", i=4),
-            )
+        def by_word(dst):
+            return dst.rearrange("p (c i t) -> p c t i", t=PACK, i=4)
+
+        def by_lane(src):
+            return src.rearrange("p t (c i) -> p c t i", i=4)
+
+        def weave(src, dst, parts=1):
+            width = HALF // parts
+            for u in range(parts):
+                nc.scalar.copy(
+                    out=by_word(dst[:, PACK * width * u : PACK * width * (u + 1)]),
+                    in_=by_lane(src[:, :, width * u : width * (u + 1)]),
+                )
             return dst
 
         gather_list = keep.tile([P, S // 16], U16, name="gather_list")
         scatter_list = keep.tile([P, S // 16], U16, name="scatter_list")
-        tab_w = keep.tile([P, T], U32, name="tab_w", align_bytes=64)
+        tab_w = staging(0, [P, T], U32, "tab_w")
         tab_s = keep.tile([P, T], U8, name="tab_s", align_bytes=64)
         wr_s_raw = keep.tile([P, PASS], U8, name="wr_s_raw", align_bytes=64)
         wr_s = keep.tile([P, PASS], U8, name="wr_s", align_bytes=64)
-        pages = [keep.tile([P, T2], F32, name=f"page{t}") for t in range(PACK)]
-        y_codes = keep.tile([P, T2], U32, name="y_codes", align_bytes=64)
+        pages = [keep.tile([P, T2], F32, name=f"page{t}") for t in range(2)]
         y_scales = keep.tile([P, T2], U8, name="y_scales", align_bytes=64)
 
         nc.vector.memset(tab_s[:].bitcast(I32), 0)
@@ -91,28 +102,28 @@ def tile_list_dislocation_recurrent_backward_kernel(
             s_tiles[a, t] = in_slot((a, t), [P, T], F32, f"s{a}{t}")
             nc.sync.dma_start(out=s_tiles[a, t][:], in_=s_rows[a, t])
 
-        def load_weight(rows, name):
-            raw = staging([P, PACK, HALF], F32, name)
-            nc.sync.dma_start(out=raw[:], in_=rows.rearrange("(p i) c -> p i c", i=PACK))
-            return raw
+        def weight_rows(rows):
+            return rows.rearrange("(p i) c -> p i c", i=PACK)
 
+        def load_weight(raw, rows):
+            nc.sync.dma_start(out=raw[:], in_=weight_rows(rows))
+
+        w1_rows = [w1[:, PASS * a : PASS * (a + 1)] for a in range(GROUPS)]
+        wo_rows = [wo[PASS * a : PASS * (a + 1), :] for a in range(GROUPS)]
         nc.sync.dma_start(gather_list[:], offs)
-        load_state(0, 0)
-        load_state(0, 1)
-        load_state(0, 2)
         nc.sync.dma_start(out=tab_w[:].bitcast(I32), in_=tab_words[0].rearrange("p t i -> p (t i)").bitcast(I32))
-        load_state(0, 3)
-        load_state(1, 0)
-        nc.sync.dma_start(scatter_list[:], offs2)
         for q in range(4):
             nc.sync.dma_start(
                 out=tab_s[32 * q : 32 * q + 4, :].bitcast(I32), in_=tab_scales[0, 4 * q : 4 * q + 4, :].bitcast(I32)
             )
-        w1_raw = [load_weight(w1[:, 0:PASS], "w1_raw0")]
-        load_state(1, 1)
-        load_state(1, 2)
-        w1_raw.append(load_weight(w1[:, PASS : 2 * PASS], "w1_raw1"))
-        load_state(1, 3)
+        w1_raw = [staging(1 + a, [P, PACK, HALF], F32, f"w1_raw{a}") for a in range(GROUPS)]
+        tiles = [(a, t) for a in range(GROUPS) for t in range(PACK)]
+        load_weight(w1_raw[0], w1_rows[0])
+        for a, t in tiles:
+            if (a, t) == (0, PACK - 1):
+                load_weight(w1_raw[1], w1_rows[1])
+            load_state(a, t)
+        nc.sync.dma_start(scatter_list[:], offs2)
         for a in range(GROUPS):
             for q in range(4):
                 nc.sync.dma_start(
@@ -121,203 +132,233 @@ def tile_list_dislocation_recurrent_backward_kernel(
                 )
         wr_w_raw = keep.tile([P, GROUPS, H], I32, name="wr_w_raw")
         nc.sync.dma_start(out=wr_w_raw[:], in_=wr_words.rearrange("a p c i -> p a (c i)").bitcast(I32))
-        wo_raw = [load_weight(wo[PASS * a : PASS * (a + 1), :], f"wo_raw{a}") for a in range(GROUPS)]
+        wo_raw = [staging(a, [P, PACK, HALF], F32, f"wo_raw{a}") for a in range(GROUPS)]
+        for a in range(GROUPS):
+            load_weight(wo_raw[a], wo_rows[a])
 
         def entries(lst, j):
             return lst[:, j * (HALF // 16) : (j + 1) * (HALF // 16)]
 
         deriv = {}
         g32 = {}
-        g_woven = {}
-        v_w = {}
-        v_s = {}
         w1_q = {}
+        v_w = keep.tile([P, S], U32, name="v_w", align_bytes=64)
+        v_s = keep.tile([P, S], U8, name="v_s", align_bytes=64)
 
-        def derivative(a, t, j):
-            d = work.tile([P, HALF], F32, name=f"d{a}{t}{j}", tag=f"d{a}{t}{j}", bufs=1, align_bytes=64)
-            nc.vector.tensor_copy(d[:], s_tiles[a, t][:].indirect(entries(gather_list, j)))
-            deriv[a, t, j] = d
-
-        def finish_derivative(a, t, j):
-            d = deriv[a, t, j]
-            if (a, t, j) == (GROUPS - 1, PACK - 1, 0):
-                rest = in_slot((1, 2), [P, HALF], F32, f"rest{a}{t}{j}")
+        def derivative(a, t):
+            if t == 0:
+                deriv[a] = keep.tile([P, PACK, S], F32, name=f"d{a}", align_bytes=64)
+            d = deriv[a][:, t, :]
+            nc.vector.tensor_copy(d, s_tiles[a, t][:].indirect(gather_list[:]))
+            if (a, t) == tiles[-1]:
+                parts = [
+                    (half(0), in_slot((0, 2), [P, HALF], F32, "rest_last0")),
+                    (half(1), work.tile([P, HALF], F32, name="rest_last1", tag="rest", bufs=2)),
+                ]
             else:
-                rest = work.tile([P, HALF], F32, name=f"rest{a}{t}{j}", tag="rest", bufs=6)
-            nc.scalar.activation(out=rest[:], in_=d[:], func=COPY, scale=-1.0, bias=1.0)
-            nc.gpsimd.tensor_tensor(d[:], d[:], rest[:], MULT)
+                parts = [(slice(0, S), work.tile([P, S], F32, name=f"rest{a}{t}", tag="rest", bufs=2))]
+            for cols, rest in parts:
+                nc.scalar.activation(out=rest[:], in_=d[:, cols], func=COPY, scale=-1.0, bias=1.0)
+                for c in range(cols.start, cols.stop, HALF):
+                    nc.gpsimd.tensor_tensor(
+                        d[:, c : c + HALF], d[:, c : c + HALF], rest[:, c - cols.start : c - cols.start + HALF], MULT
+                    )
+
+        def lane(t):
+            return slice(P * t, P * (t + 1))
 
         def first_product(bank, a, t, j, stop):
-            cols = slice(P * t, P * (t + 1))
             nc.tensor.matmul_mx(
-                out=bank[:], lhsT=w1_q[a][0][:, cols].bitcast(E4M3), lhsT_scale=w1_q[a][1][:, cols],
-                rhs=v_w[j][:].bitcast(E5M2), rhs_scale=v_s[j][:], start=True, stop=stop,
+                out=bank[:], lhsT=w1_q[a][0][:, lane(t)].bitcast(E4M3), lhsT_scale=w1_q[a][1][:, lane(t)],
+                rhs=v_w[:, half(j)].bitcast(E5M2), rhs_scale=v_s[:, half(j)], start=True, stop=stop,
             )
-
-        def repeats_first_product(b, t, j):
-            return t >= 2 and (b, j) != (0, 1)
 
         def gate(a, t, j):
-            h = psum.tile([P, HALF], F32, name=f"h{a}{t}{j}", tag="sum", bufs=6)
+            if t == 0:
+                g32[a, j] = in_slot(GRADIENT_SLOT[a, j], [P, PACK, HALF], F32, f"g{a}{j}")
+            h = psum.tile([P, HALF], F32, name=f"h{a}{t}{j}", tag="sum", bufs=8)
             first_product(h, a, t, j, stop=True)
-            nc.vector.tensor_tensor(g32[a, j][:, t, :], h[:], deriv[a, t, j][:], MULT)
+            nc.vector.tensor_tensor(g32[a, j][:, t, :], h[:], deriv[a][:, t, half(j)], MULT)
 
-        def table_gathers(j):
-            v_w[j] = keep.tile([P, HALF], U32, name=f"v_w{j}", align_bytes=64)
-            v_s[j] = keep.tile([P, HALF], U8, name=f"v_s{j}", align_bytes=64)
-            nc.vector.tensor_copy(v_w[j][:], tab_w[:].indirect(entries(gather_list, j)))
-            nc.vector.tensor_copy(v_s[j][:], tab_s[:].indirect(entries(gather_list, j)))
+        def quantize_w1(a):
+            w1_woven = weave_weight(w1_raw[a], woven(f"w1_woven{a}")[:])
+            w1_q[a] = quantize(w1_woven, HALF, f"w1_{a}", ["w1_codes", "slot11"][a])[0]
 
-        def gate_group(a, j):
-            g32[a, j] = in_slot((0, HALVES * a + j), [P, PACK, HALF], F32, f"g{a}{j}")
-            for t in range(PACK):
-                gate(a, t, j)
-            g_woven[a, j] = weave(g32[a, j], woven(f"g_woven{a}{j}"))
-
-        def derivatives(a):
-            for t in range(PACK):
-                for j in range(HALVES):
-                    derivative(a, t, j)
-                    finish_derivative(a, t, j)
-
-        g_q = {}
-
-        def quantize_gradient(a, j):
-            g_q[a, j] = quantize(g_woven[a, j], f"g_{a}{j}", f"act{j}", GROUPS)
-
-        for j in range(HALVES):
-            table_gathers(j)
-        w1_woven = [weave_weight(w1_raw[a], f"w1_woven{a}") for a in range(GROUPS)]
-        for a in range(GROUPS):
-            derivatives(a)
-        for a in range(GROUPS):
-            w1_q[a] = quantize(w1_woven[a], f"w1_{a}", "w1", GROUPS)
-        gate_group(0, 0)
-        gate_group(0, 1)
-        gate_group(1, 0)
-
-        wr_w = in_slot((1, 2), [P, GROUPS * H], I32, "wr_w")
-        for a in range(GROUPS):
-            nc.vector.tensor_copy(
-                out=wr_w[:, H * a : H * (a + 1)].rearrange("p (b t q) -> p b q t", t=PACK, q=P),
-                in_=wr_w_raw[:, a, :].rearrange("p (b q t) -> p b q t", t=PACK, q=P),
-            )
+        nc.vector.tensor_copy(v_w[:], tab_w[:].indirect(gather_list[:]))
+        nc.vector.tensor_copy(v_s[:], tab_s[:].indirect(gather_list[:]))
+        derivative(0, 0)
+        quantize_w1(0)
+        for t in range(1, PACK):
+            derivative(0, t)
+        for t in range(PACK - 1):
+            gate(0, t, 0)
+        derivative(1, 0)
+        for t in range(PACK - 1):
+            gate(0, t, 1)
+        gate(0, PACK - 1, 0)
+        gate(0, PACK - 1, 1)
+        derivative(1, 1)
+        quantize_w1(1)
+        derivative(1, 2)
+        for t in range(2):
+            gate(1, t, 1)
+        derivative(1, 3)
+        for t in range(PACK - 1):
+            gate(1, t, 0)
+        gate(1, 2, 1)
         nc.vector.tensor_copy(
             out=wr_s[:].rearrange("p (t q) -> p q t", t=PACK),
             in_=wr_s_raw[:].rearrange("p (q t) -> p q t", t=PACK),
         )
-        quantize_gradient(0, 0)
-        quantize_gradient(0, 1)
-        quantize_gradient(1, 0)
-        gate_group(1, 1)
-        wgo_rows = wgo.rearrange("(q t) j -> q t j", t=PACK)
+        wr_w = in_slot((0, 2), [P, GROUPS * H], I32, "wr_w")
+        for a in range(GROUPS):
+            gate(1, 3, a)
+            nc.vector.tensor_copy(
+                out=wr_w[:, H * a : H * (a + 1)].rearrange("p (b t q) -> p b q t", t=PACK, q=P),
+                in_=wr_w_raw[:, a, :].rearrange("p (b q t) -> p b q t", t=PACK, q=P),
+            )
+        g0_woven = wide("g0_woven")
+        for j in range(HALVES):
+            weave(g32[0, j], side(g0_woven, j), parts=2)
+        g10_woven = weave(g32[1, 0], woven("g10_woven")[:], parts=2)
+        g11_woven = weave(g32[1, 1], woven("g11_woven")[:])
+        b0_wo_woven = [wide(f"b0_wo_woven{a}") for a in range(GROUPS)]
+        for a in range(GROUPS):
+            weave_weight(wo_raw[a], side(b0_wo_woven[a], 1))
+
+        g_q = {}
+        g_q[0, 0], g_q[0, 1] = quantize(g0_woven[:], S, "g0", "g0_codes")
+
+        g10_codes = keep.tile([P, HALF], U32, name="g10_codes", align_bytes=64)
+        g10_scales = keep.tile([P, HALF], U8, name="g10_scales", align_bytes=64)
+        for u in range(2):
+            cols = slice(HALF // 2 * u, HALF // 2 * (u + 1))
+            nc.vector.quantize_mx(
+                out=g10_codes[:, cols].bitcast(E4M3), scales=g10_scales[:, cols], in_=g10_woven[:, S * u : S * (u + 1)]
+            )
+        g_q[1, 0] = (g10_codes[:], g10_scales[:])
+        wgo_rows = wgo.rearrange("(q t) j -> q (t j)", t=PACK)
         wgo_tiles = []
         for u in range(2):
-            rows = in_slot((1, u), [P, 2, S], F32, f"wgo{u}")
-            for c in range(4):
-                nc.sync.dma_start(out=rows[32 * c : 32 * c + 32], in_=wgo_rows[:, 2 * u : 2 * u + 2, :])
+            rows = in_slot((0, u), [P, 2 * S], F32, f"wgo{u}")
+            nc.sync.dma_start(out=rows[:], in_=wgo_rows[:, 2 * S * u : 2 * S * (u + 1)].partition_broadcast(4))
             wgo_tiles.append(rows)
-        wo_q = [quantize(weave_weight(wo_raw[a], f"wo_woven{a}"), f"wo_{a}", "wo", GROUPS) for a in range(GROUPS)]
 
-        def add_gradient(b, t, j):
-            if not repeats_first_product(b, t, j):
-                engine = nc.vector if (b, j) == (1, 1) else nc.gpsimd
-                engine.tensor_tensor(g32[b, j][:, t, :], g32[b, j][:, t, :], deriv[b, t, j][:], ADD)
+        def recurrent_pass(out, a, b, t, j, cols, start, stop):
+            c0 = H * a + PASS * b + P * t
+            nc.tensor.matmul_mx(
+                out=out, lhsT=wr_w[:, c0 : c0 + P].bitcast(E4M3),
+                lhsT_scale=wr_s[4 * (GROUPS * a + b) : P, lane(t)],
+                rhs=g_q[a, j][0][:, cols].bitcast(E4M3), rhs_scale=g_q[a, j][1][:, cols],
+                start=start, stop=stop,
+            )
 
-        def recurrent(b, j, dst):
+        def recurrent_by_columns(b, j, dst, on_gpsimd):
+            later = []
+            for u in range(HALF // P):
+                rec = psum.tile([P, PACK, P], F32, name=f"rec{b}{j}c{u}", tag="sum", bufs=8)
+                for a in range(GROUPS):
+                    for t in range(PACK):
+                        recurrent_pass(
+                            rec[:, t, :], a, b, t, j, lane(u), (a, t) == (0, 0), (a, t) == (GROUPS - 1, PACK - 1)
+                        )
+                term = work.tile([P, PACK, P], F32, name=f"term{b}{j}{u}", tag="term", bufs=4, align_bytes=64)
+                c0 = HALF * j + P * u
+                nc.vector.tensor_tensor(term[:], rec[:], deriv[b][:, :, c0 : c0 + P], MULT)
+                sides = by_word(dst[:, PASS * u : PASS * (u + 1)]), by_lane(term[:]), by_lane(g32[b, j][:, :, lane(u)])
+                if u < on_gpsimd:
+                    nc.gpsimd.tensor_tensor(*sides, ADD)
+                else:
+                    later.append(sides)
+            return later
+
+        def recurrent_by_lanes(b, j, dst, repeated):
             for t in range(PACK):
-                rec = psum.tile([P, HALF], F32, name=f"rec{b}{t}{j}", tag="sum", bufs=6)
-                c0 = PASS * b + P * t
-                again = repeats_first_product(b, t, j)
+                rec = psum.tile([P, HALF], F32, name=f"rec{b}{t}{j}", tag="sum", bufs=8)
+                again = t < repeated
                 if again:
                     first_product(rec, b, t, j, stop=False)
                 for a in range(GROUPS):
-                    nc.tensor.matmul_mx(
-                        out=rec[:], lhsT=wr_w[:, H * a + c0 : H * a + c0 + P].bitcast(E4M3),
-                        lhsT_scale=wr_s[4 * (GROUPS * a + b) : P, P * t : P * (t + 1)],
-                        rhs=g_q[a, j][0][:].bitcast(E4M3), rhs_scale=g_q[a, j][1][:],
-                        start=(a == 0 and not again), stop=(a == GROUPS - 1),
-                    )
-                d = deriv[b, t, j]
-                dst32 = g32[b, j][:, t, :] if again else d[:]
-                nc.vector.tensor_tensor(dst32, rec[:], d[:], MULT)
-                if t > 0:
-                    add_gradient(b, t - 1, j)
-            add_gradient(b, PACK - 1, j)
-            return weave(g32[b, j], dst)
+                    recurrent_pass(rec[:], a, b, t, j, half(0), a == 0 and not again, a == GROUPS - 1)
+                d = deriv[b][:, t, half(j)]
+                nc.vector.tensor_tensor(g32[b, j][:, t, :] if again else d, rec[:], d, MULT)
+            for t in range(repeated, PACK):
+                nc.vector.tensor_tensor(g32[b, j][:, t, :], g32[b, j][:, t, :], deriv[b][:, t, half(j)], ADD)
+            weave(g32[b, j], dst)
 
         b_q = {}
 
         y_rows = out_0.rearrange("(p t) m -> t p m", t=PACK)
         y_pairs = {}
 
+        chunks = [(0, 256), (256, 768), (768, 1280), (1280, 1792), (1792, 2048)]
+        pair_slots = list(GRADIENT_SLOT.values()) + [(1, 1)]
+
         def pair_up(t):
-            for c in range(T2 // CHUNK):
+            for c, (lo, hi) in enumerate(chunks):
                 if t == 0:
-                    y_pairs[c] = work.tile(
-                        [P, 2, CHUNK, 2], BF16, name=f"y_pairs{c}", tag=f"d{c // PACK}{c % PACK}1", bufs=1, align_bytes=64
-                    )
-                nc.scalar.copy(out=y_pairs[c][:, t // 2, :, t % 2], in_=pages[t][:, c * CHUNK : (c + 1) * CHUNK])
+                    y_pairs[c] = in_slot(pair_slots[c], [P, 2, hi - lo, 2], BF16, f"y_pairs{c}")
+                nc.scalar.copy(out=y_pairs[c][:, t // 2, :, t % 2], in_=pages[t][:, lo:hi])
 
-        e32 = {}
-
-        def output_product(t, j, bank, tag):
-            e = psum.tile([P, HALF], F32, name=f"e{t}{j}", tag=f"e{bank}", bufs=1)
-            cols = slice(P * t, P * (t + 1))
+        def output_product(t, j, dst):
+            e = psum.tile([P, HALF], F32, name=f"e{t}{j}", tag="sum", bufs=8)
             for b in range(GROUPS):
                 nc.tensor.matmul_mx(
-                    out=e[:], lhsT=wo_q[b][0][:, cols].bitcast(E4M3), lhsT_scale=wo_q[b][1][:, cols],
-                    rhs=b_q[b, j][0][:].bitcast(E4M3), rhs_scale=b_q[b, j][1][:],
+                    out=e[:], lhsT=wo_q[b][0][:, lane(t)].bitcast(E4M3), lhsT_scale=wo_q[b][1][:, lane(t)],
+                    rhs=b_q[b, j][0].bitcast(E4M3), rhs_scale=b_q[b, j][1],
                     start=(b == 0), stop=(b == GROUPS - 1),
                 )
-            e32[t, j] = work.tile([P, HALF], F32, name=f"e32_{t}{j}", tag=tag, bufs=1, align_bytes=64)
-            nc.scalar.copy(out=e32[t, j][:], in_=e[:])
+            nc.scalar.copy(out=dst, in_=e[:])
 
-        def place(t, j):
-            nc.vector.tensor_tensor(
-                pages[t][:].indirect(entries(scatter_list, j)), e32[t, j][:],
-                wgo_tiles[t // 2][:, t % 2, HALF * j : HALF * (j + 1)], MULT,
-            )
-            if j == HALVES - 1:
-                nc.sync.dma_start(out=y_rows[t], in_=pages[t][:])
+        def place(t, lst, src, cols):
+            weights = wgo_tiles[t // 2][:, S * (t % 2) : S * (t % 2 + 1)]
+            nc.vector.tensor_tensor(pages[t][:].indirect(lst), src, weights[:, cols], MULT)
 
-        b_woven = {b: recurrent(b, 0, woven(f"b_woven{b}0")) for b in range(GROUPS)}
-        quantize_gradient(1, 1)
-        first_woven = recurrent(0, 1, woven("b_woven01"))
+        wo_q = {}
+        recurrent_by_columns(0, 0, side(b0_wo_woven[0], 0), PACK)
+        g_q[1, 1] = quantize(g11_woven, HALF, "g11", "g11_codes")[0]
+        recurrent_by_lanes(1, 0, side(b0_wo_woven[1], 0), PACK)
+        b1_woven = wide("b1_woven")
+        later = recurrent_by_columns(0, 1, side(b1_woven, 0), 2)
+        recurrent_by_lanes(1, 1, side(b1_woven, 1), 2)
+        for sides in later:
+            nc.vector.tensor_tensor(*sides, ADD)
         for b in range(GROUPS):
-            b_q[b, 0] = quantize(b_woven[b], f"b_{b}0", "act0", GROUPS)
-        output_product(0, 0, 0, "d031")
-        last_woven = recurrent(1, 1, woven("b_woven11"))
-        b_q[0, 1] = quantize(first_woven, "b_01", "act1", GROUPS)
-        b_q[1, 1] = quantize(last_woven, "b_11", "act1", GROUPS)
-        place(0, 0)
-        output_product(1, 0, 1, "slot03")
-        place(1, 0)
-        rest = [(0, 1), (1, 1), (2, 0), (2, 1), (3, 0), (3, 1)]
-        for i, (t, j) in enumerate(rest):
-            output_product(t, j, i % 2, f"d0{i % 2}0")
-            place(t, j)
-            if i >= 2 and rest[i - 2][1] == HALVES - 1:
-                pair_up(rest[i - 2][0])
-        pair_up(PACK - 1)
+            b_q[b, 0], wo_q[b] = quantize(b0_wo_woven[b][:], S, f"b0_wo{b}", ["slot02", "g0_codes"][b])
+        first = [staging(j, [P, HALF], F32, f"e32_0{j}") for j in range(HALVES)]
+        output_product(0, 0, first[0][:])
+        b_q[0, 1], b_q[1, 1] = quantize(b1_woven[:], S, "b1", "b1_codes")
+        output_product(0, 1, first[1][:])
+        e32 = {}
+        for t in range(1, PACK):
+            e32[t] = work.tile([P, S], F32, name=f"e32_{t}", tag="e32", bufs=3, align_bytes=64)
+            for j in range(HALVES):
+                output_product(t, j, e32[t][:, half(j)])
+        for j in range(HALVES):
+            place(0, entries(scatter_list, j), first[j][:], half(j))
+            pages.append(staging(j, [P, T2], F32, f"page{2 + j}"))
+            nc.gpsimd.memset(pages[-1][:], 0.0)
+        for t in range(PACK):
+            if t > 0:
+                place(t, scatter_list[:], e32[t][:], slice(0, S))
+            nc.sync.dma_start(out=y_rows[t], in_=pages[t][:])
+            pair_up(t)
 
         words_out = out_1[0].rearrange("p m t -> p (m t)").bitcast(I32)
         y_woven = {}
-        for c in range(T2 // CHUNK + 1):
-            if c < T2 // CHUNK:
-                if c % 2 == 0:
-                    both_chunks = woven(f"y_woven{c}")
-                y_woven[c] = both_chunks[:, (c % 2) * PACK * CHUNK : (c % 2 + 1) * PACK * CHUNK]
+        y_codes = staging(2, [P, T2], U32, "y_codes")
+        for c in range(len(chunks) + 1):
+            if c < len(chunks):
+                width = chunks[c][1] - chunks[c][0]
+                y_woven[c] = woven(f"y_woven{c}")[:, 0 : PACK * width]
                 nc.vector.tensor_copy(
                     out=y_woven[c].bitcast(F32).rearrange("p (m u) -> p m u", u=2),
                     in_=y_pairs[c][:].rearrange("p u m e -> p u (m e)").bitcast(F32).rearrange("p u m -> p m u"),
                 )
             if c > 0:
-                cols = slice((c - 1) * CHUNK, c * CHUNK)
+                cols = slice(*chunks[c - 1])
                 nc.vector.quantize_mx(out=y_codes[:, cols].bitcast(E4M3), scales=y_scales[:, cols], in_=y_woven[c - 1])
-                if c % 2 == 0:
-                    both = slice((c - 2) * CHUNK, c * CHUNK)
-                    nc.sync.dma_start(out=words_out[:, both], in_=y_codes[:, both].bitcast(I32))
+                nc.sync.dma_start(out=words_out[:, cols], in_=y_codes[:, cols].bitcast(I32))
         for q in range(4):
             queue = nc.sync if q % 2 == 0 else nc.scalar
             queue.dma_start(

@@ -87,7 +87,7 @@ def tile_list_dislocation_recurrent_backward_kernel(
         tab_s = keep.tile([P, T], U8, name="tab_s", align_bytes=64)
         wr_s_raw = keep.tile([P, PASS], U8, name="wr_s_raw", align_bytes=64)
         wr_s = keep.tile([P, PASS], U8, name="wr_s", align_bytes=64)
-        pages = [keep.tile([P, T2], F32, name=f"page{t}") for t in range(2)]
+        pages = [keep.tile([P, T2], F32, name=f"page{t}") for t in range(PACK)]
         y_scales = keep.tile([P, T2], U8, name="y_scales", align_bytes=64)
 
         nc.vector.memset(tab_s[:].bitcast(I32), 0)
@@ -130,7 +130,7 @@ def tile_list_dislocation_recurrent_backward_kernel(
                     out=wr_s_raw[32 * q + 8 * a : 32 * q + 8 * a + 8, :].bitcast(I32),
                     in_=wr_scales[a, 4 * q : 4 * q + 4, :].bitcast(I32).rearrange("r (b c) -> b r c", b=GROUPS),
                 )
-        wr_w_raw = keep.tile([P, GROUPS, H], I32, name="wr_w_raw")
+        wr_w_raw = in_slot((0, 1), [P, GROUPS, H], I32, "wr_w_raw")
         nc.sync.dma_start(out=wr_w_raw[:], in_=wr_words.rearrange("a p c i -> p a (c i)").bitcast(I32))
         wo_raw = [staging(a, [P, PACK, HALF], F32, f"wo_raw{a}") for a in range(GROUPS)]
         for a in range(GROUPS):
@@ -325,22 +325,19 @@ def tile_list_dislocation_recurrent_backward_kernel(
             nc.vector.tensor_tensor(*sides, ADD)
         for b in range(GROUPS):
             b_q[b, 0], wo_q[b] = quantize(b0_wo_woven[b][:], S, f"b0_wo{b}", ["slot02", "g0_codes"][b])
-        first = [staging(j, [P, HALF], F32, f"e32_0{j}") for j in range(HALVES)]
-        output_product(0, 0, first[0][:])
+        e32_pairs = [staging(u, [P, 2 * S], F32, f"e32_pair{u}") for u in range(2)]
+        e32 = [e32_pairs[t // 2][:, S * (t % 2) : S * (t % 2 + 1)] for t in range(PACK)]
+        output_product(0, 0, e32[0][:, half(0)])
         b_q[0, 1], b_q[1, 1] = quantize(b1_woven[:], S, "b1", "b1_codes")
-        output_product(0, 1, first[1][:])
-        e32 = {}
+        output_product(0, 1, e32[0][:, half(1)])
         for t in range(1, PACK):
-            e32[t] = work.tile([P, S], F32, name=f"e32_{t}", tag="e32", bufs=3, align_bytes=64)
             for j in range(HALVES):
                 output_product(t, j, e32[t][:, half(j)])
         for j in range(HALVES):
-            place(0, entries(scatter_list, j), first[j][:], half(j))
-            pages.append(staging(j, [P, T2], F32, f"page{2 + j}"))
-            nc.gpsimd.memset(pages[-1][:], 0.0)
+            place(0, entries(scatter_list, j), e32[0][:, half(j)], half(j))
         for t in range(PACK):
             if t > 0:
-                place(t, scatter_list[:], e32[t][:], slice(0, S))
+                place(t, scatter_list[:], e32[t], slice(0, S))
             nc.sync.dma_start(out=y_rows[t], in_=pages[t][:])
             pair_up(t)
 

@@ -90,10 +90,10 @@ def tile_list_dislocation_recurrent_backward_kernel(
         pages = [keep.tile([P, T2], F32, name=f"page{t}") for t in range(PACK)]
         y_scales = keep.tile([P, T2], U8, name="y_scales", align_bytes=64)
 
-        nc.vector.memset(tab_s[:].bitcast(I32), 0)
-        nc.vector.memset(wr_s_raw[:].bitcast(I32), 0)
+        nc.gpsimd.memset(tab_s[:].bitcast(I32), 0)
+        nc.gpsimd.memset(wr_s_raw[:].bitcast(I32), 0)
         for page in pages:
-            nc.vector.memset(page[:], 0.0)
+            nc.gpsimd.memset(page[:], 0.0)
 
         s_rows = sT.rearrange("(a p t) c -> a t p c", p=P, t=PACK)
         s_tiles = {}

@@ -23,7 +23,7 @@ PASS = P * PACK
 HALF = 512
 HALVES = S // HALF
 GROUPS = H // PASS
-GRADIENT_SLOT = {(0, 0): (0, 3), (0, 1): (1, 0), (1, 0): (1, 3), (1, 1): (1, 2)}
+GRADIENT_SLOT = {(0, 0): (1, 3), (0, 1): (1, 1), (1, 0): (0, 2), (1, 1): (0, 3)}
 
 
 def tile_list_dislocation_recurrent_backward_kernel(
@@ -59,11 +59,13 @@ def tile_list_dislocation_recurrent_backward_kernel(
         def half(j):
             return slice(HALF * j, HALF * (j + 1))
 
-        def weave_weight(raw, dst):
-            nc.scalar.copy(
-                out=dst.rearrange("p (t m i) -> p m i t", t=PACK, i=PACK),
-                in_=raw[:].rearrange("p i (m t) -> p m i t", t=PACK),
-            )
+        def weave_weight(raw, dst, parts=1):
+            width = P // parts
+            for u in range(parts):
+                nc.scalar.copy(
+                    out=dst.rearrange("p (t m i) -> p m i t", t=PACK, i=PACK)[:, width * u : width * (u + 1)],
+                    in_=raw[:].rearrange("p i (m t) -> p m i t", t=PACK)[:, width * u : width * (u + 1)],
+                )
             return dst
 
         def by_word(dst):
@@ -120,7 +122,7 @@ def tile_list_dislocation_recurrent_backward_kernel(
         tiles = [(a, t) for a in range(GROUPS) for t in range(PACK)]
         load_weight(w1_raw[0], w1_rows[0])
         for a, t in tiles:
-            if (a, t) == (0, PACK - 1):
+            if (a, t) == (1, 2):
                 load_weight(w1_raw[1], w1_rows[1])
             load_state(a, t)
         nc.sync.dma_start(scatter_list[:], offs2)
@@ -152,8 +154,7 @@ def tile_list_dislocation_recurrent_backward_kernel(
             nc.vector.tensor_copy(d, s_tiles[a, t][:].indirect(gather_list[:]))
             if (a, t) == tiles[-1]:
                 parts = [
-                    (half(0), in_slot((0, 2), [P, HALF], F32, "rest_last0")),
-                    (half(1), work.tile([P, HALF], F32, name="rest_last1", tag="rest", bufs=2)),
+                    (half(j), in_slot(GRADIENT_SLOT[a, j], [P, HALF], F32, f"rest_last{j}")) for j in range(HALVES)
                 ]
             else:
                 parts = [(slice(0, S), work.tile([P, S], F32, name=f"rest{a}{t}", tag="rest", bufs=2))]
@@ -182,61 +183,46 @@ def tile_list_dislocation_recurrent_backward_kernel(
 
         def quantize_w1(a):
             w1_woven = weave_weight(w1_raw[a], woven(f"w1_woven{a}")[:])
-            w1_q[a] = quantize(w1_woven, HALF, f"w1_{a}", ["w1_codes", "slot11"][a])[0]
+            w1_q[a] = quantize(w1_woven, HALF, f"w1_{a}", ["slot00", "slot12"][a])[0]
 
         nc.vector.tensor_copy(v_w[:], tab_w[:].indirect(gather_list[:]))
         nc.vector.tensor_copy(v_s[:], tab_s[:].indirect(gather_list[:]))
         derivative(0, 0)
         quantize_w1(0)
-        for t in range(1, PACK):
-            derivative(0, t)
-        for t in range(PACK - 1):
-            gate(0, t, 0)
-        derivative(1, 0)
-        for t in range(PACK - 1):
+        for a, t in tiles[1:6]:
+            derivative(a, t)
+        for t in range(PACK):
             gate(0, t, 1)
-        gate(0, PACK - 1, 0)
-        gate(0, PACK - 1, 1)
-        derivative(1, 1)
-        quantize_w1(1)
         derivative(1, 2)
-        for t in range(2):
-            gate(1, t, 1)
+        quantize_w1(1)
         derivative(1, 3)
-        for t in range(PACK - 1):
-            gate(1, t, 0)
-        gate(1, 2, 1)
+        for a in range(GROUPS):
+            for t in range(PACK):
+                gate(a, t, 0)
+        g0_woven = wide("g0_woven")
+        for j in reversed(range(HALVES)):
+            weave(g32[0, j], side(g0_woven, j), parts=2)
+        g10_woven = weave(g32[1, 0], woven("g10_woven")[:])
         nc.vector.tensor_copy(
             out=wr_s[:].rearrange("p (t q) -> p q t", t=PACK),
             in_=wr_s_raw[:].rearrange("p (q t) -> p q t", t=PACK),
         )
-        wr_w = in_slot((0, 2), [P, GROUPS * H], I32, "wr_w")
-        for a in range(GROUPS):
-            gate(1, 3, a)
-            nc.vector.tensor_copy(
-                out=wr_w[:, H * a : H * (a + 1)].rearrange("p (b t q) -> p b q t", t=PACK, q=P),
-                in_=wr_w_raw[:, a, :].rearrange("p (b q t) -> p b q t", t=PACK, q=P),
+        wr_w = in_slot((1, 0), [P, GROUPS * H], I32, "wr_w")
+        for u in range(GROUPS * GROUPS):
+            nc.gpsimd.tensor_copy(
+                out=wr_w[:, PASS * u : PASS * (u + 1)].rearrange("p (t q) -> p t q", t=PACK),
+                in_=wr_w_raw[:].rearrange("p a (b q t) -> p (a b) t q", t=PACK, q=P)[:, u],
             )
-        g0_woven = wide("g0_woven")
-        for j in range(HALVES):
-            weave(g32[0, j], side(g0_woven, j), parts=2)
-        g10_woven = weave(g32[1, 0], woven("g10_woven")[:], parts=2)
+        g_q = {}
+        g_q[0, 0], g_q[0, 1] = quantize(g0_woven[:], S, "g0", "g0_codes")
+        g_q[1, 0] = quantize(g10_woven, HALF, "g10", "g10_codes")[0]
+        for t in range(PACK):
+            gate(1, t, 1)
         g11_woven = weave(g32[1, 1], woven("g11_woven")[:])
         b0_wo_woven = [wide(f"b0_wo_woven{a}") for a in range(GROUPS)]
         for a in range(GROUPS):
-            weave_weight(wo_raw[a], side(b0_wo_woven[a], 1))
+            weave_weight(wo_raw[a], side(b0_wo_woven[a], 1), parts=2)
 
-        g_q = {}
-        g_q[0, 0], g_q[0, 1] = quantize(g0_woven[:], S, "g0", "g0_codes")
-
-        g10_codes = keep.tile([P, HALF], U32, name="g10_codes", align_bytes=64)
-        g10_scales = keep.tile([P, HALF], U8, name="g10_scales", align_bytes=64)
-        for u in range(2):
-            cols = slice(HALF // 2 * u, HALF // 2 * (u + 1))
-            nc.vector.quantize_mx(
-                out=g10_codes[:, cols].bitcast(E4M3), scales=g10_scales[:, cols], in_=g10_woven[:, S * u : S * (u + 1)]
-            )
-        g_q[1, 0] = (g10_codes[:], g10_scales[:])
         wgo_rows = wgo.rearrange("(q t) j -> q (t j)", t=PACK)
         wgo_tiles = []
         for u in range(2):
@@ -292,7 +278,7 @@ def tile_list_dislocation_recurrent_backward_kernel(
         y_pairs = {}
 
         chunks = [(0, 256), (256, 768), (768, 1280), (1280, 1792), (1792, 2048)]
-        pair_slots = list(GRADIENT_SLOT.values()) + [(1, 1)]
+        pair_slots = list(GRADIENT_SLOT.values()) + [(1, 2)]
 
         def pair_up(t):
             for c, (lo, hi) in enumerate(chunks):
@@ -324,7 +310,7 @@ def tile_list_dislocation_recurrent_backward_kernel(
         for sides in later:
             nc.vector.tensor_tensor(*sides, ADD)
         for b in range(GROUPS):
-            b_q[b, 0], wo_q[b] = quantize(b0_wo_woven[b][:], S, f"b0_wo{b}", ["slot02", "g0_codes"][b])
+            b_q[b, 0], wo_q[b] = quantize(b0_wo_woven[b][:], S, f"b0_wo{b}", ["slot10", "g0_codes"][b])
         e32_pairs = [staging(u, [P, 2 * S], F32, f"e32_pair{u}") for u in range(2)]
         e32 = [e32_pairs[t // 2][:, S * (t % 2) : S * (t % 2 + 1)] for t in range(PACK)]
         output_product(0, 0, e32[0][:, half(0)])

@@ -23,7 +23,7 @@ PASS = P * PACK
 HALF = 512
 HALVES = S // HALF
 GROUPS = H // PASS
-GRADIENT_SLOT = {(0, 0): (1, 3), (0, 1): (1, 1), (1, 0): (0, 2), (1, 1): (0, 3)}
+GRADIENT_SLOT = {(0, 0): (1, 1), (0, 1): (0, 2), (1, 0): (1, 3), (1, 1): (0, 3)}
 
 
 def tile_list_dislocation_recurrent_backward_kernel(
@@ -126,14 +126,14 @@ def tile_list_dislocation_recurrent_backward_kernel(
                 load_weight(w1_raw[1], w1_rows[1])
             load_state(a, t)
         nc.sync.dma_start(scatter_list[:], offs2)
+        wr_w_raw = in_slot((0, 1), [P, GROUPS, H], I32, "wr_w_raw")
+        nc.sync.dma_start(out=wr_w_raw[:], in_=wr_words.rearrange("a p c i -> p a (c i)").bitcast(I32))
         for a in range(GROUPS):
             for q in range(4):
                 nc.sync.dma_start(
                     out=wr_s_raw[32 * q + 8 * a : 32 * q + 8 * a + 8, :].bitcast(I32),
                     in_=wr_scales[a, 4 * q : 4 * q + 4, :].bitcast(I32).rearrange("r (b c) -> b r c", b=GROUPS),
                 )
-        wr_w_raw = in_slot((0, 1), [P, GROUPS, H], I32, "wr_w_raw")
-        nc.sync.dma_start(out=wr_w_raw[:], in_=wr_words.rearrange("a p c i -> p a (c i)").bitcast(I32))
         wo_raw = [staging(a, [P, PACK, HALF], F32, f"wo_raw{a}") for a in range(GROUPS)]
         for a in range(GROUPS):
             load_weight(wo_raw[a], wo_rows[a])
@@ -154,8 +154,11 @@ def tile_list_dislocation_recurrent_backward_kernel(
             nc.vector.tensor_copy(d, s_tiles[a, t][:].indirect(gather_list[:]))
             if (a, t) == tiles[-1]:
                 parts = [
-                    (half(j), in_slot(GRADIENT_SLOT[a, j], [P, HALF], F32, f"rest_last{j}")) for j in range(HALVES)
+                    (half(0), in_slot(GRADIENT_SLOT[0, 1], [P, HALF], F32, "rest_last0")),
+                    (half(1), work.tile([P, HALF], F32, name="rest_last1", tag="g00_codes", bufs=1, align_bytes=64)),
                 ]
+            elif (a, t) == tiles[-2]:
+                parts = [(slice(0, S), in_slot(GRADIENT_SLOT[1, 1], [P, S], F32, "rest12"))]
             else:
                 parts = [(slice(0, S), work.tile([P, S], F32, name=f"rest{a}{t}", tag="rest", bufs=2))]
             for cols, rest in parts:
@@ -192,33 +195,33 @@ def tile_list_dislocation_recurrent_backward_kernel(
         for a, t in tiles[1:6]:
             derivative(a, t)
         for t in range(PACK):
-            gate(0, t, 1)
+            gate(0, t, 0)
         derivative(1, 2)
         quantize_w1(1)
         derivative(1, 3)
-        for a in range(GROUPS):
-            for t in range(PACK):
-                gate(a, t, 0)
-        g0_woven = wide("g0_woven")
-        for j in reversed(range(HALVES)):
-            weave(g32[0, j], side(g0_woven, j), parts=2)
+        g00_woven = weave(g32[0, 0], woven("g00_woven")[:], parts=2)
+        for t in range(PACK):
+            gate(1, t, 0)
         g10_woven = weave(g32[1, 0], woven("g10_woven")[:])
+        for t in range(PACK):
+            gate(0, t, 1)
         nc.vector.tensor_copy(
             out=wr_s[:].rearrange("p (t q) -> p q t", t=PACK),
             in_=wr_s_raw[:].rearrange("p (q t) -> p q t", t=PACK),
         )
         wr_w = in_slot((1, 0), [P, GROUPS * H], I32, "wr_w")
-        for u in range(GROUPS * GROUPS):
-            nc.gpsimd.tensor_copy(
-                out=wr_w[:, PASS * u : PASS * (u + 1)].rearrange("p (t q) -> p t q", t=PACK),
-                in_=wr_w_raw[:].rearrange("p a (b q t) -> p (a b) t q", t=PACK, q=P)[:, u],
-            )
+        nc.vector.tensor_copy(
+            out=wr_w[:].rearrange("p (b t q) -> p b q t", t=PACK, q=P),
+            in_=wr_w_raw[:].rearrange("p a (b q t) -> p (a b) q t", t=PACK, q=P),
+        )
         g_q = {}
-        g_q[0, 0], g_q[0, 1] = quantize(g0_woven[:], S, "g0", "g0_codes")
+        g_q[0, 0] = quantize(g00_woven, HALF, "g00", "g00_codes")[0]
         g_q[1, 0] = quantize(g10_woven, HALF, "g10", "g10_codes")[0]
         for t in range(PACK):
             gate(1, t, 1)
-        g11_woven = weave(g32[1, 1], woven("g11_woven")[:])
+        g1_woven = wide("g1_woven")
+        for a in range(GROUPS):
+            weave(g32[a, 1], side(g1_woven, a))
         b0_wo_woven = [wide(f"b0_wo_woven{a}") for a in range(GROUPS)]
         for a in range(GROUPS):
             weave_weight(wo_raw[a], side(b0_wo_woven[a], 1), parts=2)
@@ -251,11 +254,11 @@ def tile_list_dislocation_recurrent_backward_kernel(
                 term = work.tile([P, PACK, P], F32, name=f"term{b}{j}{u}", tag="term", bufs=4, align_bytes=64)
                 c0 = HALF * j + P * u
                 nc.vector.tensor_tensor(term[:], rec[:], deriv[b][:, :, c0 : c0 + P], MULT)
-                sides = by_word(dst[:, PASS * u : PASS * (u + 1)]), by_lane(term[:]), by_lane(g32[b, j][:, :, lane(u)])
+                out = by_word(dst[:, PASS * u : PASS * (u + 1)])
                 if u < on_gpsimd:
-                    nc.gpsimd.tensor_tensor(*sides, ADD)
+                    nc.gpsimd.tensor_tensor(out, by_lane(term[:]), by_lane(g32[b, j][:, :, lane(u)]), ADD)
                 else:
-                    later.append(sides)
+                    later.append((out, term, g32[b, j][:, :, lane(u)]))
             return later
 
         def recurrent_by_lanes(b, j, dst, repeated):
@@ -275,16 +278,13 @@ def tile_list_dislocation_recurrent_backward_kernel(
         b_q = {}
 
         y_rows = out_0.rearrange("(p t) m -> t p m", t=PACK)
-        y_pairs = {}
+        woven_slots = list(GRADIENT_SLOT.values())
+        y_woven = {}
 
-        chunks = [(0, 256), (256, 768), (768, 1280), (1280, 1792), (1792, 2048)]
-        pair_slots = list(GRADIENT_SLOT.values()) + [(1, 2)]
-
-        def pair_up(t):
-            for c, (lo, hi) in enumerate(chunks):
-                if t == 0:
-                    y_pairs[c] = in_slot(pair_slots[c], [P, 2, hi - lo, 2], BF16, f"y_pairs{c}")
-                nc.scalar.copy(out=y_pairs[c][:, t // 2, :, t % 2], in_=pages[t][:, lo:hi])
+        def weave_page(t, c, copy):
+            if c not in y_woven:
+                y_woven[c] = in_slot(woven_slots[c], [P, HALF, PACK], BF16, f"y_woven{c}")
+            copy(out=y_woven[c][:, :, t], in_=pages[t][:, half(c)])
 
         def output_product(t, j, dst):
             e = psum.tile([P, HALF], F32, name=f"e{t}{j}", tag="sum", bufs=8)
@@ -302,46 +302,54 @@ def tile_list_dislocation_recurrent_backward_kernel(
 
         wo_q = {}
         recurrent_by_columns(0, 0, side(b0_wo_woven[0], 0), PACK)
-        g_q[1, 1] = quantize(g11_woven, HALF, "g11", "g11_codes")[0]
+        g_q[0, 1], g_q[1, 1] = quantize(g1_woven[:], S, "g1", "g1_codes")
         recurrent_by_lanes(1, 0, side(b0_wo_woven[1], 0), PACK)
         b1_woven = wide("b1_woven")
         later = recurrent_by_columns(0, 1, side(b1_woven, 0), 2)
         recurrent_by_lanes(1, 1, side(b1_woven, 1), 2)
-        for sides in later:
-            nc.vector.tensor_tensor(*sides, ADD)
+        for out, term, gradient in later:
+            nc.vector.tensor_tensor(term[:], term[:], gradient, ADD)
+            nc.scalar.copy(out=out, in_=by_lane(term[:]))
         for b in range(GROUPS):
-            b_q[b, 0], wo_q[b] = quantize(b0_wo_woven[b][:], S, f"b0_wo{b}", ["slot10", "g0_codes"][b])
-        e32_pairs = [staging(u, [P, 2 * S], F32, f"e32_pair{u}") for u in range(2)]
-        e32 = [e32_pairs[t // 2][:, S * (t % 2) : S * (t % 2 + 1)] for t in range(PACK)]
-        output_product(0, 0, e32[0][:, half(0)])
-        b_q[0, 1], b_q[1, 1] = quantize(b1_woven[:], S, "b1", "b1_codes")
-        output_product(0, 1, e32[0][:, half(1)])
-        for t in range(1, PACK):
+            b_q[b, 0], wo_q[b] = quantize(b0_wo_woven[b][:], S, f"b0_wo{b}", ["slot10", "g1_codes"][b])
+        page_order = [2, 0, 1, 3]
+        e32 = {}
+
+        def output_products(t, bytes_of):
+            e32[t] = staging(bytes_of, [P, S], F32, f"e32_{t}")
             for j in range(HALVES):
+                if (t, j) == (page_order[0], 1):
+                    b_q[0, 1], b_q[1, 1] = quantize(b1_woven[:], S, "b1", "b1_codes")
                 output_product(t, j, e32[t][:, half(j)])
-        for j in range(HALVES):
-            place(0, entries(scatter_list, j), e32[0][:, half(j)], half(j))
-        for t in range(PACK):
-            if t > 0:
-                place(t, scatter_list[:], e32[t], slice(0, S))
+
+        for i, t in enumerate(page_order[:-1]):
+            output_products(t, i)
+        chunks = T2 // HALF
+        for i, t in enumerate(page_order):
+            if i == 0:
+                for j in range(HALVES):
+                    place(t, entries(scatter_list, j), e32[t][:, half(j)], half(j))
+            else:
+                place(t, scatter_list[:], e32[t][:], slice(0, S))
             nc.sync.dma_start(out=y_rows[t], in_=pages[t][:])
-            pair_up(t)
+            for c in range(chunks):
+                if i < PACK - 1:
+                    weave_page(t, (c + 1) % chunks, nc.scalar.copy)
+                elif c == 0:
+                    weave_page(t, c, nc.scalar.copy)
+                else:
+                    weave_page(t, c, nc.vector.tensor_copy)
+            if i == 0:
+                output_products(page_order[-1], 0)
 
         words_out = out_1[0].rearrange("p m t -> p (m t)").bitcast(I32)
-        y_woven = {}
-        y_codes = staging(2, [P, T2], U32, "y_codes")
-        for c in range(len(chunks) + 1):
-            if c < len(chunks):
-                width = chunks[c][1] - chunks[c][0]
-                y_woven[c] = woven(f"y_woven{c}")[:, 0 : PACK * width]
-                nc.vector.tensor_copy(
-                    out=y_woven[c].bitcast(F32).rearrange("p (m u) -> p m u", u=2),
-                    in_=y_pairs[c][:].rearrange("p u m e -> p u (m e)").bitcast(F32).rearrange("p u m -> p m u"),
-                )
-            if c > 0:
-                cols = slice(*chunks[c - 1])
-                nc.vector.quantize_mx(out=y_codes[:, cols].bitcast(E4M3), scales=y_scales[:, cols], in_=y_woven[c - 1])
-                nc.sync.dma_start(out=words_out[:, cols], in_=y_codes[:, cols].bitcast(I32))
+        y_codes = in_slot((1, 2), [P, T2], U32, "y_codes")
+        for c in [1, 2, 0, 3]:
+            nc.vector.quantize_mx(
+                out=y_codes[:, half(c)].bitcast(E4M3), scales=y_scales[:, half(c)],
+                in_=y_woven[c][:].rearrange("p m t -> p (m t)"),
+            )
+            nc.sync.dma_start(out=words_out[:, half(c)], in_=y_codes[:, half(c)].bitcast(I32))
         for q in range(4):
             queue = nc.sync if q % 2 == 0 else nc.scalar
             queue.dma_start(

@@ -23,7 +23,7 @@ PASS = P * PACK
 HALF = 512
 HALVES = S // HALF
 GROUPS = H // PASS
-GRADIENT_SLOT = {(0, 0): (1, 1), (0, 1): (0, 2), (1, 0): (1, 3), (1, 1): (0, 3)}
+GRADIENT_SLOT = {(0, 0): (1, 1), (0, 1): (0, 1), (1, 0): (1, 3), (1, 1): (0, 3)}
 
 
 def tile_list_dislocation_recurrent_backward_kernel(
@@ -113,20 +113,22 @@ def tile_list_dislocation_recurrent_backward_kernel(
         w1_rows = [w1[:, PASS * a : PASS * (a + 1)] for a in range(GROUPS)]
         wo_rows = [wo[PASS * a : PASS * (a + 1), :] for a in range(GROUPS)]
         nc.sync.dma_start(gather_list[:], offs)
+        tiles = [(a, t) for a in range(GROUPS) for t in range(PACK)]
+        for a, t in tiles[:2]:
+            load_state(a, t)
         nc.sync.dma_start(out=tab_w[:].bitcast(I32), in_=tab_words[0].rearrange("p t i -> p (t i)").bitcast(I32))
         for q in range(4):
             nc.sync.dma_start(
                 out=tab_s[32 * q : 32 * q + 4, :].bitcast(I32), in_=tab_scales[0, 4 * q : 4 * q + 4, :].bitcast(I32)
             )
         w1_raw = [staging(1 + a, [P, PACK, HALF], F32, f"w1_raw{a}") for a in range(GROUPS)]
-        tiles = [(a, t) for a in range(GROUPS) for t in range(PACK)]
         load_weight(w1_raw[0], w1_rows[0])
-        for a, t in tiles:
+        for a, t in tiles[2:]:
             if (a, t) == (1, 2):
                 load_weight(w1_raw[1], w1_rows[1])
             load_state(a, t)
         nc.sync.dma_start(scatter_list[:], offs2)
-        wr_w_raw = in_slot((0, 1), [P, GROUPS, H], I32, "wr_w_raw")
+        wr_w_raw = in_slot((0, 2), [P, GROUPS, H], I32, "wr_w_raw")
         nc.sync.dma_start(out=wr_w_raw[:], in_=wr_words.rearrange("a p c i -> p a (c i)").bitcast(I32))
         for a in range(GROUPS):
             for q in range(4):
@@ -154,13 +156,13 @@ def tile_list_dislocation_recurrent_backward_kernel(
             nc.vector.tensor_copy(d, s_tiles[a, t][:].indirect(gather_list[:]))
             if (a, t) == tiles[-1]:
                 parts = [
-                    (half(0), in_slot(GRADIENT_SLOT[0, 1], [P, HALF], F32, "rest_last0")),
+                    (half(0), work.tile([P, HALF], F32, name="rest_last0", tag="rest", bufs=3)),
                     (half(1), work.tile([P, HALF], F32, name="rest_last1", tag="g00_codes", bufs=1, align_bytes=64)),
                 ]
             elif (a, t) == tiles[-2]:
                 parts = [(slice(0, S), in_slot(GRADIENT_SLOT[1, 1], [P, S], F32, "rest12"))]
             else:
-                parts = [(slice(0, S), work.tile([P, S], F32, name=f"rest{a}{t}", tag="rest", bufs=2))]
+                parts = [(slice(0, S), work.tile([P, S], F32, name=f"rest{a}{t}", tag="rest", bufs=3))]
             for cols, rest in parts:
                 nc.scalar.activation(out=rest[:], in_=d[:, cols], func=COPY, scale=-1.0, bias=1.0)
                 for c in range(cols.start, cols.stop, HALF):
@@ -177,22 +179,29 @@ def tile_list_dislocation_recurrent_backward_kernel(
                 rhs=v_w[:, half(j)].bitcast(E5M2), rhs_scale=v_s[:, half(j)], start=True, stop=stop,
             )
 
-        def gate(a, t, j):
+        def gate(a, t, j, on_gpsimd=False):
             if t == 0:
                 g32[a, j] = in_slot(GRADIENT_SLOT[a, j], [P, PACK, HALF], F32, f"g{a}{j}")
             h = psum.tile([P, HALF], F32, name=f"h{a}{t}{j}", tag="sum", bufs=8)
             first_product(h, a, t, j, stop=True)
-            nc.vector.tensor_tensor(g32[a, j][:, t, :], h[:], deriv[a][:, t, half(j)], MULT)
+            if on_gpsimd:
+                nc.scalar.copy(out=g32[a, j][:, t, :], in_=h[:])
+                nc.gpsimd.tensor_tensor(g32[a, j][:, t, :], g32[a, j][:, t, :], deriv[a][:, t, half(j)], MULT)
+            else:
+                nc.vector.tensor_tensor(g32[a, j][:, t, :], h[:], deriv[a][:, t, half(j)], MULT)
 
         def quantize_w1(a):
             w1_woven = weave_weight(w1_raw[a], woven(f"w1_woven{a}")[:])
             w1_q[a] = quantize(w1_woven, HALF, f"w1_{a}", ["slot00", "slot12"][a])[0]
 
+        for a, t in tiles[:2]:
+            derivative(a, t)
         nc.vector.tensor_copy(v_w[:], tab_w[:].indirect(gather_list[:]))
         nc.vector.tensor_copy(v_s[:], tab_s[:].indirect(gather_list[:]))
-        derivative(0, 0)
         quantize_w1(0)
-        for a, t in tiles[1:6]:
+        for t in range(2):
+            gate(0, t, 1, on_gpsimd=True)
+        for a, t in tiles[2:6]:
             derivative(a, t)
         for t in range(PACK):
             gate(0, t, 0)
@@ -203,7 +212,7 @@ def tile_list_dislocation_recurrent_backward_kernel(
         for t in range(PACK):
             gate(1, t, 0)
         g10_woven = weave(g32[1, 0], woven("g10_woven")[:])
-        for t in range(PACK):
+        for t in range(2, PACK):
             gate(0, t, 1)
         nc.vector.tensor_copy(
             out=wr_s[:].rearrange("p (t q) -> p q t", t=PACK),
@@ -229,7 +238,7 @@ def tile_list_dislocation_recurrent_backward_kernel(
         wgo_rows = wgo.rearrange("(q t) j -> q (t j)", t=PACK)
         wgo_tiles = []
         for u in range(2):
-            rows = in_slot((0, u), [P, 2 * S], F32, f"wgo{u}")
+            rows = in_slot((0, 2 * u), [P, 2 * S], F32, f"wgo{u}")
             nc.sync.dma_start(out=rows[:], in_=wgo_rows[:, 2 * S * u : 2 * S * (u + 1)].partition_broadcast(4))
             wgo_tiles.append(rows)
 
@@ -278,15 +287,18 @@ def tile_list_dislocation_recurrent_backward_kernel(
         b_q = {}
 
         y_rows = out_0.rearrange("(p t) m -> t p m", t=PACK)
-        woven_slots = list(GRADIENT_SLOT.values())
+        chunks = [slice(0, 512), slice(512, 1024), slice(1024, 1280), slice(1280, 1792), slice(1792, 2048)]
+        on_vector = 3
+        woven_slots = list(GRADIENT_SLOT.values()) + [(1, 0)]
         y_woven = {}
 
         def weave_page(t, c, copy):
+            cols = chunks[c]
             if c not in y_woven:
-                y_woven[c] = in_slot(woven_slots[c], [P, HALF, PACK], BF16, f"y_woven{c}")
-            copy(out=y_woven[c][:, :, t], in_=pages[t][:, half(c)])
+                y_woven[c] = in_slot(woven_slots[c], [P, cols.stop - cols.start, PACK], BF16, f"y_woven{c}")
+            copy(out=y_woven[c][:, :, t], in_=pages[t][:, cols])
 
-        def output_product(t, j, dst):
+        def output_product(t, j):
             e = psum.tile([P, HALF], F32, name=f"e{t}{j}", tag="sum", bufs=8)
             for b in range(GROUPS):
                 nc.tensor.matmul_mx(
@@ -294,7 +306,7 @@ def tile_list_dislocation_recurrent_backward_kernel(
                     rhs=b_q[b, j][0].bitcast(E4M3), rhs_scale=b_q[b, j][1],
                     start=(b == 0), stop=(b == GROUPS - 1),
                 )
-            nc.scalar.copy(out=dst, in_=e[:])
+            return e
 
         def place(t, lst, src, cols):
             weights = wgo_tiles[t // 2][:, S * (t % 2) : S * (t % 2 + 1)]
@@ -305,7 +317,7 @@ def tile_list_dislocation_recurrent_backward_kernel(
         g_q[0, 1], g_q[1, 1] = quantize(g1_woven[:], S, "g1", "g1_codes")
         recurrent_by_lanes(1, 0, side(b0_wo_woven[1], 0), PACK)
         b1_woven = wide("b1_woven")
-        later = recurrent_by_columns(0, 1, side(b1_woven, 0), 2)
+        later = recurrent_by_columns(0, 1, side(b1_woven, 0), 3)
         recurrent_by_lanes(1, 1, side(b1_woven, 1), 2)
         for out, term, gradient in later:
             nc.vector.tensor_tensor(term[:], term[:], gradient, ADD)
@@ -313,43 +325,40 @@ def tile_list_dislocation_recurrent_backward_kernel(
         for b in range(GROUPS):
             b_q[b, 0], wo_q[b] = quantize(b0_wo_woven[b][:], S, f"b0_wo{b}", ["slot10", "g1_codes"][b])
         page_order = [2, 0, 1, 3]
-        e32 = {}
-
-        def output_products(t, bytes_of):
-            e32[t] = staging(bytes_of, [P, S], F32, f"e32_{t}")
+        first_and_last = staging(0, [P, 2 * S - P], F32, "e32_first_and_last")
+        e32 = {page_order[0]: first_and_last[:, 0:S], page_order[-1]: first_and_last[:, S - P : 2 * S - P]}
+        for i in (1, 2):
+            e32[page_order[i]] = staging(i, [P, S], F32, f"e32_{i}")[:]
+        for t in page_order:
             for j in range(HALVES):
                 if (t, j) == (page_order[0], 1):
                     b_q[0, 1], b_q[1, 1] = quantize(b1_woven[:], S, "b1", "b1_codes")
-                output_product(t, j, e32[t][:, half(j)])
-
-        for i, t in enumerate(page_order[:-1]):
-            output_products(t, i)
-        chunks = T2 // HALF
+                e = output_product(t, j)
+                if (t, j) == (page_order[-1], 0):
+                    held = e
+                    nc.scalar.copy(out=e32[t][:, P:HALF], in_=e[:, P:HALF])
+                else:
+                    nc.scalar.copy(out=e32[t][:, half(j)], in_=e[:])
         for i, t in enumerate(page_order):
             if i == 0:
                 for j in range(HALVES):
                     place(t, entries(scatter_list, j), e32[t][:, half(j)], half(j))
             else:
-                place(t, scatter_list[:], e32[t][:], slice(0, S))
+                place(t, scatter_list[:], e32[t], slice(0, S))
             nc.sync.dma_start(out=y_rows[t], in_=pages[t][:])
-            for c in range(chunks):
-                if i < PACK - 1:
-                    weave_page(t, (c + 1) % chunks, nc.scalar.copy)
-                elif c == 0:
-                    weave_page(t, c, nc.scalar.copy)
-                else:
-                    weave_page(t, c, nc.vector.tensor_copy)
+            for c in range(len(chunks)):
+                weave_page(t, c, nc.vector.tensor_copy if i == PACK - 1 and c < on_vector else nc.scalar.copy)
             if i == 0:
-                output_products(page_order[-1], 0)
+                nc.scalar.copy(out=e32[page_order[-1]][:, 0:P], in_=held[:, 0:P])
 
         words_out = out_1[0].rearrange("p m t -> p (m t)").bitcast(I32)
         y_codes = in_slot((1, 2), [P, T2], U32, "y_codes")
-        for c in [1, 2, 0, 3]:
+        for c, cols in enumerate(chunks):
             nc.vector.quantize_mx(
-                out=y_codes[:, half(c)].bitcast(E4M3), scales=y_scales[:, half(c)],
+                out=y_codes[:, cols].bitcast(E4M3), scales=y_scales[:, cols],
                 in_=y_woven[c][:].rearrange("p m t -> p (m t)"),
             )
-            nc.sync.dma_start(out=words_out[:, half(c)], in_=y_codes[:, half(c)].bitcast(I32))
+            nc.sync.dma_start(out=words_out[:, cols], in_=y_codes[:, cols].bitcast(I32))
         for q in range(4):
             queue = nc.sync if q % 2 == 0 else nc.scalar
             queue.dma_start(

@@ -42,10 +42,10 @@ def tile_list_dislocation_recurrent_backward_kernel(
             return work.tile(shape, dtype, name=name, tag=f"staging{u}", bufs=1, align_bytes=64)
 
         def woven(name):
-            return work.tile([P, PACK * HALF], BF16, name=name, tag="woven", bufs=3, align_bytes=64)
+            return work.tile([P, PACK * HALF], BF16, name=name, tag="woven", bufs=2, align_bytes=64)
 
-        def wide(name):
-            return work.tile([P, 2 * PACK * HALF], BF16, name=name, tag="wide", bufs=3, align_bytes=64)
+        def wide(u, name):
+            return work.tile([P, 2 * PACK * HALF], BF16, name=name, tag=f"wide{u}", bufs=1, align_bytes=64)
 
         def side(tile, u):
             return tile[:, PACK * HALF * u : PACK * HALF * (u + 1)]
@@ -88,7 +88,6 @@ def tile_list_dislocation_recurrent_backward_kernel(
         tab_w = staging(0, [P, T], U32, "tab_w")
         tab_s = keep.tile([P, T], U8, name="tab_s", align_bytes=64)
         wr_s_raw = keep.tile([P, PASS], U8, name="wr_s_raw", align_bytes=64)
-        wr_s = keep.tile([P, PASS], U8, name="wr_s", align_bytes=64)
         pages = [keep.tile([P, T2], F32, name=f"page{t}") for t in range(PACK)]
         y_scales = keep.tile([P, T2], U8, name="y_scales", align_bytes=64)
 
@@ -128,7 +127,7 @@ def tile_list_dislocation_recurrent_backward_kernel(
                 load_weight(w1_raw[1], w1_rows[1])
             load_state(a, t)
         nc.sync.dma_start(scatter_list[:], offs2)
-        wr_w_raw = in_slot((0, 2), [P, GROUPS, H], I32, "wr_w_raw")
+        wr_w_raw = in_slot((0, 0), [P, GROUPS, H], I32, "wr_w_raw")
         nc.sync.dma_start(out=wr_w_raw[:], in_=wr_words.rearrange("a p c i -> p a (c i)").bitcast(I32))
         for a in range(GROUPS):
             for q in range(4):
@@ -155,20 +154,33 @@ def tile_list_dislocation_recurrent_backward_kernel(
             d = deriv[a][:, t, :]
             nc.vector.tensor_copy(d, s_tiles[a, t][:].indirect(gather_list[:]))
             if (a, t) == tiles[-1]:
+                width = S // 4
+                tags = ["rest", "slot03", "g00_codes", "slot10"]
                 parts = [
-                    (half(0), work.tile([P, HALF], F32, name="rest_last0", tag="rest", bufs=3)),
-                    (half(1), work.tile([P, HALF], F32, name="rest_last1", tag="g00_codes", bufs=1, align_bytes=64)),
+                    (
+                        slice(width * u, width * (u + 1)),
+                        work.tile([P, width], F32, name=f"rest_last{u}", tag=tag, bufs=3 if u == 0 else 1, align_bytes=64),
+                    )
+                    for u, tag in enumerate(tags)
                 ]
-            elif (a, t) == tiles[-2]:
-                parts = [(slice(0, S), in_slot(GRADIENT_SLOT[1, 1], [P, S], F32, "rest12"))]
             else:
-                parts = [(slice(0, S), work.tile([P, S], F32, name=f"rest{a}{t}", tag="rest", bufs=3))]
+                parts = [(slice(0, S), work.tile([P, S], F32, name=f"rest{a}{t}", tag="rest", bufs=3, align_bytes=64))]
             for cols, rest in parts:
                 nc.scalar.activation(out=rest[:], in_=d[:, cols], func=COPY, scale=-1.0, bias=1.0)
-                for c in range(cols.start, cols.stop, HALF):
+                step = min(HALF, cols.stop - cols.start)
+                for c in range(cols.start, cols.stop, step):
                     nc.gpsimd.tensor_tensor(
-                        d[:, c : c + HALF], d[:, c : c + HALF], rest[:, c - cols.start : c - cols.start + HALF], MULT
+                        d[:, c : c + step], d[:, c : c + step], rest[:, c - cols.start : c - cols.start + step], MULT
                     )
+
+        def bank(k, shape, name):
+            return psum.tile(shape, F32, name=name, tag=f"bank{k}", bufs=1)
+
+        gate_banks = [0, 1, 2, 3, 4, 5, 6, 7, 0, 1, 6, 7, 2, 3, 4, 5]
+        later_banks = [0, 6, 7, 1, 2, 3, 4, 5] * 3
+
+        def later_bank(shape, name):
+            return bank(later_banks.pop(0), shape, name)
 
         def lane(t):
             return slice(P * t, P * (t + 1))
@@ -182,7 +194,7 @@ def tile_list_dislocation_recurrent_backward_kernel(
         def gate(a, t, j, on_gpsimd=False):
             if t == 0:
                 g32[a, j] = in_slot(GRADIENT_SLOT[a, j], [P, PACK, HALF], F32, f"g{a}{j}")
-            h = psum.tile([P, HALF], F32, name=f"h{a}{t}{j}", tag="sum", bufs=8)
+            h = bank(gate_banks.pop(0), [P, HALF], f"h{a}{t}{j}")
             first_product(h, a, t, j, stop=True)
             if on_gpsimd:
                 nc.scalar.copy(out=g32[a, j][:, t, :], in_=h[:])
@@ -192,7 +204,7 @@ def tile_list_dislocation_recurrent_backward_kernel(
 
         def quantize_w1(a):
             w1_woven = weave_weight(w1_raw[a], woven(f"w1_woven{a}")[:])
-            w1_q[a] = quantize(w1_woven, HALF, f"w1_{a}", ["slot00", "slot12"][a])[0]
+            w1_q[a] = quantize(w1_woven, HALF, f"w1_{a}", ["g10_codes", "slot12"][a])[0]
 
         for a, t in tiles[:2]:
             derivative(a, t)
@@ -211,27 +223,29 @@ def tile_list_dislocation_recurrent_backward_kernel(
         g00_woven = weave(g32[0, 0], woven("g00_woven")[:], parts=2)
         for t in range(PACK):
             gate(1, t, 0)
-        g10_woven = weave(g32[1, 0], woven("g10_woven")[:])
+        g10_woven = weave(g32[1, 0], side(wide(0, "g10_woven"), 0))
         for t in range(2, PACK):
             gate(0, t, 1)
-        nc.vector.tensor_copy(
-            out=wr_s[:].rearrange("p (t q) -> p q t", t=PACK),
-            in_=wr_s_raw[:].rearrange("p (q t) -> p q t", t=PACK),
-        )
+        gate(1, 0, 1)
         wr_w = in_slot((1, 0), [P, GROUPS * H], I32, "wr_w")
         nc.vector.tensor_copy(
             out=wr_w[:].rearrange("p (b t q) -> p b q t", t=PACK, q=P),
             in_=wr_w_raw[:].rearrange("p a (b q t) -> p (a b) q t", t=PACK, q=P),
         )
+        wr_s = in_slot((0, 0), [P, PASS], U8, "wr_s")
+        nc.vector.tensor_copy(
+            out=wr_s[:].rearrange("p (t q) -> p q t", t=PACK),
+            in_=wr_s_raw[:].rearrange("p (q t) -> p q t", t=PACK),
+        )
         g_q = {}
         g_q[0, 0] = quantize(g00_woven, HALF, "g00", "g00_codes")[0]
         g_q[1, 0] = quantize(g10_woven, HALF, "g10", "g10_codes")[0]
-        for t in range(PACK):
+        g01_woven = weave(g32[0, 1], woven("g01_woven")[:], parts=4)
+        for t in range(1, PACK):
             gate(1, t, 1)
-        g1_woven = wide("g1_woven")
-        for a in range(GROUPS):
-            weave(g32[a, 1], side(g1_woven, a))
-        b0_wo_woven = [wide(f"b0_wo_woven{a}") for a in range(GROUPS)]
+        g11_woven = weave(g32[1, 1], side(wide(1, "g11_woven"), 0))
+        g_q[0, 1] = quantize(g01_woven, HALF, "g01", "g01_codes")[0]
+        b0_wo_woven = [wide(a, f"b0_wo_woven{a}") for a in range(GROUPS)]
         for a in range(GROUPS):
             weave_weight(wo_raw[a], side(b0_wo_woven[a], 1), parts=2)
 
@@ -254,11 +268,12 @@ def tile_list_dislocation_recurrent_backward_kernel(
         def recurrent_by_columns(b, j, dst, on_gpsimd):
             later = []
             for u in range(HALF // P):
-                rec = psum.tile([P, PACK, P], F32, name=f"rec{b}{j}c{u}", tag="sum", bufs=8)
-                for a in range(GROUPS):
+                rec = later_bank([P, PACK, P], f"rec{b}{j}c{u}")
+                for i in range(GROUPS):
                     for t in range(PACK):
                         recurrent_pass(
-                            rec[:, t, :], a, b, t, j, lane(u), (a, t) == (0, 0), (a, t) == (GROUPS - 1, PACK - 1)
+                            rec[:, t, :], i, b, t, j, lane(u),
+                            (i, t) == (0, 0), (i, t) == (GROUPS - 1, PACK - 1),
                         )
                 term = work.tile([P, PACK, P], F32, name=f"term{b}{j}{u}", tag="term", bufs=4, align_bytes=64)
                 c0 = HALF * j + P * u
@@ -271,18 +286,24 @@ def tile_list_dislocation_recurrent_backward_kernel(
             return later
 
         def recurrent_by_lanes(b, j, dst, repeated):
-            for t in range(PACK):
-                rec = psum.tile([P, HALF], F32, name=f"rec{b}{t}{j}", tag="sum", bufs=8)
+            for t in reversed(range(PACK)):
+                rec = later_bank([P, HALF], f"rec{b}{t}{j}")
                 again = t < repeated
                 if again:
                     first_product(rec, b, t, j, stop=False)
-                for a in range(GROUPS):
-                    recurrent_pass(rec[:], a, b, t, j, half(0), a == 0 and not again, a == GROUPS - 1)
+                for i in range(GROUPS):
+                    recurrent_pass(rec[:], i, b, t, j, half(0), i == 0 and not again, i == GROUPS - 1)
                 d = deriv[b][:, t, half(j)]
                 nc.vector.tensor_tensor(g32[b, j][:, t, :] if again else d, rec[:], d, MULT)
-            for t in range(repeated, PACK):
-                nc.vector.tensor_tensor(g32[b, j][:, t, :], g32[b, j][:, t, :], deriv[b][:, t, half(j)], ADD)
-            weave(g32[b, j], dst)
+            if repeated == PACK:
+                weave(g32[b, j], dst)
+                return
+            width = HALF // 2
+            for u in range(2):
+                cols = slice(width * u, width * (u + 1))
+                gradient = g32[b, j][:, repeated:PACK, cols]
+                nc.vector.tensor_tensor(gradient, gradient, deriv[b][:, repeated:PACK, half(j)][:, :, cols], ADD)
+            weave(g32[b, j], dst, parts=2)
 
         b_q = {}
 
@@ -299,7 +320,7 @@ def tile_list_dislocation_recurrent_backward_kernel(
             copy(out=y_woven[c][:, :, t], in_=pages[t][:, cols])
 
         def output_product(t, j):
-            e = psum.tile([P, HALF], F32, name=f"e{t}{j}", tag="sum", bufs=8)
+            e = later_bank([P, HALF], f"e{t}{j}")
             for b in range(GROUPS):
                 nc.tensor.matmul_mx(
                     out=e[:], lhsT=wo_q[b][0][:, lane(t)].bitcast(E4M3), lhsT_scale=wo_q[b][1][:, lane(t)],
@@ -314,25 +335,24 @@ def tile_list_dislocation_recurrent_backward_kernel(
 
         wo_q = {}
         recurrent_by_columns(0, 0, side(b0_wo_woven[0], 0), PACK)
-        g_q[0, 1], g_q[1, 1] = quantize(g1_woven[:], S, "g1", "g1_codes")
+        g_q[1, 1] = quantize(g11_woven, HALF, "g11", "g11_codes")[0]
         recurrent_by_lanes(1, 0, side(b0_wo_woven[1], 0), PACK)
-        b1_woven = wide("b1_woven")
-        later = recurrent_by_columns(0, 1, side(b1_woven, 0), 3)
+        b1_woven = wide(2, "b1_woven")
+        later = recurrent_by_columns(0, 1, side(b1_woven, 0), 2)
         recurrent_by_lanes(1, 1, side(b1_woven, 1), 2)
+        b_q[0, 0], wo_q[0] = quantize(b0_wo_woven[0][:], S, "b0_wo0", "slot10")
         for out, term, gradient in later:
             nc.vector.tensor_tensor(term[:], term[:], gradient, ADD)
             nc.scalar.copy(out=out, in_=by_lane(term[:]))
-        for b in range(GROUPS):
-            b_q[b, 0], wo_q[b] = quantize(b0_wo_woven[b][:], S, f"b0_wo{b}", ["slot10", "g1_codes"][b])
+        b_q[1, 0], wo_q[1] = quantize(b0_wo_woven[1][:], S, "b0_wo1", "g11_codes")
+        b_q[0, 1], b_q[1, 1] = quantize(b1_woven[:], S, "b1", "b1_codes")
         page_order = [2, 0, 1, 3]
         first_and_last = staging(0, [P, 2 * S - P], F32, "e32_first_and_last")
         e32 = {page_order[0]: first_and_last[:, 0:S], page_order[-1]: first_and_last[:, S - P : 2 * S - P]}
         for i in (1, 2):
             e32[page_order[i]] = staging(i, [P, S], F32, f"e32_{i}")[:]
-        for t in page_order:
-            for j in range(HALVES):
-                if (t, j) == (page_order[0], 1):
-                    b_q[0, 1], b_q[1, 1] = quantize(b1_woven[:], S, "b1", "b1_codes")
+        for j in range(HALVES):
+            for t in page_order:
                 e = output_product(t, j)
                 if (t, j) == (page_order[-1], 0):
                     held = e
@@ -345,7 +365,7 @@ def tile_list_dislocation_recurrent_backward_kernel(
                     place(t, entries(scatter_list, j), e32[t][:, half(j)], half(j))
             else:
                 place(t, scatter_list[:], e32[t], slice(0, S))
-            nc.sync.dma_start(out=y_rows[t], in_=pages[t][:])
+            nc.scalar.dma_start(out=y_rows[t], in_=pages[t][:])
             for c in range(len(chunks)):
                 weave_page(t, c, nc.vector.tensor_copy if i == PACK - 1 and c < on_vector else nc.scalar.copy)
             if i == 0:

@@ -93,8 +93,9 @@ def tile_list_dislocation_recurrent_backward_kernel(
 
         nc.gpsimd.memset(tab_s[:].bitcast(I32), 0)
         nc.gpsimd.memset(wr_s_raw[:].bitcast(I32), 0)
-        for page in pages:
-            nc.gpsimd.memset(page[:], 0.0)
+        for t, page in enumerate(pages):
+            engine = nc.vector if t < 2 else nc.gpsimd
+            engine.memset(page[:], 0.0)
 
         s_rows = sT.rearrange("(a p t) c -> a t p c", p=P, t=PACK)
         s_tiles = {}
@@ -252,7 +253,7 @@ def tile_list_dislocation_recurrent_backward_kernel(
         wgo_rows = wgo.rearrange("(q t) j -> q (t j)", t=PACK)
         wgo_tiles = []
         for u in range(2):
-            rows = in_slot((0, 2 * u), [P, 2 * S], F32, f"wgo{u}")
+            rows = staging(2, [P, 2 * S], F32, "wgo0") if u == 0 else in_slot((0, 2), [P, 2 * S], F32, "wgo1")
             nc.sync.dma_start(out=rows[:], in_=wgo_rows[:, 2 * S * u : 2 * S * (u + 1)].partition_broadcast(4))
             wgo_tiles.append(rows)
 
@@ -349,8 +350,8 @@ def tile_list_dislocation_recurrent_backward_kernel(
         page_order = [2, 0, 1, 3]
         first_and_last = staging(0, [P, 2 * S - P], F32, "e32_first_and_last")
         e32 = {page_order[0]: first_and_last[:, 0:S], page_order[-1]: first_and_last[:, S - P : 2 * S - P]}
-        for i in (1, 2):
-            e32[page_order[i]] = staging(i, [P, S], F32, f"e32_{i}")[:]
+        e32[page_order[1]] = staging(1, [P, S], F32, "e32_second")[:]
+        e32[page_order[2]] = in_slot((0, 0), [P, S], F32, "e32_third")[:]
         for j in range(HALVES):
             for t in page_order:
                 e = output_product(t, j)
@@ -365,7 +366,8 @@ def tile_list_dislocation_recurrent_backward_kernel(
                     place(t, entries(scatter_list, j), e32[t][:, half(j)], half(j))
             else:
                 place(t, scatter_list[:], e32[t], slice(0, S))
-            nc.scalar.dma_start(out=y_rows[t], in_=pages[t][:])
+            queue = nc.sync if i == PACK - 1 else nc.scalar
+            queue.dma_start(out=y_rows[t], in_=pages[t][:])
             for c in range(len(chunks)):
                 weave_page(t, c, nc.vector.tensor_copy if i == PACK - 1 and c < on_vector else nc.scalar.copy)
             if i == 0:

@@ -23,7 +23,6 @@ PASS = P * PACK
 HALF = 512
 HALVES = S // HALF
 GROUPS = H // PASS
-GRADIENT_SLOT = {(0, 0): (1, 1), (0, 1): (0, 1), (1, 0): (1, 3), (1, 1): (0, 3)}
 
 
 def tile_list_dislocation_recurrent_backward_kernel(
@@ -33,40 +32,51 @@ def tile_list_dislocation_recurrent_backward_kernel(
     with ExitStack() as ctx:
         keep = ctx.enter_context(tc.tile_pool(name="keep", bufs=1))
         work = ctx.enter_context(tc.tile_pool(name="work", bufs=1))
+        shared = ctx.enter_context(tc.tile_pool(name="shared", bufs=1))
         psum = ctx.enter_context(tc.psum_pool(name="psum", bufs=1))
 
-        def in_slot(slot, shape, dtype, name):
-            return work.tile(shape, dtype, name=name, tag=f"slot{slot[0]}{slot[1]}", bufs=1, align_bytes=64)
+        def at(tag, shape, dtype, name, bufs=1):
+            return work.tile(shape, dtype, name=name, tag=tag, bufs=bufs, align_bytes=64)
 
-        def staging(u, shape, dtype, name):
-            return work.tile(shape, dtype, name=name, tag=f"staging{u}", bufs=1, align_bytes=64)
+        def ring(k, shape, dtype, name):
+            return at(f"ring{k % 3}", shape, dtype, name)
 
-        def woven(name):
-            return work.tile([P, PACK * HALF], BF16, name=name, tag="woven", bufs=2, align_bytes=64)
+        def woven(shape, dtype, name):
+            return at("woven", shape, dtype, name, bufs=2)
 
-        def wide(u, name):
-            return work.tile([P, 2 * PACK * HALF], BF16, name=name, tag=f"wide{u}", bufs=1, align_bytes=64)
-
-        def side(tile, u):
-            return tile[:, PACK * HALF * u : PACK * HALF * (u + 1)]
-
-        def quantize(src, width, name, codes_tag):
-            codes = work.tile([P, width], U32, name=name + "_codes", tag=codes_tag, bufs=1, align_bytes=64)
-            scales = keep.tile([P, width], U8, name=name + "_scales", align_bytes=64)
-            nc.vector.quantize_mx(out=codes[:].bitcast(E4M3), scales=scales[:], in_=src)
-            return [(codes[:, half(u)], scales[:, half(u)]) for u in range(width // HALF)]
+        def bank(k, shape, name):
+            return psum.tile(shape, F32, name=name, tag=f"bank{k % 8}", bufs=1)
 
         def half(j):
             return slice(HALF * j, HALF * (j + 1))
 
-        def weave_weight(raw, dst, parts=1):
+        def lane(t):
+            return slice(P * t, P * (t + 1))
+
+        def side(tile, u):
+            return tile[:, PACK * HALF * u : PACK * HALF * (u + 1)]
+
+        def quantize(src, codes, name, parts=1):
+            width = codes.shape[1]
+            scales = keep.tile([P, width], U8, name=name + "_scales", align_bytes=64)
+            calls = []
+            for u in range(parts):
+                cols = slice(width // parts * u, width // parts * (u + 1))
+                calls.append(
+                    lambda cols=cols: nc.vector.quantize_mx(
+                        out=codes[:, cols].bitcast(E4M3), scales=scales[:, cols],
+                        in_=src[:, PACK * cols.start : PACK * cols.stop],
+                    )
+                )
+            return [(codes[:, half(u)], scales[:, half(u)]) for u in range(width // HALF)], calls
+
+        def weave_weight(copy, raw, dst, parts=1):
             width = P // parts
             for u in range(parts):
-                nc.scalar.copy(
+                copy(
                     out=dst.rearrange("p (t m i) -> p m i t", t=PACK, i=PACK)[:, width * u : width * (u + 1)],
                     in_=raw[:].rearrange("p i (m t) -> p m i t", t=PACK)[:, width * u : width * (u + 1)],
                 )
-            return dst
 
         def by_word(dst):
             return dst.rearrange("p (c i t) -> p c t i", t=PACK, i=4)
@@ -74,23 +84,23 @@ def tile_list_dislocation_recurrent_backward_kernel(
         def by_lane(src):
             return src.rearrange("p t (c i) -> p c t i", i=4)
 
-        def weave(src, dst, parts=1):
-            width = HALF // parts
-            for u in range(parts):
-                nc.scalar.copy(
-                    out=by_word(dst[:, PACK * width * u : PACK * width * (u + 1)]),
-                    in_=by_lane(src[:, :, width * u : width * (u + 1)]),
-                )
-            return dst
+        def weave(src, dst, cols):
+            nc.scalar.copy(out=by_word(dst[:, PACK * cols.start : PACK * cols.stop]), in_=by_lane(src[:, :, cols]))
+
+        def pieces(total, parts):
+            return [slice(total // parts * u, total // parts * (u + 1)) for u in range(parts)]
 
         gather_list = keep.tile([P, S // 16], U16, name="gather_list")
         scatter_list = keep.tile([P, S // 16], U16, name="scatter_list")
-        tab_w = staging(0, [P, T], U32, "tab_w")
         tab_s = keep.tile([P, T], U8, name="tab_s", align_bytes=64)
-        wr_s_raw = keep.tile([P, PASS], U8, name="wr_s_raw", align_bytes=64)
-        pages = [keep.tile([P, T2], F32, name=f"page{t}") for t in range(PACK)]
         y_scales = keep.tile([P, T2], U8, name="y_scales", align_bytes=64)
-
+        v_w = keep.tile([P, S], U32, name="v_w", align_bytes=64)
+        v_s = keep.tile([P, S], U8, name="v_s", align_bytes=64)
+        deriv = [keep.tile([P, PACK, S], F32, name=f"d{a}", align_bytes=64) for a in range(GROUPS)]
+        weights = keep.tile([P, PACK, S], F32, name="weights", align_bytes=64)
+        page_order = [2, 0, 1, 3]
+        pages = [keep.tile([P, T2], F32, name=f"page{t}") for t in range(PACK)]
+        wr_s_raw = keep.tile([P, PASS], U8, name="wr_s_raw", align_bytes=64)
         nc.gpsimd.memset(tab_s[:].bitcast(I32), 0)
         nc.gpsimd.memset(wr_s_raw[:].bitcast(I32), 0)
         for t, page in enumerate(pages):
@@ -100,272 +110,297 @@ def tile_list_dislocation_recurrent_backward_kernel(
         s_rows = sT.rearrange("(a p t) c -> a t p c", p=P, t=PACK)
         s_tiles = {}
 
-        def load_state(a, t):
-            s_tiles[a, t] = in_slot((a, t), [P, T], F32, f"s{a}{t}")
-            nc.sync.dma_start(out=s_tiles[a, t][:], in_=s_rows[a, t])
+        def load_state(k):
+            if k == 5:
+                s_tiles[k] = shared.tile([P, T], F32, name="s5", align_bytes=64, offset=0)
+            else:
+                s_tiles[k] = at(f"s{k}", [P, T], F32, f"s{k}")
+            nc.sync.dma_start(out=s_tiles[k][:], in_=s_rows[k // PACK, k % PACK])
 
-        def weight_rows(rows):
-            return rows.rearrange("(p i) c -> p i c", i=PACK)
+        def load_weight(tag, name, rows):
+            raw = at(tag, [P, PACK, HALF], F32, name)
+            nc.sync.dma_start(out=raw[:], in_=rows.rearrange("(p i) c -> p i c", i=PACK))
+            return raw
 
-        def load_weight(raw, rows):
-            nc.sync.dma_start(out=raw[:], in_=weight_rows(rows))
-
-        w1_rows = [w1[:, PASS * a : PASS * (a + 1)] for a in range(GROUPS)]
-        wo_rows = [wo[PASS * a : PASS * (a + 1), :] for a in range(GROUPS)]
         nc.sync.dma_start(gather_list[:], offs)
-        tiles = [(a, t) for a in range(GROUPS) for t in range(PACK)]
-        for a, t in tiles[:2]:
-            load_state(a, t)
+        load_state(0)
+        load_state(1)
+        tab_w = at("tw", [P, T], U32, "tab_w")
         nc.sync.dma_start(out=tab_w[:].bitcast(I32), in_=tab_words[0].rearrange("p t i -> p (t i)").bitcast(I32))
         for q in range(4):
             nc.sync.dma_start(
                 out=tab_s[32 * q : 32 * q + 4, :].bitcast(I32), in_=tab_scales[0, 4 * q : 4 * q + 4, :].bitcast(I32)
             )
-        w1_raw = [staging(1 + a, [P, PACK, HALF], F32, f"w1_raw{a}") for a in range(GROUPS)]
-        load_weight(w1_raw[0], w1_rows[0])
-        for a, t in tiles[2:]:
-            if (a, t) == (1, 2):
-                load_weight(w1_raw[1], w1_rows[1])
-            load_state(a, t)
-        nc.sync.dma_start(scatter_list[:], offs2)
-        wr_w_raw = in_slot((0, 0), [P, GROUPS, H], I32, "wr_w_raw")
-        nc.sync.dma_start(out=wr_w_raw[:], in_=wr_words.rearrange("a p c i -> p a (c i)").bitcast(I32))
-        for a in range(GROUPS):
+        w1_raw = [load_weight("w1a", "w1_raw0", w1[:, 0:PASS])]
+
+        def load_scale_rows(a):
             for q in range(4):
                 nc.sync.dma_start(
                     out=wr_s_raw[32 * q + 8 * a : 32 * q + 8 * a + 8, :].bitcast(I32),
                     in_=wr_scales[a, 4 * q : 4 * q + 4, :].bitcast(I32).rearrange("r (b c) -> b r c", b=GROUPS),
                 )
-        wo_raw = [staging(a, [P, PACK, HALF], F32, f"wo_raw{a}") for a in range(GROUPS)]
-        for a in range(GROUPS):
-            load_weight(wo_raw[a], wo_rows[a])
 
-        def entries(lst, j):
-            return lst[:, j * (HALF // 16) : (j + 1) * (HALF // 16)]
+        load_state(2)
+        load_state(3)
+        load_scale_rows(0)
+        load_state(4)
+        load_scale_rows(1)
+        w1_raw.append(load_weight("w1b", "w1_raw1", w1[:, PASS : 2 * PASS]))
+        for k in (5, 6, 7):
+            load_state(k)
+        wr_w_raw = at("s0", [P, GROUPS, H], I32, "wr_w_raw")
+        nc.sync.dma_start(out=wr_w_raw[:], in_=wr_words.rearrange("a p c i -> p a (c i)").bitcast(I32))
+        wo_raw = [load_weight(tag, f"wo_raw{a}", wo[PASS * a : PASS * (a + 1), :]) for a, tag in enumerate(["s1", "s2"])]
+        nc.sync.dma_start(scatter_list[:], offs2)
+        for q in range(4):
+            nc.sync.dma_start(out=weights[32 * q : 32 * q + 32], in_=wgo.rearrange("(q t) j -> q t j", t=PACK))
 
-        deriv = {}
+        def entries(lst, cols):
+            return lst[:, cols.start // 16 : cols.stop // 16]
+
         g32 = {}
         w1_q = {}
-        v_w = keep.tile([P, S], U32, name="v_w", align_bytes=64)
-        v_s = keep.tile([P, S], U8, name="v_s", align_bytes=64)
 
-        def derivative(a, t):
-            if t == 0:
-                deriv[a] = keep.tile([P, PACK, S], F32, name=f"d{a}", align_bytes=64)
-            d = deriv[a][:, t, :]
-            nc.vector.tensor_copy(d, s_tiles[a, t][:].indirect(gather_list[:]))
-            if (a, t) == tiles[-1]:
-                width = S // 4
-                tags = ["rest", "slot03", "g00_codes", "slot10"]
-                parts = [
-                    (
-                        slice(width * u, width * (u + 1)),
-                        work.tile([P, width], F32, name=f"rest_last{u}", tag=tag, bufs=3 if u == 0 else 1, align_bytes=64),
-                    )
-                    for u, tag in enumerate(tags)
-                ]
-            else:
-                parts = [(slice(0, S), work.tile([P, S], F32, name=f"rest{a}{t}", tag="rest", bufs=3, align_bytes=64))]
-            for cols, rest in parts:
-                nc.scalar.activation(out=rest[:], in_=d[:, cols], func=COPY, scale=-1.0, bias=1.0)
-                step = min(HALF, cols.stop - cols.start)
-                for c in range(cols.start, cols.stop, step):
-                    nc.gpsimd.tensor_tensor(
-                        d[:, c : c + step], d[:, c : c + step], rest[:, c - cols.start : c - cols.start + step], MULT
-                    )
+        def derivative(k, cols, rest):
+            d = deriv[k // PACK][:, k % PACK, :]
+            nc.vector.tensor_copy(d[:, cols], s_tiles[k][:].indirect(entries(gather_list, cols)))
+            nc.scalar.activation(out=rest[:], in_=d[:, cols], func=COPY, scale=-1.0, bias=1.0)
+            nc.gpsimd.tensor_tensor(d[:, cols], d[:, cols], rest[:], MULT)
 
-        def bank(k, shape, name):
-            return psum.tile(shape, F32, name=name, tag=f"bank{k}", bufs=1)
+        def whole(k):
+            derivative(k, slice(0, S), ring(k, [P, S], F32, f"rest{k}"))
 
-        gate_banks = [0, 1, 2, 3, 4, 5, 6, 7, 0, 1, 6, 7, 2, 3, 4, 5]
-        later_banks = [0, 6, 7, 1, 2, 3, 4, 5] * 3
-
-        def later_bank(shape, name):
-            return bank(later_banks.pop(0), shape, name)
-
-        def lane(t):
-            return slice(P * t, P * (t + 1))
-
-        def first_product(bank, a, t, j, stop):
+        def first_product(out, a, t, cols, start, stop):
             nc.tensor.matmul_mx(
-                out=bank[:], lhsT=w1_q[a][0][:, lane(t)].bitcast(E4M3), lhsT_scale=w1_q[a][1][:, lane(t)],
-                rhs=v_w[:, half(j)].bitcast(E5M2), rhs_scale=v_s[:, half(j)], start=True, stop=stop,
+                out=out, lhsT=w1_q[a][0][:, lane(t)].bitcast(E4M3), lhsT_scale=w1_q[a][1][:, lane(t)],
+                rhs=v_w[:, cols].bitcast(E5M2), rhs_scale=v_s[:, cols], start=start, stop=stop,
             )
 
-        def gate(a, t, j, on_gpsimd=False):
-            if t == 0:
-                g32[a, j] = in_slot(GRADIENT_SLOT[a, j], [P, PACK, HALF], F32, f"g{a}{j}")
-            h = bank(gate_banks.pop(0), [P, HALF], f"h{a}{t}{j}")
-            first_product(h, a, t, j, stop=True)
-            if on_gpsimd:
-                nc.scalar.copy(out=g32[a, j][:, t, :], in_=h[:])
-                nc.gpsimd.tensor_tensor(g32[a, j][:, t, :], g32[a, j][:, t, :], deriv[a][:, t, half(j)], MULT)
+        def gate(a, t, j, k, staged=None):
+            h = bank(k, [P, HALF], f"h{a}{t}{j}")
+            first_product(h[:], a, t, half(j), True, True)
+            if staged is not None:
+                nc.scalar.copy(out=staged[:], in_=h[:])
+                nc.gpsimd.tensor_tensor(g32[a, j][:, t, :], staged[:], deriv[a][:, t, half(j)], MULT)
             else:
                 nc.vector.tensor_tensor(g32[a, j][:, t, :], h[:], deriv[a][:, t, half(j)], MULT)
 
-        def quantize_w1(a):
-            w1_woven = weave_weight(w1_raw[a], woven(f"w1_woven{a}")[:])
-            w1_q[a] = quantize(w1_woven, HALF, f"w1_{a}", ["g10_codes", "slot12"][a])[0]
+        def gradient(a, j, tag):
+            g32[a, j] = at(tag, [P, PACK, HALF], F32, f"g{a}{j}")
 
-        for a, t in tiles[:2]:
-            derivative(a, t)
+        whole(0)
+        whole(1)
         nc.vector.tensor_copy(v_w[:], tab_w[:].indirect(gather_list[:]))
         nc.vector.tensor_copy(v_s[:], tab_s[:].indirect(gather_list[:]))
-        quantize_w1(0)
-        for t in range(2):
-            gate(0, t, 1, on_gpsimd=True)
-        for a, t in tiles[2:6]:
-            derivative(a, t)
+        w1_woven = woven([P, PACK * HALF], BF16, "w1_woven0")
+        weave_weight(nc.scalar.copy, w1_raw[0], w1_woven[:])
+        (w1_q[0],), calls = quantize(w1_woven, at("w1a_codes", [P, HALF], U32, "w1a_codes"), "w1a")
+        calls[0]()
+        gradient(0, 1, "tw")
+        gate(0, 0, 1, 0, staged=ring(1, [P, HALF], F32, "h001_staged"))
+        whole(2)
+        whole(3)
+        gate(0, 1, 1, 1, staged=ring(2, [P, HALF], F32, "h011_staged"))
+        whole(4)
+        w1_woven = woven([P, PACK * HALF], BF16, "w1_woven1")
+        weave_weight(nc.scalar.copy, w1_raw[1], w1_woven[:], parts=2)
+        gradient(0, 0, "s4")
         for t in range(PACK):
-            gate(0, t, 0)
-        derivative(1, 2)
-        quantize_w1(1)
-        derivative(1, 3)
-        g00_woven = weave(g32[0, 0], woven("g00_woven")[:], parts=2)
-        for t in range(PACK):
-            gate(1, t, 0)
-        g10_woven = weave(g32[1, 0], side(wide(0, "g10_woven"), 0))
-        for t in range(2, PACK):
-            gate(0, t, 1)
-        gate(1, 0, 1)
-        wr_w = in_slot((1, 0), [P, GROUPS * H], I32, "wr_w")
-        nc.vector.tensor_copy(
-            out=wr_w[:].rearrange("p (b t q) -> p b q t", t=PACK, q=P),
-            in_=wr_w_raw[:].rearrange("p a (b q t) -> p (a b) q t", t=PACK, q=P),
+            gate(0, t, 0, 2 + t)
+        whole(5)
+        (w1_q[1],), calls = quantize(
+            w1_woven, shared.tile([P, HALF], U32, name="w1b_codes", align_bytes=64, offset=0), "w1b"
         )
-        wr_s = in_slot((0, 0), [P, PASS], U8, "wr_s")
+        calls[0]()
+        wr_s = shared.tile([P, PASS], U8, name="wr_s", align_bytes=64, offset=4 * HALF)
         nc.vector.tensor_copy(
             out=wr_s[:].rearrange("p (t q) -> p q t", t=PACK),
             in_=wr_s_raw[:].rearrange("p (q t) -> p q t", t=PACK),
         )
-        g_q = {}
-        g_q[0, 0] = quantize(g00_woven, HALF, "g00", "g00_codes")[0]
-        g_q[1, 0] = quantize(g10_woven, HALF, "g10", "g10_codes")[0]
-        g01_woven = weave(g32[0, 1], woven("g01_woven")[:], parts=4)
-        for t in range(1, PACK):
-            gate(1, t, 1)
-        g11_woven = weave(g32[1, 1], side(wide(1, "g11_woven"), 0))
-        g_q[0, 1] = quantize(g01_woven, HALF, "g01", "g01_codes")[0]
-        b0_wo_woven = [wide(a, f"b0_wo_woven{a}") for a in range(GROUPS)]
-        for a in range(GROUPS):
-            weave_weight(wo_raw[a], side(b0_wo_woven[a], 1), parts=2)
+        for j in range(HALVES):
+            derivative(6, half(j), at(["ring0", "w1a"][j], [P, HALF], F32, f"rest6{j}"))
+        derivative(7, half(0), at("s6", [P, HALF], F32, "rest70"))
+        derivative(7, half(1), at("g00_codes", [P, HALF], F32, "rest71"))
+        g00_woven = at("w1b", [P, PACK * HALF], BF16, "g00_woven")
+        for cols in pieces(HALF, 4):
+            weave(g32[0, 0], g00_woven, cols)
 
-        wgo_rows = wgo.rearrange("(q t) j -> q (t j)", t=PACK)
-        wgo_tiles = []
-        for u in range(2):
-            rows = staging(2, [P, 2 * S], F32, "wgo0") if u == 0 else in_slot((0, 2), [P, 2 * S], F32, "wgo1")
-            nc.sync.dma_start(out=rows[:], in_=wgo_rows[:, 2 * S * u : 2 * S * (u + 1)].partition_broadcast(4))
-            wgo_tiles.append(rows)
+        wr_w = at("w1a", [P, GROUPS, GROUPS, PASS], U32, "wr_w")
+        for b in range(GROUPS):
+            for a in range(GROUPS):
+                nc.scalar.copy(
+                    out=wr_w[:, a, b, :].rearrange("p (t q) -> p q t", t=PACK),
+                    in_=wr_w_raw[:].bitcast(U32)[:, a, PASS * b : PASS * (b + 1)].rearrange("p (q t) -> p q t", t=PACK),
+                )
+
+        gradient(1, 0, "s7")
+        for t in range(PACK):
+            gate(1, t, 0, 6 + t)
+        g10_woven = at("s3", [P, PACK * HALF], BF16, "g10_woven")
+        for cols in pieces(HALF, 2):
+            weave(g32[1, 0], g10_woven, cols)
+        gradient(1, 1, "s6")
+        for t in range(2):
+            gate(1, t, 1, 2 + t)
+        (g00_q,), calls = quantize(g00_woven, at("g00_codes", [P, HALF], U32, "g00_codes"), "g00")
+        calls[0]()
+        (g10_q,), g10_calls = quantize(g10_woven, at("g10_codes", [P, HALF], U32, "g10_codes"), "g10", parts=2)
+        g10_calls[0]()
+        gate(1, 2, 1, 4)
+        gate(1, 3, 1, 5)
+        g10_calls[1]()
+        quarter = HALF // 2
+        g1_woven = [ring(u, [P, PACK * HALF], BF16, f"g1_woven{u}") for u in range(2)]
+
+        def weave_second_half(a):
+            for u, cols in enumerate(pieces(HALF, 2)):
+                nc.scalar.copy(
+                    out=by_word(g1_woven[u][:, PACK * quarter * a : PACK * quarter * (a + 1)]),
+                    in_=by_lane(g32[a, 1][:, :, cols]),
+                )
+
+        weave_second_half(1)
+
+        g1_q = []
+
+        def moving(a, j, cols):
+            if j == 0:
+                codes, scales = (g00_q, g10_q)[a]
+                return codes[:, cols], scales[:, cols]
+            codes, scales = g1_q[cols.start // quarter]
+            c0 = quarter * a + cols.start % quarter
+            return codes[:, c0 : c0 + P], scales[:, c0 : c0 + P]
 
         def recurrent_pass(out, a, b, t, j, cols, start, stop):
-            c0 = H * a + PASS * b + P * t
+            codes, scales = moving(a, j, cols)
             nc.tensor.matmul_mx(
-                out=out, lhsT=wr_w[:, c0 : c0 + P].bitcast(E4M3),
+                out=out, lhsT=wr_w[:, a, b, lane(t)].bitcast(E4M3),
                 lhsT_scale=wr_s[4 * (GROUPS * a + b) : P, lane(t)],
-                rhs=g_q[a, j][0][:, cols].bitcast(E4M3), rhs_scale=g_q[a, j][1][:, cols],
-                start=start, stop=stop,
+                rhs=codes.bitcast(E4M3), rhs_scale=scales, start=start, stop=stop,
             )
 
-        def recurrent_by_columns(b, j, dst, on_gpsimd):
-            later = []
-            for u in range(HALF // P):
-                rec = later_bank([P, PACK, P], f"rec{b}{j}c{u}")
-                for i in range(GROUPS):
-                    for t in range(PACK):
-                        recurrent_pass(
-                            rec[:, t, :], i, b, t, j, lane(u),
-                            (i, t) == (0, 0), (i, t) == (GROUPS - 1, PACK - 1),
-                        )
-                term = work.tile([P, PACK, P], F32, name=f"term{b}{j}{u}", tag="term", bufs=4, align_bytes=64)
-                c0 = HALF * j + P * u
-                nc.vector.tensor_tensor(term[:], rec[:], deriv[b][:, :, c0 : c0 + P], MULT)
-                out = by_word(dst[:, PASS * u : PASS * (u + 1)])
-                if u < on_gpsimd:
-                    nc.gpsimd.tensor_tensor(out, by_lane(term[:]), by_lane(g32[b, j][:, :, lane(u)]), ADD)
-                else:
-                    later.append((out, term, g32[b, j][:, :, lane(u)]))
-            return later
+        def by_columns(b, j, u, k, term, repeated=False):
+            rec = bank(k, [P, PACK, P], f"rec{b}{j}c{u}")
+            cols = slice(HALF * j + P * u, HALF * j + P * (u + 1))
+            if repeated:
+                for t in range(PACK):
+                    first_product(rec[:, t, :], b, t, cols, t == 0, False)
+            for i in range(GROUPS):
+                for t in range(PACK):
+                    recurrent_pass(
+                        rec[:, t, :], i, b, t, j, lane(u),
+                        (i, t) == (0, 0) and not repeated, (i, t) == (GROUPS - 1, PACK - 1),
+                    )
+            nc.vector.tensor_tensor(term, rec[:], deriv[b][:, :, cols], MULT)
 
-        def recurrent_by_lanes(b, j, dst, repeated):
-            for t in reversed(range(PACK)):
-                rec = later_bank([P, HALF], f"rec{b}{t}{j}")
-                again = t < repeated
-                if again:
-                    first_product(rec, b, t, j, stop=False)
-                for i in range(GROUPS):
-                    recurrent_pass(rec[:], i, b, t, j, half(0), i == 0 and not again, i == GROUPS - 1)
-                d = deriv[b][:, t, half(j)]
-                nc.vector.tensor_tensor(g32[b, j][:, t, :] if again else d, rec[:], d, MULT)
-            if repeated == PACK:
-                weave(g32[b, j], dst)
-                return
-            width = HALF // 2
-            for u in range(2):
-                cols = slice(width * u, width * (u + 1))
-                gradient = g32[b, j][:, repeated:PACK, cols]
-                nc.vector.tensor_tensor(gradient, gradient, deriv[b][:, repeated:PACK, half(j)][:, :, cols], ADD)
-            weave(g32[b, j], dst, parts=2)
+        b_woven = [at(f"b{j}", [P, 2 * PACK * HALF], BF16, f"b{j}_woven") for j in range(HALVES)]
 
-        b_q = {}
+        def summed_on_gpsimd(b, j, u, k, tag):
+            term = at(tag, [P, PACK, P], F32, f"term{b}{j}{u}")
+            by_columns(b, j, u, k, term[:])
+            nc.gpsimd.tensor_tensor(
+                by_word(side(b_woven[j], b)[:, PASS * u : PASS * (u + 1)]),
+                by_lane(term[:]), by_lane(g32[b, j][:, :, lane(u)]), ADD,
+            )
+
+        summed_on_gpsimd(0, 0, 0, 6, "term0")
+        gate(0, 2, 1, 5)
+        summed_on_gpsimd(0, 0, 1, 7, "term1")
+        gate(0, 3, 1, 6)
+        summed_on_gpsimd(0, 0, 2, 0, "term2")
+        weave_second_half(0)
+        for t in range(PACK):
+            rec = bank(1 + t, [P, HALF], f"rec1{t}0")
+            first_product(rec[:], 1, t, half(0), True, False)
+            for i in range(GROUPS):
+                recurrent_pass(rec[:], i, 1, t, 0, half(0), False, i == GROUPS - 1)
+            nc.vector.tensor_tensor(g32[1, 0][:, t, :], rec[:], deriv[1][:, t, half(0)], MULT)
+        for u, tag in enumerate(["term2", "g1_codes"]):
+            (codes,), calls = quantize(g1_woven[u], at(tag, [P, HALF], U32, f"g1_codes{u}"), f"g1{u}")
+            calls[0]()
+            g1_q.append(codes)
+        wo_woven = at("s3", [P, 2 * PACK * HALF], BF16, "wo_woven")
+        for a in range(GROUPS):
+            for rows in pieces(P, 4):
+                nc.scalar.copy(
+                    out=wo_woven[:].rearrange("p (t a m i) -> p a m i t", t=PACK, a=GROUPS, i=PACK)[:, a, rows],
+                    in_=wo_raw[a][:].rearrange("p i (m t) -> p m i t", t=PACK)[:, rows],
+                )
+        for cols in pieces(HALF, 2):
+            weave(g32[1, 0], side(b_woven[0], 1), cols)
+        summed_on_gpsimd(0, 0, 3, 5, "ring0")
+        summed_on_gpsimd(1, 1, 0, 0, "term0")
+        terms = [ring(1 + u, [P, PACK, quarter], F32, f"terms{u}") for u in range(2)]
+        for u in range(2):
+            by_columns(0, 1, u, 6 + u, terms[0][:, :, lane(u)])
+        summed_on_gpsimd(1, 1, 1, 1, "s4")
+        for u in range(2):
+            by_columns(0, 1, 2 + u, 2 + u, terms[1][:, :, lane(u)])
+        for u in range(2, PACK):
+            by_columns(1, 1, u, 2 + u, g32[1, 1][:, :, lane(u)], repeated=True)
+            weave(g32[1, 1], side(b_woven[1], 1), lane(u))
+        b32 = at("s4", [P, PACK, HALF], F32, "b32")
+        for u, cols in enumerate(pieces(HALF, 2)):
+            nc.vector.tensor_tensor(b32[:, :, cols], terms[u][:], g32[0, 1][:, :, cols], ADD)
+            weave(b32, side(b_woven[1], 0), cols)
+        wo_q, wo_calls = quantize(wo_woven, ring(1, [P, S], U32, "wo_codes"), "wo", parts=2)
+        b_q = []
+        for j, tag in enumerate(["tw", "ring2"]):
+            wo_calls[1 - j]()
+            codes, calls = quantize(b_woven[j], at(tag, [P, S], U32, f"b{j}_codes"), f"b{j}")
+            calls[0]()
+            b_q.append(codes)
 
         y_rows = out_0.rearrange("(p t) m -> t p m", t=PACK)
         chunks = [slice(0, 512), slice(512, 1024), slice(1024, 1280), slice(1280, 1792), slice(1792, 2048)]
         on_vector = 3
-        woven_slots = list(GRADIENT_SLOT.values()) + [(1, 0)]
+        woven_slots = ["s6", "s7", "w1b", "w1a", "s4"]
         y_woven = {}
 
         def weave_page(t, c, copy):
             cols = chunks[c]
             if c not in y_woven:
-                y_woven[c] = in_slot(woven_slots[c], [P, cols.stop - cols.start, PACK], BF16, f"y_woven{c}")
+                y_woven[c] = at(woven_slots[c], [P, cols.stop - cols.start, PACK], BF16, f"y_woven{c}")
             copy(out=y_woven[c][:, :, t], in_=pages[t][:, cols])
 
-        def output_product(t, j):
-            e = later_bank([P, HALF], f"e{t}{j}")
+        def output_product(t, j, k):
+            e = bank(k, [P, HALF], f"e{t}{j}")
             for b in range(GROUPS):
                 nc.tensor.matmul_mx(
-                    out=e[:], lhsT=wo_q[b][0][:, lane(t)].bitcast(E4M3), lhsT_scale=wo_q[b][1][:, lane(t)],
-                    rhs=b_q[b, j][0].bitcast(E4M3), rhs_scale=b_q[b, j][1],
+                    out=e[:], lhsT=wo_q[t // 2][0][:, lane(2 * (t % 2) + b)].bitcast(E4M3),
+                    lhsT_scale=wo_q[t // 2][1][:, lane(2 * (t % 2) + b)],
+                    rhs=b_q[j][b][0].bitcast(E4M3), rhs_scale=b_q[j][b][1],
                     start=(b == 0), stop=(b == GROUPS - 1),
                 )
             return e
 
-        def place(t, lst, src, cols):
-            weights = wgo_tiles[t // 2][:, S * (t % 2) : S * (t % 2 + 1)]
-            nc.vector.tensor_tensor(pages[t][:].indirect(lst), src, weights[:, cols], MULT)
+        def place(t, src, cols):
+            nc.vector.tensor_tensor(pages[t][:].indirect(entries(scatter_list, cols)), src, weights[:, t, cols], MULT)
 
-        wo_q = {}
-        recurrent_by_columns(0, 0, side(b0_wo_woven[0], 0), PACK)
-        g_q[1, 1] = quantize(g11_woven, HALF, "g11", "g11_codes")[0]
-        recurrent_by_lanes(1, 0, side(b0_wo_woven[1], 0), PACK)
-        b1_woven = wide(2, "b1_woven")
-        later = recurrent_by_columns(0, 1, side(b1_woven, 0), 2)
-        recurrent_by_lanes(1, 1, side(b1_woven, 1), 2)
-        b_q[0, 0], wo_q[0] = quantize(b0_wo_woven[0][:], S, "b0_wo0", "slot10")
-        for out, term, gradient in later:
-            nc.vector.tensor_tensor(term[:], term[:], gradient, ADD)
-            nc.scalar.copy(out=out, in_=by_lane(term[:]))
-        b_q[1, 0], wo_q[1] = quantize(b0_wo_woven[1][:], S, "b0_wo1", "g11_codes")
-        b_q[0, 1], b_q[1, 1] = quantize(b1_woven[:], S, "b1", "b1_codes")
-        page_order = [2, 0, 1, 3]
-        first_and_last = staging(0, [P, 2 * S - P], F32, "e32_first_and_last")
-        e32 = {page_order[0]: first_and_last[:, 0:S], page_order[-1]: first_and_last[:, S - P : 2 * S - P]}
-        e32[page_order[1]] = staging(1, [P, S], F32, "e32_second")[:]
-        e32[page_order[2]] = in_slot((0, 0), [P, S], F32, "e32_third")[:]
-        for j in range(HALVES):
-            for t in page_order:
-                e = output_product(t, j)
-                if (t, j) == (page_order[-1], 0):
-                    held = e
-                    nc.scalar.copy(out=e32[t][:, P:HALF], in_=e[:, P:HALF])
-                else:
-                    nc.scalar.copy(out=e32[t][:, half(j)], in_=e[:])
+        chained = at("s1", [P, 2 * S + HALF - P], F32, "e32_chained")
+        starts = {page_order[1]: 0, page_order[0]: HALF, page_order[3]: HALF + S - P}
+        e32 = {t: chained[:, c0 : c0 + S] for t, c0 in starts.items()}
+        e32[page_order[2]] = at("s0", [P, S], F32, "e32_third")[:]
+
+        def empty(i, j, k):
+            t = page_order[i]
+            nc.scalar.copy(out=e32[t][:, half(j)], in_=output_product(t, j, k)[:])
+
+        empty(0, 0, 0)
+        empty(1, 0, 6)
+        empty(2, 0, 7)
+        held = output_product(page_order[3], 0, 1)
+        nc.scalar.copy(out=e32[page_order[3]][:, P:HALF], in_=held[:, P:HALF])
+        empty(0, 1, 2)
+        empty(3, 1, 4)
+        place(page_order[0], e32[page_order[0]][:, half(0)], half(0))
+        empty(1, 1, 3)
+        empty(2, 1, 3)
         for i, t in enumerate(page_order):
             if i == 0:
-                for j in range(HALVES):
-                    place(t, entries(scatter_list, j), e32[t][:, half(j)], half(j))
+                place(t, e32[t][:, half(1)], half(1))
             else:
-                place(t, scatter_list[:], e32[t], slice(0, S))
+                place(t, e32[t], slice(0, S))
             queue = nc.sync if i == PACK - 1 else nc.scalar
             queue.dma_start(out=y_rows[t], in_=pages[t][:])
             for c in range(len(chunks)):
@@ -374,7 +409,7 @@ def tile_list_dislocation_recurrent_backward_kernel(
                 nc.scalar.copy(out=e32[page_order[-1]][:, 0:P], in_=held[:, 0:P])
 
         words_out = out_1[0].rearrange("p m t -> p (m t)").bitcast(I32)
-        y_codes = in_slot((1, 2), [P, T2], U32, "y_codes")
+        y_codes = shared.tile([P, T2], U32, name="y_codes", align_bytes=64, offset=0)
         for c, cols in enumerate(chunks):
             nc.vector.quantize_mx(
                 out=y_codes[:, cols].bitcast(E4M3), scales=y_scales[:, cols],

@@ -291,7 +291,11 @@ def tile_list_dislocation_recurrent_backward_kernel(
                         rec[:, t, :], i, b, t, j, lane(u),
                         (i, t) == (0, 0) and not repeated, (i, t) == (GROUPS - 1, PACK - 1),
                     )
-            nc.vector.tensor_tensor(term, rec[:], deriv[b][:, :, cols], MULT)
+            if repeated:
+                out = by_word(side(b_woven[j], b)[:, PASS * u : PASS * (u + 1)])
+                nc.vector.tensor_tensor(out, by_lane(rec[:]), by_lane(deriv[b][:, :, cols]), MULT)
+            else:
+                nc.vector.tensor_tensor(term, rec[:], deriv[b][:, :, cols], MULT)
 
         b_woven = [at(f"b{j}", [P, 2 * PACK * HALF], BF16, f"b{j}_woven") for j in range(HALVES)]
 
@@ -309,12 +313,8 @@ def tile_list_dislocation_recurrent_backward_kernel(
         gate(0, 3, 1, 6)
         summed_on_gpsimd(0, 0, 2, 0, "term2")
         weave_second_half(0)
-        for t in range(PACK):
-            rec = bank(1 + t, [P, HALF], f"rec1{t}0")
-            first_product(rec[:], 1, t, half(0), True, False)
-            for i in range(GROUPS):
-                recurrent_pass(rec[:], i, 1, t, 0, half(0), False, i == GROUPS - 1)
-            nc.vector.tensor_tensor(g32[1, 0][:, t, :], rec[:], deriv[1][:, t, half(0)], MULT)
+        for u in range(PACK):
+            by_columns(1, 0, u, 1 + u, None, repeated=True)
         for u, tag in enumerate(["term2", "g1_codes"]):
             (codes,), calls = quantize(g1_woven[u], at(tag, [P, HALF], U32, f"g1_codes{u}"), f"g1{u}")
             calls[0]()
@@ -326,8 +326,6 @@ def tile_list_dislocation_recurrent_backward_kernel(
                     out=wo_woven[:].rearrange("p (t a m i) -> p a m i t", t=PACK, a=GROUPS, i=PACK)[:, a, rows],
                     in_=wo_raw[a][:].rearrange("p i (m t) -> p m i t", t=PACK)[:, rows],
                 )
-        for cols in pieces(HALF, 2):
-            weave(g32[1, 0], side(b_woven[0], 1), cols)
         summed_on_gpsimd(0, 0, 3, 5, "ring0")
         summed_on_gpsimd(1, 1, 0, 0, "term0")
         terms = [ring(1 + u, [P, PACK, quarter], F32, f"terms{u}") for u in range(2)]
@@ -337,8 +335,7 @@ def tile_list_dislocation_recurrent_backward_kernel(
         for u in range(2):
             by_columns(0, 1, 2 + u, 2 + u, terms[1][:, :, lane(u)])
         for u in range(2, PACK):
-            by_columns(1, 1, u, 2 + u, g32[1, 1][:, :, lane(u)], repeated=True)
-            weave(g32[1, 1], side(b_woven[1], 1), lane(u))
+            by_columns(1, 1, u, 2 + u, None, repeated=True)
         b32 = at("s4", [P, PACK, HALF], F32, "b32")
         for u, cols in enumerate(pieces(HALF, 2)):
             nc.vector.tensor_tensor(b32[:, :, cols], terms[u][:], g32[0, 1][:, :, cols], ADD)

@@ -33,6 +33,7 @@ def tile_list_dislocation_recurrent_backward_kernel(
         keep = ctx.enter_context(tc.tile_pool(name="keep", bufs=1))
         work = ctx.enter_context(tc.tile_pool(name="work", bufs=1))
         shared = ctx.enter_context(tc.tile_pool(name="shared", bufs=1))
+        behind = ctx.enter_context(tc.tile_pool(name="behind", bufs=1))
         psum = ctx.enter_context(tc.psum_pool(name="psum", bufs=1))
 
         def at(tag, shape, dtype, name, bufs=1):
@@ -56,9 +57,10 @@ def tile_list_dislocation_recurrent_backward_kernel(
         def side(tile, u):
             return tile[:, PACK * HALF * u : PACK * HALF * (u + 1)]
 
-        def quantize(src, codes, name, parts=1):
+        def quantize(src, codes, name, parts=1, scales=None):
             width = codes.shape[1]
-            scales = keep.tile([P, width], U8, name=name + "_scales", align_bytes=64)
+            if scales is None:
+                scales = keep.tile([P, width], U8, name=name + "_scales", align_bytes=64)
             calls = []
             for u in range(parts):
                 cols = slice(width // parts * u, width // parts * (u + 1))
@@ -219,7 +221,7 @@ def tile_list_dislocation_recurrent_backward_kernel(
         )
         for j in range(HALVES):
             derivative(6, half(j), at(["ring0", "w1a"][j], [P, HALF], F32, f"rest6{j}"))
-        derivative(7, half(0), at("s6", [P, HALF], F32, "rest70"))
+        derivative(7, half(0), ring(2, [P, HALF], F32, "rest70"))
         derivative(7, half(1), at("g00_codes", [P, HALF], F32, "rest71"))
         g00_woven = at("w1b", [P, PACK * HALF], BF16, "g00_woven")
         for cols in pieces(HALF, 4):
@@ -233,21 +235,26 @@ def tile_list_dislocation_recurrent_backward_kernel(
                     in_=wr_w_raw[:].bitcast(U32)[:, a, PASS * b : PASS * (b + 1)].rearrange("p (q t) -> p q t", t=PACK),
                 )
 
-        gradient(1, 0, "s7")
-        for t in range(PACK):
-            gate(1, t, 0, 6 + t)
-        g10_woven = at("s3", [P, PACK * HALF], BF16, "g10_woven")
-        for cols in pieces(HALF, 2):
-            weave(g32[1, 0], g10_woven, cols)
-        gradient(1, 1, "s6")
-        for t in range(2):
-            gate(1, t, 1, 2 + t)
+        gradient(1, 1, "s7")
+        for t in range(PACK - 1):
+            gate(1, t, 1, 6 + t)
+        g10_woven = woven([P, PACK * HALF], BF16, "g10_woven")
+
+        def woven_gate(u):
+            h = bank(2 + u, [P, PACK, P], f"h10c{u}")
+            for t in range(PACK):
+                first_product(h[:, t, :], 1, t, lane(u), t == 0, t == PACK - 1)
+            out = by_word(g10_woven[:, PASS * u : PASS * (u + 1)])
+            nc.vector.tensor_tensor(out, by_lane(h[:]), by_lane(deriv[1][:, :, lane(u)]), MULT)
+
+        woven_gate(0)
+        woven_gate(1)
         (g00_q,), calls = quantize(g00_woven, at("g00_codes", [P, HALF], U32, "g00_codes"), "g00")
         calls[0]()
         (g10_q,), g10_calls = quantize(g10_woven, at("g10_codes", [P, HALF], U32, "g10_codes"), "g10", parts=2)
         g10_calls[0]()
-        gate(1, 2, 1, 4)
-        gate(1, 3, 1, 5)
+        woven_gate(2)
+        woven_gate(3)
         g10_calls[1]()
         quarter = HALF // 2
         g1_woven = [ring(u, [P, PACK * HALF], BF16, f"g1_woven{u}") for u in range(2)]
@@ -258,8 +265,6 @@ def tile_list_dislocation_recurrent_backward_kernel(
                     out=by_word(g1_woven[u][:, PACK * quarter * a : PACK * quarter * (a + 1)]),
                     in_=by_lane(g32[a, 1][:, :, cols]),
                 )
-
-        weave_second_half(1)
 
         g1_q = []
 
@@ -279,7 +284,7 @@ def tile_list_dislocation_recurrent_backward_kernel(
                 rhs=codes.bitcast(E4M3), rhs_scale=scales, start=start, stop=stop,
             )
 
-        def by_columns(b, j, u, k, term, repeated=False):
+        def recurrent_sum(b, j, u, k, repeated):
             rec = bank(k, [P, PACK, P], f"rec{b}{j}c{u}")
             cols = slice(HALF * j + P * u, HALF * j + P * (u + 1))
             if repeated:
@@ -291,62 +296,92 @@ def tile_list_dislocation_recurrent_backward_kernel(
                         rec[:, t, :], i, b, t, j, lane(u),
                         (i, t) == (0, 0) and not repeated, (i, t) == (GROUPS - 1, PACK - 1),
                     )
-            if repeated:
-                out = by_word(side(b_woven[j], b)[:, PASS * u : PASS * (u + 1)])
-                nc.vector.tensor_tensor(out, by_lane(rec[:]), by_lane(deriv[b][:, :, cols]), MULT)
-            else:
-                nc.vector.tensor_tensor(term, rec[:], deriv[b][:, :, cols], MULT)
+            return rec, deriv[b][:, :, cols]
 
-        b_woven = [at(f"b{j}", [P, 2 * PACK * HALF], BF16, f"b{j}_woven") for j in range(HALVES)]
+        b_woven = {}
 
-        def summed_on_gpsimd(b, j, u, k, tag):
-            term = at(tag, [P, PACK, P], F32, f"term{b}{j}{u}")
-            by_columns(b, j, u, k, term[:])
-            nc.gpsimd.tensor_tensor(
-                by_word(side(b_woven[j], b)[:, PASS * u : PASS * (u + 1)]),
-                by_lane(term[:]), by_lane(g32[b, j][:, :, lane(u)]), ADD,
-            )
+        def words_of(b, j, cols):
+            return by_word(b_woven[b, j][:, PACK * cols.start : PACK * cols.stop])
 
-        summed_on_gpsimd(0, 0, 0, 6, "term0")
-        gate(0, 2, 1, 5)
-        summed_on_gpsimd(0, 0, 1, 7, "term1")
-        gate(0, 3, 1, 6)
-        summed_on_gpsimd(0, 0, 2, 0, "term2")
+        def with_repeated_product(b, j, u, k):
+            rec, d = recurrent_sum(b, j, u, k, True)
+            nc.vector.tensor_tensor(words_of(b, j, lane(u)), by_lane(rec[:]), by_lane(d), MULT)
+
+        def term_into(term, b, j, u, k):
+            rec, d = recurrent_sum(b, j, u, k, False)
+            nc.vector.tensor_tensor(term, rec[:], d, MULT)
+
+        def summed_on_gpsimd(b, j, u, k, term):
+            term_into(term[:], b, j, u, k)
+            nc.gpsimd.tensor_tensor(words_of(b, j, lane(u)), by_lane(term[:]), by_lane(g32[b, j][:, :, lane(u)]), ADD)
+
+        def term_tile(tag, name):
+            return at(tag, [P, PACK, P], F32, name)
+
+        def placed(offset, shape, dtype, name):
+            return behind.tile(shape, dtype, name=name, align_bytes=64, offset=offset)
+
+        b0_woven = at("b0", [P, 2 * PACK * HALF], BF16, "b0_woven")
+        for b in range(GROUPS):
+            b_woven[b, 0] = side(b0_woven, b)
+        summed_on_gpsimd(0, 0, 0, 6, term_tile("term0", "term000"))
+        gate(1, 3, 1, 1)
+        weave_second_half(1)
+        summed_on_gpsimd(0, 0, 1, 7, term_tile("term1", "term001"))
+        gate(0, 2, 1, 6)
+        summed_on_gpsimd(0, 0, 2, 0, term_tile("term2", "term002"))
+        gate(0, 3, 1, 7)
         weave_second_half(0)
+        summed_on_gpsimd(0, 0, 3, 2, placed(0, [P, PACK, P], F32, "term003"))
         for u in range(PACK):
-            by_columns(1, 0, u, 1 + u, None, repeated=True)
-        for u, tag in enumerate(["term2", "g1_codes"]):
-            (codes,), calls = quantize(g1_woven[u], at(tag, [P, HALF], U32, f"g1_codes{u}"), f"g1{u}")
+            with_repeated_product(1, 0, u, [3, 4, 5, 1][u])
+        wo_woven = at("s3", [P, 2 * PACK * HALF], BF16, "wo_woven")
+        for pair in (1, 0):
+            for a in range(GROUPS):
+                lanes = slice(2 * pair, 2 * pair + 2)
+                nc.scalar.copy(
+                    out=wo_woven[:].rearrange("p (t a m i) -> p a m i t", t=PACK, a=GROUPS, i=PACK)[:, a, :, :, lanes],
+                    in_=wo_raw[a][:].rearrange("p i (m t) -> p m i t", t=PACK)[:, :, :, lanes],
+                )
+        for u in range(2):
+            (codes,), calls = quantize(
+                g1_woven[u], at(f"g1_codes{u}", [P, HALF], U32, f"g1_codes{u}"), f"g1{u}",
+                scales=placed(HALF * u, [P, HALF], U8, f"g1_scales{u}"),
+            )
             calls[0]()
             g1_q.append(codes)
-        wo_woven = at("s3", [P, 2 * PACK * HALF], BF16, "wo_woven")
-        for a in range(GROUPS):
-            for rows in pieces(P, 4):
-                nc.scalar.copy(
-                    out=wo_woven[:].rearrange("p (t a m i) -> p a m i t", t=PACK, a=GROUPS, i=PACK)[:, a, rows],
-                    in_=wo_raw[a][:].rearrange("p i (m t) -> p m i t", t=PACK)[:, rows],
-                )
-        summed_on_gpsimd(0, 0, 3, 5, "ring0")
-        summed_on_gpsimd(1, 1, 0, 0, "term0")
-        terms = [ring(1 + u, [P, PACK, quarter], F32, f"terms{u}") for u in range(2)]
-        for u in range(2):
-            by_columns(0, 1, u, 6 + u, terms[0][:, :, lane(u)])
-        summed_on_gpsimd(1, 1, 1, 1, "s4")
-        for u in range(2):
-            by_columns(0, 1, 2 + u, 2 + u, terms[1][:, :, lane(u)])
-        for u in range(2, PACK):
-            by_columns(1, 1, u, 2 + u, None, repeated=True)
-        b32 = at("s4", [P, PACK, HALF], F32, "b32")
-        for u, cols in enumerate(pieces(HALF, 2)):
-            nc.vector.tensor_tensor(b32[:, :, cols], terms[u][:], g32[0, 1][:, :, cols], ADD)
-            weave(b32, side(b_woven[1], 0), cols)
-        wo_q, wo_calls = quantize(wo_woven, ring(1, [P, S], U32, "wo_codes"), "wo", parts=2)
-        b_q = []
-        for j, tag in enumerate(["tw", "ring2"]):
-            wo_calls[1 - j]()
-            codes, calls = quantize(b_woven[j], at(tag, [P, S], U32, f"b{j}_codes"), f"b{j}")
+        b0_q, calls = quantize(b0_woven, ring(2, [P, S], U32, "b0_codes"), "b0")
+        calls[0]()
+        wo_q = {}
+
+        def quantize_wo(pair, offset):
+            (wo_q[pair],), calls = quantize(
+                side(wo_woven, pair), at(f"term{pair}", [P, HALF], U32, f"wo_codes{pair}"), f"wo{pair}",
+                scales=placed(offset, [P, HALF], U8, f"wo_scales{pair}"),
+            )
             calls[0]()
-            b_q.append(codes)
+
+        quantize_wo(1, 2 * HALF)
+        b_woven[1, 1] = at("b1", [P, PACK * HALF], BF16, "b11_woven")[:]
+        summed_on_gpsimd(1, 1, 0, 0, term_tile("term2", "term110"))
+        summed_on_gpsimd(1, 1, 1, 6, placed(4 * HALF, [P, PACK, P], F32, "term111"))
+        terms = at("s4", [P, PACK, HALF], F32, "terms")
+        for u in range(PACK):
+            term_into(terms[:, :, lane(u)], 0, 1, u, [7, 2, 3, 4][u])
+        for u in range(2, PACK):
+            with_repeated_product(1, 1, u, [5, 1][u - 2])
+        b_woven[0, 1] = placed(5 * HALF, [P, PACK * HALF], BF16, "b01_woven")[:]
+        nc.vector.tensor_tensor(words_of(0, 1, half(0)), by_lane(terms[:]), by_lane(g32[0, 1][:]), ADD)
+        b1_q = {}
+
+        def quantize_b1(b):
+            (b1_q[b],), calls = quantize(b_woven[b, 1], ring(b, [P, HALF], U32, f"b{b}1_codes"), f"b{b}1")
+            calls[0]()
+
+        quantize_b1(1)
+        quantize_wo(0, 4 * HALF)
+        quantize_b1(0)
+        b_q = [b0_q, b1_q]
 
         y_rows = out_0.rearrange("(p t) m -> t p m", t=PACK)
         chunks = [slice(0, 512), slice(512, 1024), slice(1024, 1280), slice(1280, 1792), slice(1792, 2048)]

@@ -34,6 +34,7 @@ def tile_list_dislocation_recurrent_backward_kernel(
         work = ctx.enter_context(tc.tile_pool(name="work", bufs=1))
         shared = ctx.enter_context(tc.tile_pool(name="shared", bufs=1))
         behind = ctx.enter_context(tc.tile_pool(name="behind", bufs=1))
+        results = ctx.enter_context(tc.tile_pool(name="results", bufs=1))
         psum = ctx.enter_context(tc.psum_pool(name="psum", bufs=1))
 
         def at(tag, shape, dtype, name, bufs=1):
@@ -321,7 +322,7 @@ def tile_list_dislocation_recurrent_backward_kernel(
         def placed(offset, shape, dtype, name):
             return behind.tile(shape, dtype, name=name, align_bytes=64, offset=offset)
 
-        b0_woven = at("b0", [P, 2 * PACK * HALF], BF16, "b0_woven")
+        b0_woven = at("s0", [P, 2 * PACK * HALF], BF16, "b0_woven")
         for b in range(GROUPS):
             b_woven[b, 0] = side(b0_woven, b)
         summed_on_gpsimd(0, 0, 0, 6, term_tile("term0", "term000"))
@@ -362,7 +363,7 @@ def tile_list_dislocation_recurrent_backward_kernel(
             calls[0]()
 
         quantize_wo(1, 2 * HALF)
-        b_woven[1, 1] = at("b1", [P, PACK * HALF], BF16, "b11_woven")[:]
+        b_woven[1, 1] = at("s6", [P, PACK * HALF], BF16, "b11_woven")[:]
         summed_on_gpsimd(1, 1, 0, 0, term_tile("term2", "term110"))
         summed_on_gpsimd(1, 1, 1, 6, placed(4 * HALF, [P, PACK, P], F32, "term111"))
         terms = at("s4", [P, PACK, HALF], F32, "terms")
@@ -379,21 +380,16 @@ def tile_list_dislocation_recurrent_backward_kernel(
             calls[0]()
 
         quantize_b1(1)
-        quantize_wo(0, 4 * HALF)
         quantize_b1(0)
+        quantize_wo(0, 4 * HALF)
         b_q = [b0_q, b1_q]
 
         y_rows = out_0.rearrange("(p t) m -> t p m", t=PACK)
-        chunks = [slice(0, 512), slice(512, 1024), slice(1024, 1280), slice(1280, 1792), slice(1792, 2048)]
-        on_vector = 3
-        woven_slots = ["s6", "s7", "w1b", "w1a", "s4"]
-        y_woven = {}
+        y_woven = [at(tag, [P, T2 // 2, PACK], BF16, f"y_woven{u}") for u, tag in enumerate(["s7", "w1b"])]
 
-        def weave_page(t, c, copy):
-            cols = chunks[c]
-            if c not in y_woven:
-                y_woven[c] = at(woven_slots[c], [P, cols.stop - cols.start, PACK], BF16, f"y_woven{c}")
-            copy(out=y_woven[c][:, :, t], in_=pages[t][:, cols])
+        def weave_page(t, cols, copy):
+            u, c0 = divmod(cols.start, T2 // 2)
+            copy(out=y_woven[u][:, c0 : c0 + cols.stop - cols.start, t], in_=pages[t][:, cols])
 
         def output_product(t, j, k):
             e = bank(k, [P, HALF], f"e{t}{j}")
@@ -409,47 +405,54 @@ def tile_list_dislocation_recurrent_backward_kernel(
         def place(t, src, cols):
             nc.vector.tensor_tensor(pages[t][:].indirect(entries(scatter_list, cols)), src, weights[:, t, cols], MULT)
 
-        chained = at("s1", [P, 2 * S + HALF - P], F32, "e32_chained")
-        starts = {page_order[1]: 0, page_order[0]: HALF, page_order[3]: HALF + S - P}
-        e32 = {t: chained[:, c0 : c0 + S] for t, c0 in starts.items()}
-        e32[page_order[2]] = at("s0", [P, S], F32, "e32_third")[:]
+        first, second, third, last = page_order
 
-        def empty(i, j, k):
-            t = page_order[i]
-            nc.scalar.copy(out=e32[t][:, half(j)], in_=output_product(t, j, k)[:])
+        def result_tile(offset, width, name):
+            return results.tile([P, width], F32, name=name, align_bytes=64, offset=4 * offset)
 
-        empty(0, 0, 0)
-        empty(1, 0, 6)
-        empty(2, 0, 7)
-        held = output_product(page_order[3], 0, 1)
-        nc.scalar.copy(out=e32[page_order[3]][:, P:HALF], in_=held[:, P:HALF])
-        empty(0, 1, 2)
-        empty(3, 1, 4)
-        place(page_order[0], e32[page_order[0]][:, half(0)], half(0))
-        empty(1, 1, 3)
-        empty(2, 1, 3)
-        for i, t in enumerate(page_order):
-            if i == 0:
-                place(t, e32[t][:, half(1)], half(1))
-            else:
-                place(t, e32[t], slice(0, S))
-            queue = nc.sync if i == PACK - 1 else nc.scalar
-            queue.dma_start(out=y_rows[t], in_=pages[t][:])
-            for c in range(len(chunks)):
-                weave_page(t, c, nc.vector.tensor_copy if i == PACK - 1 and c < on_vector else nc.scalar.copy)
-            if i == 0:
-                nc.scalar.copy(out=e32[page_order[-1]][:, 0:P], in_=held[:, 0:P])
+        def empty(dst, t, j, k):
+            nc.scalar.copy(out=dst, in_=output_product(t, j, k)[:])
+
+        first_half = result_tile(S - quarter, HALF, "e_first_half")
+        empty(first_half[:], first, 0, 0)
+        chained = at("s1", [P, S + HALF - P], F32, "e_chained")
+        e_last = chained[:, HALF - P : HALF - P + S]
+        held = output_product(last, 0, 6)
+        nc.scalar.copy(out=e_last[:, P:HALF], in_=held[:, P:HALF])
+        empty(chained[:, half(0)], first, 1, 7)
+        empty(e_last[:, half(1)], last, 1, 2)
+        place(first, first_half[:], half(0))
+        e32 = {first: chained[:, half(0)], last: e_last}
+        for u, t in enumerate((second, third)):
+            e32[t] = result_tile(S * u, S, f"e_page{t}")[:]
+            for j in range(HALVES):
+                empty(e32[t][:, half(j)], t, j, [3, 4, 5, 1][2 * u + j])
+        for t in page_order[:-1]:
+            place(t, e32[t], half(1) if t == first else slice(0, S))
+            nc.sync.dma_start(out=y_rows[t], in_=pages[t][:])
+            for cols in pieces(T2, 2):
+                weave_page(t, cols, nc.scalar.copy)
+            if t == first:
+                nc.scalar.copy(out=e_last[:, 0:P], in_=held[:, 0:P])
+        place(last, e_last, slice(0, S))
+        nc.sync.dma_start(out=y_rows[last], in_=pages[last][:])
+        chunks = [slice(0, 512), slice(512, 1024), slice(1024, 1536), slice(1536, 1792), slice(1792, 2048)]
+        for cols in chunks:
+            weave_page(last, cols, nc.vector.tensor_copy if cols.stop <= T2 // 2 else nc.scalar.copy)
 
         words_out = out_1[0].rearrange("p m t -> p (m t)").bitcast(I32)
         y_codes = shared.tile([P, T2], U32, name="y_codes", align_bytes=64, offset=0)
-        for c, cols in enumerate(chunks):
+        stored = 0
+        for cols in chunks:
+            u, c0 = divmod(cols.start, T2 // 2)
             nc.vector.quantize_mx(
                 out=y_codes[:, cols].bitcast(E4M3), scales=y_scales[:, cols],
-                in_=y_woven[c][:].rearrange("p m t -> p (m t)"),
+                in_=y_woven[u][:, c0 : c0 + cols.stop - cols.start, :].rearrange("p m t -> p (m t)"),
             )
-            nc.sync.dma_start(out=words_out[:, cols], in_=y_codes[:, cols].bitcast(I32))
+            if cols.stop != 1536:
+                nc.sync.dma_start(out=words_out[:, stored : cols.stop], in_=y_codes[:, stored : cols.stop].bitcast(I32))
+                stored = cols.stop
         for q in range(4):
-            queue = nc.sync if q % 2 == 0 else nc.scalar
-            queue.dma_start(
+            nc.scalar.dma_start(
                 out=out_2[0, 4 * q : 4 * q + 4, :].bitcast(I32), in_=y_scales[32 * q : 32 * q + 4, :].bitcast(I32)
             )

@@ -125,8 +125,8 @@ def tile_list_dislocation_recurrent_backward_kernel(
             nc.sync.dma_start(out=raw[:], in_=rows.rearrange("(p i) c -> p i c", i=PACK))
             return raw
 
-        nc.sync.dma_start(gather_list[:], offs)
         load_state(0)
+        nc.sync.dma_start(gather_list[:], offs)
         load_state(1)
         tab_w = at("tw", [P, T], U32, "tab_w")
         nc.sync.dma_start(out=tab_w[:].bitcast(I32), in_=tab_words[0].rearrange("p t i -> p (t i)").bitcast(I32))
@@ -371,8 +371,11 @@ def tile_list_dislocation_recurrent_backward_kernel(
             term_into(terms[:, :, lane(u)], 0, 1, u, [7, 2, 3, 4][u])
         for u in range(2, PACK):
             with_repeated_product(1, 1, u, [5, 1][u - 2])
-        b_woven[0, 1] = placed(5 * HALF, [P, PACK * HALF], BF16, "b01_woven")[:]
-        nc.vector.tensor_tensor(words_of(0, 1, half(0)), by_lane(terms[:]), by_lane(g32[0, 1][:]), ADD)
+        b_woven[0, 1] = at("s2", [P, PACK * HALF], BF16, "b01_woven")[:]
+        b32 = placed(5 * HALF, [P, PACK, HALF], F32, "b32")
+        for u in range(PACK):
+            nc.vector.tensor_tensor(b32[:, :, lane(u)], terms[:, :, lane(u)], g32[0, 1][:, :, lane(u)], ADD)
+            weave(b32, b_woven[0, 1], lane(u))
         b1_q = {}
 
         def quantize_b1(b):
@@ -380,8 +383,8 @@ def tile_list_dislocation_recurrent_backward_kernel(
             calls[0]()
 
         quantize_b1(1)
-        quantize_b1(0)
         quantize_wo(0, 4 * HALF)
+        quantize_b1(0)
         b_q = [b0_q, b1_q]
 
         y_rows = out_0.rearrange("(p t) m -> t p m", t=PACK)

@@ -35,6 +35,7 @@ def tile_list_dislocation_recurrent_backward_kernel(
         shared = ctx.enter_context(tc.tile_pool(name="shared", bufs=1))
         behind = ctx.enter_context(tc.tile_pool(name="behind", bufs=1))
         results = ctx.enter_context(tc.tile_pool(name="results", bufs=1))
+        late = ctx.enter_context(tc.tile_pool(name="late", bufs=1))
         psum = ctx.enter_context(tc.psum_pool(name="psum", bufs=1))
 
         def at(tag, shape, dtype, name, bufs=1):
@@ -102,13 +103,12 @@ def tile_list_dislocation_recurrent_backward_kernel(
         deriv = [keep.tile([P, PACK, S], F32, name=f"d{a}", align_bytes=64) for a in range(GROUPS)]
         weights = keep.tile([P, PACK, S], F32, name="weights", align_bytes=64)
         page_order = [2, 0, 1, 3]
-        pages = [keep.tile([P, T2], F32, name=f"page{t}") for t in range(PACK)]
+        pages = {t: keep.tile([P, T2], F32, name=f"page{t}") for t in page_order[:2]}
         wr_s_raw = keep.tile([P, PASS], U8, name="wr_s_raw", align_bytes=64)
         nc.gpsimd.memset(tab_s[:].bitcast(I32), 0)
         nc.gpsimd.memset(wr_s_raw[:].bitcast(I32), 0)
-        for t, page in enumerate(pages):
-            engine = nc.vector if t < 2 else nc.gpsimd
-            engine.memset(page[:], 0.0)
+        for page in pages.values():
+            nc.vector.memset(page[:], 0.0)
 
         s_rows = sT.rearrange("(a p t) c -> a t p c", p=P, t=PACK)
         s_tiles = {}
@@ -371,7 +371,7 @@ def tile_list_dislocation_recurrent_backward_kernel(
             term_into(terms[:, :, lane(u)], 0, 1, u, [7, 2, 3, 4][u])
         for u in range(2, PACK):
             with_repeated_product(1, 1, u, [5, 1][u - 2])
-        b_woven[0, 1] = at("s2", [P, PACK * HALF], BF16, "b01_woven")[:]
+        b_woven[0, 1] = late.tile([P, PACK * HALF], BF16, name="b01_woven", align_bytes=64, offset=3 * T2)[:]
         b32 = placed(5 * HALF, [P, PACK, HALF], F32, "b32")
         for u in range(PACK):
             nc.vector.tensor_tensor(b32[:, :, lane(u)], terms[:, :, lane(u)], g32[0, 1][:, :, lane(u)], ADD)
@@ -386,6 +386,9 @@ def tile_list_dislocation_recurrent_backward_kernel(
         quantize_wo(0, 4 * HALF)
         quantize_b1(0)
         b_q = [b0_q, b1_q]
+        for u, t in enumerate(page_order[2:]):
+            pages[t] = late.tile([P, T2], F32, name=f"page{t}", align_bytes=64, offset=4 * T2 * u)
+            nc.gpsimd.memset(pages[t][:], 0.0)
 
         y_rows = out_0.rearrange("(p t) m -> t p m", t=PACK)
         y_woven = [at(tag, [P, T2 // 2, PACK], BF16, f"y_woven{u}") for u, tag in enumerate(["s7", "w1b"])]

@@ -103,10 +103,10 @@ def tile_list_dislocation_recurrent_backward_kernel(
         deriv = [keep.tile([P, PACK, S], F32, name=f"d{a}", align_bytes=64) for a in range(GROUPS)]
         weights = keep.tile([P, PACK, S], F32, name="weights", align_bytes=64)
         page_order = [2, 0, 1, 3]
-        pages = {t: keep.tile([P, T2], F32, name=f"page{t}") for t in page_order[:2]}
+        pages = {t: keep.tile([P, T2], F32, name=f"page{t}") for t in page_order[:1]}
         wr_s_raw = keep.tile([P, PASS], U8, name="wr_s_raw", align_bytes=64)
-        nc.gpsimd.memset(tab_s[:].bitcast(I32), 0)
-        nc.gpsimd.memset(wr_s_raw[:].bitcast(I32), 0)
+        nc.vector.memset(tab_s[:].bitcast(I32), 0)
+        nc.vector.memset(wr_s_raw[:].bitcast(I32), 0)
         for page in pages.values():
             nc.vector.memset(page[:], 0.0)
 
@@ -379,14 +379,14 @@ def tile_list_dislocation_recurrent_backward_kernel(
         b1_q = {}
 
         def quantize_b1(b):
-            (b1_q[b],), calls = quantize(b_woven[b, 1], ring(b, [P, HALF], U32, f"b{b}1_codes"), f"b{b}1")
+            (b1_q[b],), calls = quantize(b_woven[b, 1], at(["s2", "ring1"][b], [P, HALF], U32, f"b{b}1_codes"), f"b{b}1")
             calls[0]()
 
         quantize_b1(1)
         quantize_wo(0, 4 * HALF)
         quantize_b1(0)
         b_q = [b0_q, b1_q]
-        for u, t in enumerate(page_order[2:]):
+        for u, t in enumerate(page_order[1:3]):
             pages[t] = late.tile([P, T2], F32, name=f"page{t}", align_bytes=64, offset=4 * T2 * u)
             nc.gpsimd.memset(pages[t][:], 0.0)
 
@@ -433,6 +433,8 @@ def tile_list_dislocation_recurrent_backward_kernel(
             e32[t] = result_tile(S * u, S, f"e_page{t}")[:]
             for j in range(HALVES):
                 empty(e32[t][:, half(j)], t, j, [3, 4, 5, 1][2 * u + j])
+        pages[last] = at("s2", [P, T2], F32, f"page{last}")
+        nc.gpsimd.memset(pages[last][:], 0.0)
         for t in page_order[:-1]:
             place(t, e32[t], half(1) if t == first else slice(0, S))
             nc.sync.dma_start(out=y_rows[t], in_=pages[t][:])

@@ -24,6 +24,19 @@ HALF = 512
 HALVES = S // HALF
 GROUPS = H // PASS
 
+KB = 1024
+DERIV = 0
+PAGES = DERIV + 32 * KB
+STATES = PAGES + 24 * KB
+TABLE = STATES + 64 * KB
+W1_RAW = TABLE + 8 * KB
+WR_RAW = W1_RAW + 16 * KB
+RING = WR_RAW + 8 * KB
+WOVEN = RING + 12 * KB
+W1A_CODES = WOVEN + 8 * KB
+G_CODES = W1A_CODES + 2 * KB
+TERMS = G_CODES + 8 * KB
+
 
 def tile_list_dislocation_recurrent_backward_kernel(
     tc, tab_words, tab_scales, offs, offs2, sT, w1, wr_words, wr_scales, wo, wgo, out_0, out_1, out_2
@@ -31,21 +44,20 @@ def tile_list_dislocation_recurrent_backward_kernel(
     nc = tc.nc
     with ExitStack() as ctx:
         keep = ctx.enter_context(tc.tile_pool(name="keep", bufs=1))
-        work = ctx.enter_context(tc.tile_pool(name="work", bufs=1))
-        shared = ctx.enter_context(tc.tile_pool(name="shared", bufs=1))
-        behind = ctx.enter_context(tc.tile_pool(name="behind", bufs=1))
-        results = ctx.enter_context(tc.tile_pool(name="results", bufs=1))
-        late = ctx.enter_context(tc.tile_pool(name="late", bufs=1))
+        mem = ctx.enter_context(tc.tile_pool(name="mem", bufs=1))
         psum = ctx.enter_context(tc.psum_pool(name="psum", bufs=1))
 
-        def at(tag, shape, dtype, name, bufs=1):
-            return work.tile(shape, dtype, name=name, tag=tag, bufs=bufs, align_bytes=64)
+        def at(place, shape, dtype, name):
+            return mem.tile(shape, dtype, name=name, align_bytes=64, offset=place)
 
         def ring(k, shape, dtype, name):
-            return at(f"ring{k % 3}", shape, dtype, name)
+            return at(RING + 4 * KB * (k % 3), shape, dtype, name)
 
-        def woven(shape, dtype, name):
-            return at("woven", shape, dtype, name, bufs=2)
+        def state(k):
+            return STATES + 8 * KB * k
+
+        def term_place(k):
+            return TERMS + 2 * KB * k
 
         def bank(k, shape, name):
             return psum.tile(shape, F32, name=name, tag=f"bank{k % 8}", bufs=1)
@@ -100,10 +112,10 @@ def tile_list_dislocation_recurrent_backward_kernel(
         y_scales = keep.tile([P, T2], U8, name="y_scales", align_bytes=64)
         v_w = keep.tile([P, S], U32, name="v_w", align_bytes=64)
         v_s = keep.tile([P, S], U8, name="v_s", align_bytes=64)
-        deriv = [keep.tile([P, PACK, S], F32, name=f"d{a}", align_bytes=64) for a in range(GROUPS)]
+        deriv = [at(DERIV + 16 * KB * a, [P, PACK, S], F32, f"d{a}") for a in range(GROUPS)]
         weights = keep.tile([P, PACK, S], F32, name="weights", align_bytes=64)
         page_order = [2, 0, 1, 3]
-        pages = {t: keep.tile([P, T2], F32, name=f"page{t}") for t in page_order[:1]}
+        pages = {t: at(PAGES + 8 * KB * u, [P, T2], F32, f"page{t}") for u, t in enumerate(page_order[:-1])}
         wr_s_raw = keep.tile([P, PASS], U8, name="wr_s_raw", align_bytes=64)
         nc.vector.memset(tab_s[:].bitcast(I32), 0)
         nc.vector.memset(wr_s_raw[:].bitcast(I32), 0)
@@ -114,10 +126,7 @@ def tile_list_dislocation_recurrent_backward_kernel(
         s_tiles = {}
 
         def load_state(k):
-            if k == 5:
-                s_tiles[k] = shared.tile([P, T], F32, name="s5", align_bytes=64, offset=0)
-            else:
-                s_tiles[k] = at(f"s{k}", [P, T], F32, f"s{k}")
+            s_tiles[k] = at(state(k), [P, T], F32, f"s{k}")
             nc.sync.dma_start(out=s_tiles[k][:], in_=s_rows[k // PACK, k % PACK])
 
         def load_weight(tag, name, rows):
@@ -128,13 +137,13 @@ def tile_list_dislocation_recurrent_backward_kernel(
         load_state(0)
         nc.sync.dma_start(gather_list[:], offs)
         load_state(1)
-        tab_w = at("tw", [P, T], U32, "tab_w")
+        tab_w = at(TABLE, [P, T], U32, "tab_w")
         nc.sync.dma_start(out=tab_w[:].bitcast(I32), in_=tab_words[0].rearrange("p t i -> p (t i)").bitcast(I32))
         for q in range(4):
             nc.sync.dma_start(
                 out=tab_s[32 * q : 32 * q + 4, :].bitcast(I32), in_=tab_scales[0, 4 * q : 4 * q + 4, :].bitcast(I32)
             )
-        w1_raw = [load_weight("w1a", "w1_raw0", w1[:, 0:PASS])]
+        w1_raw = [load_weight(W1_RAW, "w1_raw0", w1[:, 0:PASS])]
 
         def load_scale_rows(a):
             for q in range(4):
@@ -148,12 +157,12 @@ def tile_list_dislocation_recurrent_backward_kernel(
         load_scale_rows(0)
         load_state(4)
         load_scale_rows(1)
-        w1_raw.append(load_weight("w1b", "w1_raw1", w1[:, PASS : 2 * PASS]))
+        w1_raw.append(load_weight(W1_RAW + 8 * KB, "w1_raw1", w1[:, PASS : 2 * PASS]))
         for k in (5, 6, 7):
             load_state(k)
-        wr_w_raw = at("s0", [P, GROUPS, H], I32, "wr_w_raw")
+        wr_w_raw = at(WR_RAW, [P, GROUPS, H], I32, "wr_w_raw")
         nc.sync.dma_start(out=wr_w_raw[:], in_=wr_words.rearrange("a p c i -> p a (c i)").bitcast(I32))
-        wo_raw = [load_weight(tag, f"wo_raw{a}", wo[PASS * a : PASS * (a + 1), :]) for a, tag in enumerate(["s1", "s2"])]
+        wo_raw = [load_weight(tag, f"wo_raw{a}", wo[PASS * a : PASS * (a + 1), :]) for a, tag in enumerate([state(1), state(2)])]
         nc.sync.dma_start(scatter_list[:], offs2)
         for q in range(4):
             nc.sync.dma_start(out=weights[32 * q : 32 * q + 32], in_=wgo.rearrange("(q t) j -> q t j", t=PACK))
@@ -192,43 +201,45 @@ def tile_list_dislocation_recurrent_backward_kernel(
             g32[a, j] = at(tag, [P, PACK, HALF], F32, f"g{a}{j}")
 
         whole(0)
+        pages[page_order[-1]] = at(state(0), [P, T2], F32, "page_last")
+        nc.gpsimd.memset(pages[page_order[-1]][:], 0.0)
         whole(1)
         nc.vector.tensor_copy(v_w[:], tab_w[:].indirect(gather_list[:]))
         nc.vector.tensor_copy(v_s[:], tab_s[:].indirect(gather_list[:]))
-        w1_woven = woven([P, PACK * HALF], BF16, "w1_woven0")
+        w1_woven = at(WOVEN, [P, PACK * HALF], BF16, "w1_woven0")
         weave_weight(nc.scalar.copy, w1_raw[0], w1_woven[:])
-        (w1_q[0],), calls = quantize(w1_woven, at("w1a_codes", [P, HALF], U32, "w1a_codes"), "w1a")
+        (w1_q[0],), calls = quantize(w1_woven, at(W1A_CODES, [P, HALF], U32, "w1a_codes"), "w1a")
         calls[0]()
-        gradient(0, 1, "tw")
+        gradient(0, 1, TABLE)
         gate(0, 0, 1, 0, staged=ring(1, [P, HALF], F32, "h001_staged"))
         whole(2)
         whole(3)
         gate(0, 1, 1, 1, staged=ring(2, [P, HALF], F32, "h011_staged"))
         whole(4)
-        w1_woven = woven([P, PACK * HALF], BF16, "w1_woven1")
+        w1_woven = at(WOVEN + 4 * KB, [P, PACK * HALF], BF16, "w1_woven1")
         weave_weight(nc.scalar.copy, w1_raw[1], w1_woven[:], parts=2)
-        gradient(0, 0, "s4")
+        gradient(0, 0, state(4))
         for t in range(PACK):
             gate(0, t, 0, 2 + t)
         whole(5)
         (w1_q[1],), calls = quantize(
-            w1_woven, shared.tile([P, HALF], U32, name="w1b_codes", align_bytes=64, offset=0), "w1b"
+            w1_woven, at(state(5), [P, HALF], U32, "w1b_codes"), "w1b"
         )
         calls[0]()
-        wr_s = shared.tile([P, PASS], U8, name="wr_s", align_bytes=64, offset=4 * HALF)
+        wr_s = at(state(5) + 2 * KB, [P, PASS], U8, "wr_s")
         nc.vector.tensor_copy(
             out=wr_s[:].rearrange("p (t q) -> p q t", t=PACK),
             in_=wr_s_raw[:].rearrange("p (q t) -> p q t", t=PACK),
         )
         for j in range(HALVES):
-            derivative(6, half(j), at(["ring0", "w1a"][j], [P, HALF], F32, f"rest6{j}"))
+            derivative(6, half(j), at([RING, W1_RAW][j], [P, HALF], F32, f"rest6{j}"))
         derivative(7, half(0), ring(2, [P, HALF], F32, "rest70"))
-        derivative(7, half(1), at("g00_codes", [P, HALF], F32, "rest71"))
-        g00_woven = at("w1b", [P, PACK * HALF], BF16, "g00_woven")
+        derivative(7, half(1), at(G_CODES, [P, HALF], F32, "rest71"))
+        g00_woven = at(W1_RAW + 8 * KB, [P, PACK * HALF], BF16, "g00_woven")
         for cols in pieces(HALF, 4):
             weave(g32[0, 0], g00_woven, cols)
 
-        wr_w = at("w1a", [P, GROUPS, GROUPS, PASS], U32, "wr_w")
+        wr_w = at(W1_RAW, [P, GROUPS, GROUPS, PASS], U32, "wr_w")
         for b in range(GROUPS):
             for a in range(GROUPS):
                 nc.scalar.copy(
@@ -236,10 +247,10 @@ def tile_list_dislocation_recurrent_backward_kernel(
                     in_=wr_w_raw[:].bitcast(U32)[:, a, PASS * b : PASS * (b + 1)].rearrange("p (q t) -> p q t", t=PACK),
                 )
 
-        gradient(1, 1, "s7")
+        gradient(1, 1, state(7))
         for t in range(PACK - 1):
             gate(1, t, 1, 6 + t)
-        g10_woven = woven([P, PACK * HALF], BF16, "g10_woven")
+        g10_woven = at(WOVEN, [P, PACK * HALF], BF16, "g10_woven")
 
         def woven_gate(u):
             h = bank(2 + u, [P, PACK, P], f"h10c{u}")
@@ -250,9 +261,9 @@ def tile_list_dislocation_recurrent_backward_kernel(
 
         woven_gate(0)
         woven_gate(1)
-        (g00_q,), calls = quantize(g00_woven, at("g00_codes", [P, HALF], U32, "g00_codes"), "g00")
+        (g00_q,), calls = quantize(g00_woven, at(G_CODES, [P, HALF], U32, "g00_codes"), "g00")
         calls[0]()
-        (g10_q,), g10_calls = quantize(g10_woven, at("g10_codes", [P, HALF], U32, "g10_codes"), "g10", parts=2)
+        (g10_q,), g10_calls = quantize(g10_woven, at(G_CODES + 2 * KB, [P, HALF], U32, "g10_codes"), "g10", parts=2)
         g10_calls[0]()
         woven_gate(2)
         woven_gate(3)
@@ -316,27 +327,24 @@ def tile_list_dislocation_recurrent_backward_kernel(
             term_into(term[:], b, j, u, k)
             nc.gpsimd.tensor_tensor(words_of(b, j, lane(u)), by_lane(term[:]), by_lane(g32[b, j][:, :, lane(u)]), ADD)
 
-        def term_tile(tag, name):
-            return at(tag, [P, PACK, P], F32, name)
+        def term_tile(place, name):
+            return at(place, [P, PACK, P], F32, name)
 
-        def placed(offset, shape, dtype, name):
-            return behind.tile(shape, dtype, name=name, align_bytes=64, offset=offset)
-
-        b0_woven = at("s0", [P, 2 * PACK * HALF], BF16, "b0_woven")
+        b0_woven = at(WR_RAW, [P, 2 * PACK * HALF], BF16, "b0_woven")
         for b in range(GROUPS):
             b_woven[b, 0] = side(b0_woven, b)
-        summed_on_gpsimd(0, 0, 0, 6, term_tile("term0", "term000"))
+        summed_on_gpsimd(0, 0, 0, 6, term_tile(term_place(0), "term000"))
         gate(1, 3, 1, 1)
         weave_second_half(1)
-        summed_on_gpsimd(0, 0, 1, 7, term_tile("term1", "term001"))
+        summed_on_gpsimd(0, 0, 1, 7, term_tile(term_place(1), "term001"))
         gate(0, 2, 1, 6)
-        summed_on_gpsimd(0, 0, 2, 0, term_tile("term2", "term002"))
+        summed_on_gpsimd(0, 0, 2, 0, term_tile(term_place(2), "term002"))
         gate(0, 3, 1, 7)
         weave_second_half(0)
-        summed_on_gpsimd(0, 0, 3, 2, placed(0, [P, PACK, P], F32, "term003"))
+        summed_on_gpsimd(0, 0, 3, 2, term_tile(term_place(3), "term003"))
         for u in range(PACK):
             with_repeated_product(1, 0, u, [3, 4, 5, 1][u])
-        wo_woven = at("s3", [P, 2 * PACK * HALF], BF16, "wo_woven")
+        wo_woven = at(state(3), [P, 2 * PACK * HALF], BF16, "wo_woven")
         for pair in (1, 0):
             for a in range(GROUPS):
                 lanes = slice(2 * pair, 2 * pair + 2)
@@ -346,56 +354,20 @@ def tile_list_dislocation_recurrent_backward_kernel(
                 )
         for u in range(2):
             (codes,), calls = quantize(
-                g1_woven[u], at(f"g1_codes{u}", [P, HALF], U32, f"g1_codes{u}"), f"g1{u}",
-                scales=placed(HALF * u, [P, HALF], U8, f"g1_scales{u}"),
+                g1_woven[u], at(G_CODES + 4 * KB + 2 * KB * u, [P, HALF], U32, f"g1_codes{u}"), f"g1{u}",
+                scales=at(term_place(3) + HALF * u, [P, HALF], U8, f"g1_scales{u}"),
             )
             calls[0]()
             g1_q.append(codes)
         b0_q, calls = quantize(b0_woven, ring(2, [P, S], U32, "b0_codes"), "b0")
         calls[0]()
-        wo_q = {}
+        wo_q, calls = quantize(
+            wo_woven, at(term_place(0), [P, S], U32, "wo_codes"), "wo",
+            scales=at(term_place(3) + KB, [P, S], U8, "wo_scales"),
+        )
+        calls[0]()
 
-        def quantize_wo(pair, offset):
-            (wo_q[pair],), calls = quantize(
-                side(wo_woven, pair), at(f"term{pair}", [P, HALF], U32, f"wo_codes{pair}"), f"wo{pair}",
-                scales=placed(offset, [P, HALF], U8, f"wo_scales{pair}"),
-            )
-            calls[0]()
-
-        quantize_wo(1, 2 * HALF)
-        b_woven[1, 1] = at("s6", [P, PACK * HALF], BF16, "b11_woven")[:]
-        summed_on_gpsimd(1, 1, 0, 0, term_tile("term2", "term110"))
-        summed_on_gpsimd(1, 1, 1, 6, placed(4 * HALF, [P, PACK, P], F32, "term111"))
-        terms = at("s4", [P, PACK, HALF], F32, "terms")
-        for u in range(PACK):
-            term_into(terms[:, :, lane(u)], 0, 1, u, [7, 2, 3, 4][u])
-        for u in range(2, PACK):
-            with_repeated_product(1, 1, u, [5, 1][u - 2])
-        b_woven[0, 1] = late.tile([P, PACK * HALF], BF16, name="b01_woven", align_bytes=64, offset=3 * T2)[:]
-        b32 = placed(5 * HALF, [P, PACK, HALF], F32, "b32")
-        for u in range(PACK):
-            nc.vector.tensor_tensor(b32[:, :, lane(u)], terms[:, :, lane(u)], g32[0, 1][:, :, lane(u)], ADD)
-            weave(b32, b_woven[0, 1], lane(u))
-        b1_q = {}
-
-        def quantize_b1(b):
-            (b1_q[b],), calls = quantize(b_woven[b, 1], at(["s2", "ring1"][b], [P, HALF], U32, f"b{b}1_codes"), f"b{b}1")
-            calls[0]()
-
-        quantize_b1(1)
-        quantize_wo(0, 4 * HALF)
-        quantize_b1(0)
-        b_q = [b0_q, b1_q]
-        for u, t in enumerate(page_order[1:3]):
-            pages[t] = late.tile([P, T2], F32, name=f"page{t}", align_bytes=64, offset=4 * T2 * u)
-            nc.gpsimd.memset(pages[t][:], 0.0)
-
-        y_rows = out_0.rearrange("(p t) m -> t p m", t=PACK)
-        y_woven = [at(tag, [P, T2 // 2, PACK], BF16, f"y_woven{u}") for u, tag in enumerate(["s7", "w1b"])]
-
-        def weave_page(t, cols, copy):
-            u, c0 = divmod(cols.start, T2 // 2)
-            copy(out=y_woven[u][:, c0 : c0 + cols.stop - cols.start, t], in_=pages[t][:, cols])
+        b_q = [b0_q]
 
         def output_product(t, j, k):
             e = bank(k, [P, HALF], f"e{t}{j}")
@@ -408,55 +380,119 @@ def tile_list_dislocation_recurrent_backward_kernel(
                 )
             return e
 
-        def place(t, src, cols):
-            nc.vector.tensor_tensor(pages[t][:].indirect(entries(scatter_list, cols)), src, weights[:, t, cols], MULT)
-
-        first, second, third, last = page_order
-
-        def result_tile(offset, width, name):
-            return results.tile([P, width], F32, name=name, align_bytes=64, offset=4 * offset)
-
         def empty(dst, t, j, k):
             nc.scalar.copy(out=dst, in_=output_product(t, j, k)[:])
 
-        first_half = result_tile(S - quarter, HALF, "e_first_half")
-        empty(first_half[:], first, 0, 0)
-        chained = at("s1", [P, S + HALF - P], F32, "e_chained")
-        e_last = chained[:, HALF - P : HALF - P + S]
-        held = output_product(last, 0, 6)
-        nc.scalar.copy(out=e_last[:, P:HALF], in_=held[:, P:HALF])
-        empty(chained[:, half(0)], first, 1, 7)
-        empty(e_last[:, half(1)], last, 1, 2)
-        place(first, first_half[:], half(0))
-        e32 = {first: chained[:, half(0)], last: e_last}
+        summed = [[(0, 0)], [(0, 1)], [(1, 0), (1, 1)], [(0, 2)], [(0, 3)]]
+        term_places = [state(3), state(3) + 2 * KB, state(4), state(4) + 4 * KB, state(4) + 6 * KB]
+        terms = [
+            at(place, [P, PACK, P * len(run)], F32, f"terms{n}") for n, (place, run) in enumerate(zip(term_places, summed))
+        ]
+        staged_places = [state(1), state(1) + 2 * KB, state(1) + 6 * KB, state(1) + 6 * KB]
+        staged = [at(place, [P, HALF], F32, f"e_first{u}") for u, place in enumerate(staged_places)]
+        weighted_places = [state(1) + 10 * KB, term_places[1], term_places[2]]
+        weighted = [at(place, [P, HALF], F32, f"y_first{u}") for u, place in enumerate(weighted_places)]
+        sum_places = [state(1) + 12 * KB] + staged_places[:2] + [staged_places[2] - KB, staged_places[2] + KB]
+        b1_woven = at(state(6), [P, 2 * PACK * HALF], BF16, "b1_woven")
+        for b in range(GROUPS):
+            b_woven[b, 1] = side(b1_woven, b)
+
+        def add_gradient(n):
+            (b, u), count = summed[n][0], len(summed[n])
+            total = at(sum_places[n], [P, PACK, P * count], F32, f"b32_{n}")
+            nc.gpsimd.tensor_tensor(total[:], terms[n][:], g32[b, 1][:, :, P * u : P * (u + count)], ADD)
+            for i in range(count):
+                nc.scalar.copy(out=words_of(b, 1, lane(u + i)), in_=by_lane(total[:, :, lane(i)]))
+
+        def weigh(u):
+            nc.gpsimd.tensor_tensor(weighted[u][:], staged[u][:], weights[:, page_order[u], half(0)], MULT)
+
+        def place_first(u):
+            nc.vector.tensor_copy(pages[page_order[u]][:].indirect(entries(scatter_list, half(0))), weighted[u][:])
+
+        term_banks = [[0], [6], [7, 2], [3], [4]]
+        empty(staged[0][:], page_order[0], 0, 1)
+        for n, run in enumerate(summed):
+            for i, (b, u) in enumerate(run):
+                term_into(terms[n][:, :, lane(i)], b, 1, u, term_banks[n][i])
+        for u in range(2, PACK):
+            with_repeated_product(1, 1, u, [5, 1][u - 2])
+        for u in range(1, PACK - 1):
+            empty(staged[u][:], page_order[u], 0, [4, 5][u - 1])
+        add_gradient(0)
+        weigh(0)
+        place_first(0)
+        add_gradient(1)
+        weigh(1)
+        place_first(1)
+        add_gradient(2)
+        weigh(2)
+        place_first(2)
+        add_gradient(3)
+        add_gradient(4)
+        empty(staged[3][:], page_order[3], 0, 1)
+        b1_q, calls = quantize(b1_woven, ring(1, [P, S], U32, "b1_codes"), "b1")
+        calls[0]()
+        b_q.append(b1_q)
+
+        def place_weighing(t, src, j):
+            nc.vector.tensor_tensor(pages[t][:].indirect(entries(scatter_list, half(j))), src, weights[:, t, half(j)], MULT)
+
+        place_weighing(page_order[3], staged[3][:], 0)
+
+        first, second, third, last = page_order
+        y_rows = out_0.rearrange("(p t) m -> t p m", t=PACK)
+        pairs = [at(DERIV + 8 * KB * u, [P, 2, T2], BF16, f"y_pairs{u}") for u in range(2)]
+
+        def pair_page(t, cols, copy):
+            u, c0 = divmod(cols.start, T2 // 2)
+            dst = pairs[u][:, t // 2, :].rearrange("p (m l) -> p m l", l=2)
+            copy(out=dst[:, c0 : c0 + cols.stop - cols.start, t % 2], in_=pages[t][:, cols])
+
+        chained = at(state(7), [P, 2 * HALF - P], F32, "e_chained")
+        e32 = {first: chained[:, 0:HALF], last: chained[:, HALF - P : 2 * HALF - P]}
+        empty(e32[first], first, 1, 0)
         for u, t in enumerate((second, third)):
-            e32[t] = result_tile(S * u, S, f"e_page{t}")[:]
-            for j in range(HALVES):
-                empty(e32[t][:, half(j)], t, j, [3, 4, 5, 1][2 * u + j])
-        pages[last] = at("s2", [P, T2], F32, f"page{last}")
-        nc.gpsimd.memset(pages[last][:], 0.0)
-        for t in page_order[:-1]:
-            place(t, e32[t], half(1) if t == first else slice(0, S))
+            e32[t] = at(state(7) + 4 * KB + 2 * KB * u, [P, HALF], F32, f"e_second{t}")[:]
+            empty(e32[t], t, 1, [6, 7][u])
+        held = output_product(last, 1, 2)
+        nc.scalar.copy(out=e32[last][:, P:HALF], in_=held[:, P:HALF])
+        for t in page_order:
+            place_weighing(t, e32[t], 1)
             nc.sync.dma_start(out=y_rows[t], in_=pages[t][:])
-            for cols in pieces(T2, 2):
-                weave_page(t, cols, nc.scalar.copy)
+            if t != last:
+                for cols in pieces(T2, 2):
+                    pair_page(t, cols, nc.scalar.copy)
             if t == first:
-                nc.scalar.copy(out=e_last[:, 0:P], in_=held[:, 0:P])
-        place(last, e_last, slice(0, S))
-        nc.sync.dma_start(out=y_rows[last], in_=pages[last][:])
+                nc.scalar.copy(out=e32[last][:, 0:P], in_=held[:, 0:P])
+
         chunks = [slice(0, 512), slice(512, 1024), slice(1024, 1536), slice(1536, 1792), slice(1792, 2048)]
-        for cols in chunks:
-            weave_page(last, cols, nc.vector.tensor_copy if cols.stop <= T2 // 2 else nc.scalar.copy)
+        y_woven = [
+            at(DERIV + 16 * KB + 8 * cols.start, [P, PACK * (cols.stop - cols.start)], BF16, f"y_woven{n}")
+            for n, cols in enumerate(chunks)
+        ]
+
+        def join_pairs(n, copy, word):
+            u, c0 = divmod(chunks[n].start, T2 // 2)
+            src = pairs[u][:].bitcast(word)[:, :, c0 : c0 + chunks[n].stop - chunks[n].start]
+            copy(
+                out=y_woven[n][:].bitcast(word).rearrange("p (c i u) -> p c u i", u=2, i=4),
+                in_=src.rearrange("p u (c i) -> p c u i", i=4),
+            )
+
+        for n in range(2):
+            pair_page(last, chunks[n], nc.vector.tensor_copy)
+        for n in range(2):
+            join_pairs(n, nc.vector.tensor_copy, I32)
+        for n in range(2, len(chunks)):
+            pair_page(last, chunks[n], nc.scalar.copy)
+            join_pairs(n, nc.scalar.copy, U32)
 
         words_out = out_1[0].rearrange("p m t -> p (m t)").bitcast(I32)
-        y_codes = shared.tile([P, T2], U32, name="y_codes", align_bytes=64, offset=0)
+        y_codes = at(state(5), [P, T2], U32, "y_codes")
         stored = 0
-        for cols in chunks:
-            u, c0 = divmod(cols.start, T2 // 2)
-            nc.vector.quantize_mx(
-                out=y_codes[:, cols].bitcast(E4M3), scales=y_scales[:, cols],
-                in_=y_woven[u][:, c0 : c0 + cols.stop - cols.start, :].rearrange("p m t -> p (m t)"),
-            )
+        for n, cols in enumerate(chunks):
+            nc.vector.quantize_mx(out=y_codes[:, cols].bitcast(E4M3), scales=y_scales[:, cols], in_=y_woven[n][:])
             if cols.stop != 1536:
                 nc.sync.dma_start(out=words_out[:, stored : cols.stop], in_=y_codes[:, stored : cols.stop].bitcast(I32))
                 stored = cols.stop

@@ -27,14 +27,13 @@ GROUPS = H // PASS
 KB = 1024
 DERIV = 0
 PAGES = DERIV + 32 * KB
-STATES = PAGES + 24 * KB
+STATES = PAGES + 32 * KB
 TABLE = STATES + 64 * KB
 W1_RAW = TABLE + 8 * KB
 WR_RAW = W1_RAW + 16 * KB
 RING = WR_RAW + 8 * KB
-WOVEN = RING + 12 * KB
-W1A_CODES = WOVEN + 8 * KB
-G_CODES = W1A_CODES + 2 * KB
+WOVEN = RING + 13 * KB
+G_CODES = WOVEN + 14 * KB
 TERMS = G_CODES + 8 * KB
 
 
@@ -110,12 +109,12 @@ def tile_list_dislocation_recurrent_backward_kernel(
         scatter_list = keep.tile([P, S // 16], U16, name="scatter_list")
         tab_s = keep.tile([P, T], U8, name="tab_s", align_bytes=64)
         y_scales = keep.tile([P, T2], U8, name="y_scales", align_bytes=64)
-        v_w = keep.tile([P, S], U32, name="v_w", align_bytes=64)
+        v_w = [keep.tile([P, HALF], U32, name="v_w0", align_bytes=64)]
         v_s = keep.tile([P, S], U8, name="v_s", align_bytes=64)
         deriv = [at(DERIV + 16 * KB * a, [P, PACK, S], F32, f"d{a}") for a in range(GROUPS)]
         weights = keep.tile([P, PACK, S], F32, name="weights", align_bytes=64)
         page_order = [2, 0, 1, 3]
-        pages = {t: at(PAGES + 8 * KB * u, [P, T2], F32, f"page{t}") for u, t in enumerate(page_order[:-1])}
+        pages = {t: at(PAGES + 8 * KB * u, [P, T2], F32, f"page{t}") for u, t in enumerate(page_order)}
         wr_s_raw = keep.tile([P, PASS], U8, name="wr_s_raw", align_bytes=64)
         nc.vector.memset(tab_s[:].bitcast(I32), 0)
         nc.vector.memset(wr_s_raw[:].bitcast(I32), 0)
@@ -134,17 +133,6 @@ def tile_list_dislocation_recurrent_backward_kernel(
             nc.sync.dma_start(out=raw[:], in_=rows.rearrange("(p i) c -> p i c", i=PACK))
             return raw
 
-        load_state(0)
-        nc.sync.dma_start(gather_list[:], offs)
-        load_state(1)
-        tab_w = at(TABLE, [P, T], U32, "tab_w")
-        nc.sync.dma_start(out=tab_w[:].bitcast(I32), in_=tab_words[0].rearrange("p t i -> p (t i)").bitcast(I32))
-        for q in range(4):
-            nc.sync.dma_start(
-                out=tab_s[32 * q : 32 * q + 4, :].bitcast(I32), in_=tab_scales[0, 4 * q : 4 * q + 4, :].bitcast(I32)
-            )
-        w1_raw = [load_weight(W1_RAW, "w1_raw0", w1[:, 0:PASS])]
-
         def load_scale_rows(a):
             for q in range(4):
                 nc.sync.dma_start(
@@ -152,14 +140,28 @@ def tile_list_dislocation_recurrent_backward_kernel(
                     in_=wr_scales[a, 4 * q : 4 * q + 4, :].bitcast(I32).rearrange("r (b c) -> b r c", b=GROUPS),
                 )
 
-        load_state(2)
-        load_state(3)
-        load_scale_rows(0)
-        load_state(4)
-        load_scale_rows(1)
-        w1_raw.append(load_weight(W1_RAW + 8 * KB, "w1_raw1", w1[:, PASS : 2 * PASS]))
-        for k in (5, 6, 7):
+        def load_w1_part(u):
+            raw = at(W1_RAW + 4 * KB * u, [P, PACK, HALF // 2], F32, f"w1_part{u}")
+            cols = slice(HALF // 2 * u, HALF // 2 * (u + 1))
+            nc.sync.dma_start(out=raw[:], in_=w1[:, cols].rearrange("(p i) c -> p i c", i=PACK))
+            return raw
+
+        load_state(0)
+        nc.sync.dma_start(gather_list[:], offs)
+        for k in range(1, 7):
             load_state(k)
+        tab_w = at(TABLE, [P, T], U32, "tab_w")
+        nc.sync.dma_start(out=tab_w[:].bitcast(I32), in_=tab_words[0].rearrange("p t i -> p (t i)").bitcast(I32))
+        for q in range(4):
+            nc.sync.dma_start(
+                out=tab_s[32 * q : 32 * q + 4, :].bitcast(I32), in_=tab_scales[0, 4 * q : 4 * q + 4, :].bitcast(I32)
+            )
+        w1_parts = [load_w1_part(0)]
+        load_state(7)
+        load_scale_rows(0)
+        w1_parts.append(load_w1_part(1))
+        w1b_raw = load_weight(W1_RAW + 8 * KB, "w1b_raw", w1[:, PASS : 2 * PASS])
+        load_scale_rows(1)
         wr_w_raw = at(WR_RAW, [P, GROUPS, H], I32, "wr_w_raw")
         nc.sync.dma_start(out=wr_w_raw[:], in_=wr_words.rearrange("a p c i -> p a (c i)").bitcast(I32))
         wo_raw = [load_weight(tag, f"wo_raw{a}", wo[PASS * a : PASS * (a + 1), :]) for a, tag in enumerate([state(1), state(2)])]
@@ -173,19 +175,18 @@ def tile_list_dislocation_recurrent_backward_kernel(
         g32 = {}
         w1_q = {}
 
-        def derivative(k, cols, rest):
-            d = deriv[k // PACK][:, k % PACK, :]
-            nc.vector.tensor_copy(d[:, cols], s_tiles[k][:].indirect(entries(gather_list, cols)))
-            nc.scalar.activation(out=rest[:], in_=d[:, cols], func=COPY, scale=-1.0, bias=1.0)
-            nc.gpsimd.tensor_tensor(d[:, cols], d[:, cols], rest[:], MULT)
+        def gather_state(k):
+            nc.vector.tensor_copy(deriv[k // PACK][:, k % PACK, :], s_tiles[k][:].indirect(gather_list[:]))
 
-        def whole(k):
-            derivative(k, slice(0, S), ring(k, [P, S], F32, f"rest{k}"))
+        def derivative(k, cols, rest):
+            d = deriv[k // PACK][:, k % PACK, cols]
+            nc.scalar.activation(out=rest[:], in_=d, func=COPY, scale=-1.0, bias=1.0)
+            nc.gpsimd.tensor_tensor(d, d, rest[:], MULT)
 
         def first_product(out, a, t, cols, start, stop):
             nc.tensor.matmul_mx(
                 out=out, lhsT=w1_q[a][0][:, lane(t)].bitcast(E4M3), lhsT_scale=w1_q[a][1][:, lane(t)],
-                rhs=v_w[:, cols].bitcast(E5M2), rhs_scale=v_s[:, cols], start=start, stop=stop,
+                rhs=v_w[cols.start // HALF][:, cols.start % HALF : cols.start % HALF + cols.stop - cols.start].bitcast(E5M2), rhs_scale=v_s[:, cols], start=start, stop=stop,
             )
 
         def gate(a, t, j, k, staged=None):
@@ -200,42 +201,42 @@ def tile_list_dislocation_recurrent_backward_kernel(
         def gradient(a, j, tag):
             g32[a, j] = at(tag, [P, PACK, HALF], F32, f"g{a}{j}")
 
-        whole(0)
-        pages[page_order[-1]] = at(state(0), [P, T2], F32, "page_last")
-        nc.gpsimd.memset(pages[page_order[-1]][:], 0.0)
-        whole(1)
-        nc.vector.tensor_copy(v_w[:], tab_w[:].indirect(gather_list[:]))
+        for k in range(7):
+            gather_state(k)
+            derivative(k, slice(0, S), ring(k, [P, S], F32, f"rest{k}"))
+        nc.vector.tensor_copy(v_w[0][:], tab_w[:].indirect(entries(gather_list, half(0))))
         nc.vector.tensor_copy(v_s[:], tab_s[:].indirect(gather_list[:]))
+        gather_state(7)
         w1_woven = at(WOVEN, [P, PACK * HALF], BF16, "w1_woven0")
-        weave_weight(nc.scalar.copy, w1_raw[0], w1_woven[:])
-        (w1_q[0],), calls = quantize(w1_woven, at(W1A_CODES, [P, HALF], U32, "w1a_codes"), "w1a")
+        for u, raw in enumerate(w1_parts):
+            nc.scalar.copy(
+                out=w1_woven[:].rearrange("p (t m i) -> p m i t", t=PACK, i=PACK)[:, P // 2 * u : P // 2 * (u + 1)],
+                in_=raw[:].rearrange("p i (m t) -> p m i t", t=PACK),
+            )
+        (w1_q[0],), calls = quantize(w1_woven, ring(6, [P, HALF], U32, "w1a_codes"), "w1a")
         calls[0]()
-        gradient(0, 1, TABLE)
-        gate(0, 0, 1, 0, staged=ring(1, [P, HALF], F32, "h001_staged"))
-        whole(2)
-        whole(3)
-        gate(0, 1, 1, 1, staged=ring(2, [P, HALF], F32, "h011_staged"))
-        whole(4)
-        w1_woven = at(WOVEN + 4 * KB, [P, PACK * HALF], BF16, "w1_woven1")
-        weave_weight(nc.scalar.copy, w1_raw[1], w1_woven[:], parts=2)
+        v_w.append(at(WOVEN - KB, [P, HALF], U32, "v_w1"))
+        nc.vector.tensor_copy(v_w[1][:], tab_w[:].indirect(entries(gather_list, half(1))))
+        derivative(7, half(0), at(WOVEN + KB, [P, HALF], F32, "rest70"))
+        derivative(7, half(1), at(WOVEN + 3 * KB, [P, HALF], F32, "rest71"))
+        w1_woven = at(WOVEN + 6 * KB, [P, PACK * HALF], BF16, "w1_woven1")
+        weave_weight(nc.scalar.copy, w1b_raw, w1_woven[:], parts=4)
         gradient(0, 0, state(4))
         for t in range(PACK):
-            gate(0, t, 0, 2 + t)
-        whole(5)
-        (w1_q[1],), calls = quantize(
-            w1_woven, at(state(5), [P, HALF], U32, "w1b_codes"), "w1b"
-        )
-        calls[0]()
-        wr_s = at(state(5) + 2 * KB, [P, PASS], U8, "wr_s")
+            gate(0, t, 0, t)
+        wr_s = at(WOVEN + 3 * KB, [P, PASS], U8, "wr_s")
         nc.vector.tensor_copy(
             out=wr_s[:].rearrange("p (t q) -> p q t", t=PACK),
             in_=wr_s_raw[:].rearrange("p (q t) -> p q t", t=PACK),
         )
-        for j in range(HALVES):
-            derivative(6, half(j), at([RING, W1_RAW][j], [P, HALF], F32, f"rest6{j}"))
-        derivative(7, half(0), ring(2, [P, HALF], F32, "rest70"))
-        derivative(7, half(1), at(G_CODES, [P, HALF], F32, "rest71"))
-        g00_woven = at(W1_RAW + 8 * KB, [P, PACK * HALF], BF16, "g00_woven")
+        (w1_q[1],), calls = quantize(w1_woven, at(WOVEN + 4 * KB, [P, HALF], U32, "w1b_codes"), "w1b")
+        calls[0]()
+        gradient(0, 1, WOVEN + 6 * KB)
+        for t in range(2):
+            gate(0, t, 1, 4 + t, staged=at(G_CODES + 2 * KB * (1 - t), [P, HALF], F32, f"h0{t}1_staged"))
+        for t in range(2, PACK):
+            gate(0, t, 1, 4 + t)
+        g00_woven = at(state(5), [P, PACK * HALF], BF16, "g00_woven")
         for cols in pieces(HALF, 4):
             weave(g32[0, 0], g00_woven, cols)
 
@@ -247,29 +248,24 @@ def tile_list_dislocation_recurrent_backward_kernel(
                     in_=wr_w_raw[:].bitcast(U32)[:, a, PASS * b : PASS * (b + 1)].rearrange("p (q t) -> p q t", t=PACK),
                 )
 
-        gradient(1, 1, state(7))
-        for t in range(PACK - 1):
-            gate(1, t, 1, 6 + t)
-        g10_woven = at(WOVEN, [P, PACK * HALF], BF16, "g10_woven")
+        g10_woven = at(state(7), [P, PACK * HALF], BF16, "g10_woven")
 
         def woven_gate(u):
-            h = bank(2 + u, [P, PACK, P], f"h10c{u}")
+            h = bank(u, [P, PACK, P], f"h10c{u}")
             for t in range(PACK):
                 first_product(h[:, t, :], 1, t, lane(u), t == 0, t == PACK - 1)
             out = by_word(g10_woven[:, PASS * u : PASS * (u + 1)])
             nc.vector.tensor_tensor(out, by_lane(h[:]), by_lane(deriv[1][:, :, lane(u)]), MULT)
 
-        woven_gate(0)
-        woven_gate(1)
+        for u in range(PACK):
+            woven_gate(u)
         (g00_q,), calls = quantize(g00_woven, at(G_CODES, [P, HALF], U32, "g00_codes"), "g00")
         calls[0]()
-        (g10_q,), g10_calls = quantize(g10_woven, at(G_CODES + 2 * KB, [P, HALF], U32, "g10_codes"), "g10", parts=2)
-        g10_calls[0]()
-        woven_gate(2)
-        woven_gate(3)
-        g10_calls[1]()
+        (g10_q,), calls = quantize(g10_woven, at(G_CODES + 2 * KB, [P, HALF], U32, "g10_codes"), "g10")
+        calls[0]()
+        gradient(1, 1, state(7))
         quarter = HALF // 2
-        g1_woven = [ring(u, [P, PACK * HALF], BF16, f"g1_woven{u}") for u in range(2)]
+        g1_woven = [at(state(0) + 4 * KB * u, [P, PACK * HALF], BF16, f"g1_woven{u}") for u in range(2)]
 
         def weave_second_half(a):
             for u, cols in enumerate(pieces(HALF, 2)):
@@ -333,17 +329,18 @@ def tile_list_dislocation_recurrent_backward_kernel(
         b0_woven = at(WR_RAW, [P, 2 * PACK * HALF], BF16, "b0_woven")
         for b in range(GROUPS):
             b_woven[b, 0] = side(b0_woven, b)
-        summed_on_gpsimd(0, 0, 0, 6, term_tile(term_place(0), "term000"))
-        gate(1, 3, 1, 1)
-        weave_second_half(1)
-        summed_on_gpsimd(0, 0, 1, 7, term_tile(term_place(1), "term001"))
-        gate(0, 2, 1, 6)
-        summed_on_gpsimd(0, 0, 2, 0, term_tile(term_place(2), "term002"))
-        gate(0, 3, 1, 7)
         weave_second_half(0)
-        summed_on_gpsimd(0, 0, 3, 2, term_tile(term_place(3), "term003"))
+        gate(1, 0, 1, 4)
+        summed_on_gpsimd(0, 0, 0, 0, term_tile(term_place(0), "term000"))
+        gate(1, 1, 1, 5)
+        summed_on_gpsimd(0, 0, 1, 1, term_tile(term_place(1), "term001"))
+        gate(1, 2, 1, 6)
+        gate(1, 3, 1, 7)
+        weave_second_half(1)
+        summed_on_gpsimd(0, 0, 2, 2, term_tile(term_place(2), "term002"))
+        summed_on_gpsimd(0, 0, 3, 3, term_tile(term_place(3), "term003"))
         for u in range(PACK):
-            with_repeated_product(1, 0, u, [3, 4, 5, 1][u])
+            with_repeated_product(1, 0, u, 4 + u)
         wo_woven = at(state(3), [P, 2 * PACK * HALF], BF16, "wo_woven")
         for pair in (1, 0):
             for a in range(GROUPS):
@@ -410,15 +407,15 @@ def tile_list_dislocation_recurrent_backward_kernel(
         def place_first(u):
             nc.vector.tensor_copy(pages[page_order[u]][:].indirect(entries(scatter_list, half(0))), weighted[u][:])
 
-        term_banks = [[0], [6], [7, 2], [3], [4]]
-        empty(staged[0][:], page_order[0], 0, 1)
+        term_banks = [[0], [1], [2, 3], [4], [5]]
+        empty(staged[0][:], page_order[0], 0, 7)
         for n, run in enumerate(summed):
             for i, (b, u) in enumerate(run):
                 term_into(terms[n][:, :, lane(i)], b, 1, u, term_banks[n][i])
         for u in range(2, PACK):
-            with_repeated_product(1, 1, u, [5, 1][u - 2])
+            with_repeated_product(1, 1, u, 4 + u)
         for u in range(1, PACK - 1):
-            empty(staged[u][:], page_order[u], 0, [4, 5][u - 1])
+            empty(staged[u][:], page_order[u], 0, 4 + u)
         add_gradient(0)
         weigh(0)
         place_first(0)
@@ -430,8 +427,8 @@ def tile_list_dislocation_recurrent_backward_kernel(
         place_first(2)
         add_gradient(3)
         add_gradient(4)
-        empty(staged[3][:], page_order[3], 0, 1)
-        b1_q, calls = quantize(b1_woven, ring(1, [P, S], U32, "b1_codes"), "b1")
+        empty(staged[3][:], page_order[3], 0, 7)
+        b1_q, calls = quantize(b1_woven, at(state(0), [P, S], U32, "b1_codes"), "b1")
         calls[0]()
         b_q.append(b1_q)
 

@@ -33,8 +33,10 @@ W1_RAW = TABLE + 8 * KB
 WR_RAW = W1_RAW + 16 * KB
 RING = WR_RAW + 8 * KB
 WOVEN = RING + 13 * KB
-G_CODES = WOVEN + 14 * KB
+G_CODES = WOVEN + 11 * KB
 TERMS = G_CODES + 8 * KB
+STAGED = W1_RAW + 9 * KB
+LATE_WOVEN = W1_RAW + 12 * KB
 
 
 def tile_list_dislocation_recurrent_backward_kernel(
@@ -110,16 +112,15 @@ def tile_list_dislocation_recurrent_backward_kernel(
         tab_s = keep.tile([P, T], U8, name="tab_s", align_bytes=64)
         y_scales = keep.tile([P, T2], U8, name="y_scales", align_bytes=64)
         v_w = [keep.tile([P, HALF], U32, name="v_w0", align_bytes=64)]
-        v_s = keep.tile([P, S], U8, name="v_s", align_bytes=64)
         deriv = [at(DERIV + 16 * KB * a, [P, PACK, S], F32, f"d{a}") for a in range(GROUPS)]
-        weights = keep.tile([P, PACK, S], F32, name="weights", align_bytes=64)
+        weights = [keep.tile([P, PACK, HALF], F32, name=f"weights{j}", align_bytes=64) for j in range(HALVES)]
         page_order = [2, 0, 1, 3]
         pages = {t: at(PAGES + 8 * KB * u, [P, T2], F32, f"page{t}") for u, t in enumerate(page_order)}
         wr_s_raw = keep.tile([P, PASS], U8, name="wr_s_raw", align_bytes=64)
-        nc.vector.memset(tab_s[:].bitcast(I32), 0)
         nc.vector.memset(wr_s_raw[:].bitcast(I32), 0)
         for page in pages.values():
             nc.vector.memset(page[:], 0.0)
+        nc.vector.memset(tab_s[:].bitcast(I32), 0)
 
         s_rows = sT.rearrange("(a p t) c -> a t p c", p=P, t=PACK)
         s_tiles = {}
@@ -153,21 +154,25 @@ def tile_list_dislocation_recurrent_backward_kernel(
         tab_w = at(TABLE, [P, T], U32, "tab_w")
         nc.sync.dma_start(out=tab_w[:].bitcast(I32), in_=tab_words[0].rearrange("p t i -> p (t i)").bitcast(I32))
         for q in range(4):
-            nc.sync.dma_start(
+            nc.gpsimd.dma_start(
                 out=tab_s[32 * q : 32 * q + 4, :].bitcast(I32), in_=tab_scales[0, 4 * q : 4 * q + 4, :].bitcast(I32)
             )
         w1_parts = [load_w1_part(0)]
         load_state(7)
-        load_scale_rows(0)
         w1_parts.append(load_w1_part(1))
         w1b_raw = load_weight(W1_RAW + 8 * KB, "w1b_raw", w1[:, PASS : 2 * PASS])
-        load_scale_rows(1)
         wr_w_raw = at(WR_RAW, [P, GROUPS, H], I32, "wr_w_raw")
         nc.sync.dma_start(out=wr_w_raw[:], in_=wr_words.rearrange("a p c i -> p a (c i)").bitcast(I32))
-        wo_raw = [load_weight(tag, f"wo_raw{a}", wo[PASS * a : PASS * (a + 1), :]) for a, tag in enumerate([state(1), state(2)])]
+        wo_raw = []
+        for a in range(GROUPS):
+            load_scale_rows(a)
+            wo_raw.append(load_weight(state(1 + a), f"wo_raw{a}", wo[PASS * a : PASS * (a + 1), :]))
         nc.sync.dma_start(scatter_list[:], offs2)
-        for q in range(4):
-            nc.sync.dma_start(out=weights[32 * q : 32 * q + 32], in_=wgo.rearrange("(q t) j -> q t j", t=PACK))
+        for j in range(HALVES):
+            for q in range(4):
+                nc.sync.dma_start(
+                    out=weights[j][32 * q : 32 * q + 32], in_=wgo.rearrange("(q t) j -> q t j", t=PACK)[:, :, half(j)]
+                )
 
         def entries(lst, cols):
             return lst[:, cols.start // 16 : cols.stop // 16]
@@ -205,6 +210,7 @@ def tile_list_dislocation_recurrent_backward_kernel(
             gather_state(k)
             derivative(k, slice(0, S), ring(k, [P, S], F32, f"rest{k}"))
         nc.vector.tensor_copy(v_w[0][:], tab_w[:].indirect(entries(gather_list, half(0))))
+        v_s = at(state(6), [P, S], U8, "v_s")
         nc.vector.tensor_copy(v_s[:], tab_s[:].indirect(gather_list[:]))
         gather_state(7)
         w1_woven = at(WOVEN, [P, PACK * HALF], BF16, "w1_woven0")
@@ -215,32 +221,28 @@ def tile_list_dislocation_recurrent_backward_kernel(
             )
         (w1_q[0],), calls = quantize(w1_woven, ring(6, [P, HALF], U32, "w1a_codes"), "w1a")
         calls[0]()
-        v_w.append(at(WOVEN - KB, [P, HALF], U32, "v_w1"))
+        v_w.append(at(WOVEN + KB // 2, [P, HALF], U32, "v_w1"))
         nc.vector.tensor_copy(v_w[1][:], tab_w[:].indirect(entries(gather_list, half(1))))
-        derivative(7, half(0), at(WOVEN + KB, [P, HALF], F32, "rest70"))
-        derivative(7, half(1), at(WOVEN + 3 * KB, [P, HALF], F32, "rest71"))
-        w1_woven = at(WOVEN + 6 * KB, [P, PACK * HALF], BF16, "w1_woven1")
+        rest7 = at(WOVEN - 7 * KB // 2, [P, S], F32, "rest7")
+        for j in range(HALVES):
+            derivative(7, half(j), rest7[:, half(j)])
+        w1_woven = at(WOVEN + 5 * KB // 2, [P, PACK * HALF], BF16, "w1_woven1")
         weave_weight(nc.scalar.copy, w1b_raw, w1_woven[:], parts=4)
         gradient(0, 0, state(4))
         for t in range(PACK):
             gate(0, t, 0, t)
-        wr_s = at(WOVEN + 3 * KB, [P, PASS], U8, "wr_s")
-        nc.vector.tensor_copy(
-            out=wr_s[:].rearrange("p (t q) -> p q t", t=PACK),
-            in_=wr_s_raw[:].rearrange("p (q t) -> p q t", t=PACK),
-        )
-        (w1_q[1],), calls = quantize(w1_woven, at(WOVEN + 4 * KB, [P, HALF], U32, "w1b_codes"), "w1b")
+        (w1_q[1],), calls = quantize(w1_woven, at(WOVEN - 7 * KB // 2, [P, HALF], U32, "w1b_codes"), "w1b")
         calls[0]()
-        gradient(0, 1, WOVEN + 6 * KB)
+        gradient(0, 1, WOVEN + 5 * KB // 2)
         for t in range(2):
-            gate(0, t, 1, 4 + t, staged=at(G_CODES + 2 * KB * (1 - t), [P, HALF], F32, f"h0{t}1_staged"))
+            gate(0, t, 1, 4 + t, staged=at([WOVEN - 3 * KB // 2, STAGED][t], [P, HALF], F32, f"h0{t}1_staged"))
         for t in range(2, PACK):
             gate(0, t, 1, 4 + t)
-        g00_woven = at(state(5), [P, PACK * HALF], BF16, "g00_woven")
+        g00_woven = at(LATE_WOVEN, [P, PACK * HALF], BF16, "g00_woven")
         for cols in pieces(HALF, 4):
             weave(g32[0, 0], g00_woven, cols)
 
-        wr_w = at(W1_RAW, [P, GROUPS, GROUPS, PASS], U32, "wr_w")
+        wr_w = at(W1_RAW + KB, [P, GROUPS, GROUPS, PASS], U32, "wr_w")
         for b in range(GROUPS):
             for a in range(GROUPS):
                 nc.scalar.copy(
@@ -259,7 +261,14 @@ def tile_list_dislocation_recurrent_backward_kernel(
 
         for u in range(PACK):
             woven_gate(u)
-        (g00_q,), calls = quantize(g00_woven, at(G_CODES, [P, HALF], U32, "g00_codes"), "g00")
+        wr_s = at(STAGED, [P, PASS], U8, "wr_s")
+        nc.vector.tensor_copy(
+            out=wr_s[:].rearrange("p (t q) -> p q t", t=PACK),
+            in_=wr_s_raw[:].rearrange("p (q t) -> p q t", t=PACK),
+        )
+        (g00_q,), calls = quantize(
+            g00_woven, at(G_CODES, [P, HALF], U32, "g00_codes"), "g00", scales=at(STAGED + KB, [P, HALF], U8, "g00_scales")
+        )
         calls[0]()
         (g10_q,), calls = quantize(g10_woven, at(G_CODES + 2 * KB, [P, HALF], U32, "g10_codes"), "g10")
         calls[0]()
@@ -326,22 +335,21 @@ def tile_list_dislocation_recurrent_backward_kernel(
         def term_tile(place, name):
             return at(place, [P, PACK, P], F32, name)
 
-        b0_woven = at(WR_RAW, [P, 2 * PACK * HALF], BF16, "b0_woven")
+        b0_woven = at(state(5), [P, 2 * PACK * HALF], BF16, "b0_woven")
         for b in range(GROUPS):
             b_woven[b, 0] = side(b0_woven, b)
         weave_second_half(0)
         gate(1, 0, 1, 4)
-        summed_on_gpsimd(0, 0, 0, 0, term_tile(term_place(0), "term000"))
-        gate(1, 1, 1, 5)
-        summed_on_gpsimd(0, 0, 1, 1, term_tile(term_place(1), "term001"))
-        gate(1, 2, 1, 6)
-        gate(1, 3, 1, 7)
-        weave_second_half(1)
-        summed_on_gpsimd(0, 0, 2, 2, term_tile(term_place(2), "term002"))
-        summed_on_gpsimd(0, 0, 3, 3, term_tile(term_place(3), "term003"))
         for u in range(PACK):
-            with_repeated_product(1, 0, u, 4 + u)
-        wo_woven = at(state(3), [P, 2 * PACK * HALF], BF16, "wo_woven")
+            summed_on_gpsimd(0, 0, u, u, term_tile(term_place(u), f"term00{u}"))
+            if 0 < u < PACK - 1:
+                gate(1, u, 1, u - 1)
+            if u == PACK - 2:
+                gate(1, PACK - 1, 1, u)
+                weave_second_half(1)
+        for u in range(PACK):
+            with_repeated_product(1, 0, u, [5, 6, 7, 4][u])
+        wo_woven = at(LATE_WOVEN, [P, 2 * PACK * HALF], BF16, "wo_woven")
         for pair in (1, 0):
             for a in range(GROUPS):
                 lanes = slice(2 * pair, 2 * pair + 2)
@@ -356,7 +364,7 @@ def tile_list_dislocation_recurrent_backward_kernel(
             )
             calls[0]()
             g1_q.append(codes)
-        b0_q, calls = quantize(b0_woven, ring(2, [P, S], U32, "b0_codes"), "b0")
+        b0_q, calls = quantize(b0_woven, ring(1, [P, S], U32, "b0_codes"), "b0")
         calls[0]()
         wo_q, calls = quantize(
             wo_woven, at(term_place(0), [P, S], U32, "wo_codes"), "wo",
@@ -381,7 +389,7 @@ def tile_list_dislocation_recurrent_backward_kernel(
             nc.scalar.copy(out=dst, in_=output_product(t, j, k)[:])
 
         summed = [[(0, 0)], [(0, 1)], [(1, 0), (1, 1)], [(0, 2)], [(0, 3)]]
-        term_places = [state(3), state(3) + 2 * KB, state(4), state(4) + 4 * KB, state(4) + 6 * KB]
+        term_places = [LATE_WOVEN, LATE_WOVEN + 2 * KB, state(4), state(4) + 4 * KB, state(4) + 6 * KB]
         terms = [
             at(place, [P, PACK, P * len(run)], F32, f"terms{n}") for n, (place, run) in enumerate(zip(term_places, summed))
         ]
@@ -390,7 +398,7 @@ def tile_list_dislocation_recurrent_backward_kernel(
         weighted_places = [state(1) + 10 * KB, term_places[1], term_places[2]]
         weighted = [at(place, [P, HALF], F32, f"y_first{u}") for u, place in enumerate(weighted_places)]
         sum_places = [state(1) + 12 * KB] + staged_places[:2] + [staged_places[2] - KB, staged_places[2] + KB]
-        b1_woven = at(state(6), [P, 2 * PACK * HALF], BF16, "b1_woven")
+        b1_woven = at(state(3), [P, 2 * PACK * HALF], BF16, "b1_woven")
         for b in range(GROUPS):
             b_woven[b, 1] = side(b1_woven, b)
 
@@ -402,20 +410,20 @@ def tile_list_dislocation_recurrent_backward_kernel(
                 nc.scalar.copy(out=words_of(b, 1, lane(u + i)), in_=by_lane(total[:, :, lane(i)]))
 
         def weigh(u):
-            nc.gpsimd.tensor_tensor(weighted[u][:], staged[u][:], weights[:, page_order[u], half(0)], MULT)
+            nc.gpsimd.tensor_tensor(weighted[u][:], staged[u][:], weights[0][:, page_order[u], :], MULT)
 
         def place_first(u):
             nc.vector.tensor_copy(pages[page_order[u]][:].indirect(entries(scatter_list, half(0))), weighted[u][:])
 
-        term_banks = [[0], [1], [2, 3], [4], [5]]
-        empty(staged[0][:], page_order[0], 0, 7)
+        term_banks = [[0], [1], [2, 3], [5], [6]]
+        empty(staged[0][:], page_order[0], 0, 4)
         for n, run in enumerate(summed):
             for i, (b, u) in enumerate(run):
                 term_into(terms[n][:, :, lane(i)], b, 1, u, term_banks[n][i])
         for u in range(2, PACK):
-            with_repeated_product(1, 1, u, 4 + u)
+            with_repeated_product(1, 1, u, [7, 4][u - 2])
         for u in range(1, PACK - 1):
-            empty(staged[u][:], page_order[u], 0, 4 + u)
+            empty(staged[u][:], page_order[u], 0, u - 1)
         add_gradient(0)
         weigh(0)
         place_first(0)
@@ -427,13 +435,13 @@ def tile_list_dislocation_recurrent_backward_kernel(
         place_first(2)
         add_gradient(3)
         add_gradient(4)
-        empty(staged[3][:], page_order[3], 0, 7)
+        empty(staged[3][:], page_order[3], 0, 4)
         b1_q, calls = quantize(b1_woven, at(state(0), [P, S], U32, "b1_codes"), "b1")
         calls[0]()
         b_q.append(b1_q)
 
         def place_weighing(t, src, j):
-            nc.vector.tensor_tensor(pages[t][:].indirect(entries(scatter_list, half(j))), src, weights[:, t, half(j)], MULT)
+            nc.vector.tensor_tensor(pages[t][:].indirect(entries(scatter_list, half(j))), src, weights[j][:, t, :], MULT)
 
         place_weighing(page_order[3], staged[3][:], 0)
 
@@ -486,7 +494,7 @@ def tile_list_dislocation_recurrent_backward_kernel(
             join_pairs(n, nc.scalar.copy, U32)
 
         words_out = out_1[0].rearrange("p m t -> p (m t)").bitcast(I32)
-        y_codes = at(state(5), [P, T2], U32, "y_codes")
+        y_codes = at(state(6), [P, T2], U32, "y_codes")
         stored = 0
         for n, cols in enumerate(chunks):
             nc.vector.quantize_mx(out=y_codes[:, cols].bitcast(E4M3), scales=y_scales[:, cols], in_=y_woven[n][:])

@@ -35,6 +35,7 @@ RING = WR_RAW + 8 * KB
 WOVEN = RING + 13 * KB
 G_CODES = WOVEN + 11 * KB
 TERMS = G_CODES + 8 * KB
+WR_SCALES = TERMS + 9 * KB
 STAGED = W1_RAW + 9 * KB
 LATE_WOVEN = W1_RAW + 12 * KB
 
@@ -116,7 +117,7 @@ def tile_list_dislocation_recurrent_backward_kernel(
         weights = [keep.tile([P, PACK, HALF], F32, name=f"weights{j}", align_bytes=64) for j in range(HALVES)]
         page_order = [2, 0, 1, 3]
         pages = {t: at(PAGES + 8 * KB * u, [P, T2], F32, f"page{t}") for u, t in enumerate(page_order)}
-        wr_s_raw = keep.tile([P, PASS], U8, name="wr_s_raw", align_bytes=64)
+        wr_s_raw = at(WR_SCALES, [P, PASS], U8, "wr_s_raw")
         nc.vector.memset(wr_s_raw[:].bitcast(I32), 0)
         for page in pages.values():
             nc.vector.memset(page[:], 0.0)
@@ -153,20 +154,18 @@ def tile_list_dislocation_recurrent_backward_kernel(
             load_state(k)
         tab_w = at(TABLE, [P, T], U32, "tab_w")
         nc.sync.dma_start(out=tab_w[:].bitcast(I32), in_=tab_words[0].rearrange("p t i -> p (t i)").bitcast(I32))
+        load_state(7)
         for q in range(4):
-            nc.gpsimd.dma_start(
+            nc.sync.dma_start(
                 out=tab_s[32 * q : 32 * q + 4, :].bitcast(I32), in_=tab_scales[0, 4 * q : 4 * q + 4, :].bitcast(I32)
             )
-        w1_parts = [load_w1_part(0)]
-        load_state(7)
-        w1_parts.append(load_w1_part(1))
+        w1_parts = [load_w1_part(u) for u in range(2)]
         w1b_raw = load_weight(W1_RAW + 8 * KB, "w1b_raw", w1[:, PASS : 2 * PASS])
+        load_scale_rows(0)
         wr_w_raw = at(WR_RAW, [P, GROUPS, H], I32, "wr_w_raw")
         nc.sync.dma_start(out=wr_w_raw[:], in_=wr_words.rearrange("a p c i -> p a (c i)").bitcast(I32))
-        wo_raw = []
-        for a in range(GROUPS):
-            load_scale_rows(a)
-            wo_raw.append(load_weight(state(1 + a), f"wo_raw{a}", wo[PASS * a : PASS * (a + 1), :]))
+        load_scale_rows(1)
+        wo_raw = [load_weight(state(1 + a), f"wo_raw{a}", wo[PASS * a : PASS * (a + 1), :]) for a in range(GROUPS)]
         nc.sync.dma_start(scatter_list[:], offs2)
         for j in range(HALVES):
             for q in range(4):
@@ -210,9 +209,9 @@ def tile_list_dislocation_recurrent_backward_kernel(
             gather_state(k)
             derivative(k, slice(0, S), ring(k, [P, S], F32, f"rest{k}"))
         nc.vector.tensor_copy(v_w[0][:], tab_w[:].indirect(entries(gather_list, half(0))))
-        v_s = at(state(6), [P, S], U8, "v_s")
-        nc.vector.tensor_copy(v_s[:], tab_s[:].indirect(gather_list[:]))
         gather_state(7)
+        v_s = keep.tile([P, S], U8, name="v_s", align_bytes=64)
+        nc.vector.tensor_copy(v_s[:], tab_s[:].indirect(gather_list[:]))
         w1_woven = at(WOVEN, [P, PACK * HALF], BF16, "w1_woven0")
         for u, raw in enumerate(w1_parts):
             nc.scalar.copy(
@@ -252,36 +251,41 @@ def tile_list_dislocation_recurrent_backward_kernel(
 
         g10_woven = at(state(7), [P, PACK * HALF], BF16, "g10_woven")
 
-        def woven_gate(u):
-            h = bank(u, [P, PACK, P], f"h10c{u}")
+        def column_gate(j, u, k, woven=None):
+            h = bank(k, [P, PACK, P], f"h1{j}c{u}")
+            cols = slice(HALF * j + P * u, HALF * j + P * (u + 1))
             for t in range(PACK):
-                first_product(h[:, t, :], 1, t, lane(u), t == 0, t == PACK - 1)
-            out = by_word(g10_woven[:, PASS * u : PASS * (u + 1)])
-            nc.vector.tensor_tensor(out, by_lane(h[:]), by_lane(deriv[1][:, :, lane(u)]), MULT)
+                first_product(h[:, t, :], 1, t, cols, t == 0, t == PACK - 1)
+            if woven is None:
+                nc.vector.tensor_tensor(g32[1, j][:, :, lane(u)], h[:], deriv[1][:, :, cols], MULT)
+            else:
+                nc.vector.tensor_tensor(by_word(woven), by_lane(h[:]), by_lane(deriv[1][:, :, cols]), MULT)
 
         for u in range(PACK):
-            woven_gate(u)
+            column_gate(0, u, u, g10_woven[:, PASS * u : PASS * (u + 1)])
         wr_s = at(STAGED, [P, PASS], U8, "wr_s")
         nc.vector.tensor_copy(
             out=wr_s[:].rearrange("p (t q) -> p q t", t=PACK),
             in_=wr_s_raw[:].rearrange("p (q t) -> p q t", t=PACK),
         )
         (g00_q,), calls = quantize(
-            g00_woven, at(G_CODES, [P, HALF], U32, "g00_codes"), "g00", scales=at(STAGED + KB, [P, HALF], U8, "g00_scales")
+            g00_woven, at(G_CODES, [P, HALF], U32, "g00_codes"), "g00", scales=at(WR_SCALES - PASS // 2, [P, HALF], U8, "g00_scales")
         )
         calls[0]()
-        (g10_q,), calls = quantize(g10_woven, at(G_CODES + 2 * KB, [P, HALF], U32, "g10_codes"), "g10")
+        (g10_q,), calls = quantize(
+            g10_woven, at(G_CODES + 2 * KB, [P, HALF], U32, "g10_codes"), "g10",
+            scales=at(WR_SCALES + PASS // 2, [P, HALF], U8, "g10_scales"),
+        )
         calls[0]()
-        gradient(1, 1, state(7))
         quarter = HALF // 2
-        g1_woven = [at(state(0) + 4 * KB * u, [P, PACK * HALF], BF16, f"g1_woven{u}") for u in range(2)]
+        g32[1, 1] = at(state(7) - 2 * KB, [P, PACK, quarter], F32, "g11")
+        g1_woven = [
+            at(place, [P, PACK * HALF], BF16, f"g1_woven{u}") for u, place in enumerate([state(0), state(7) + 2 * KB])
+        ]
 
-        def weave_second_half(a):
-            for u, cols in enumerate(pieces(HALF, 2)):
-                nc.scalar.copy(
-                    out=by_word(g1_woven[u][:, PACK * quarter * a : PACK * quarter * (a + 1)]),
-                    in_=by_lane(g32[a, 1][:, :, cols]),
-                )
+        def quarter_views(a, u):
+            dst = by_word(g1_woven[u][:, PACK * quarter * a : PACK * quarter * (a + 1)])
+            return dst, by_lane(g32[a, 1][:, :, quarter * u : quarter * (u + 1)])
 
         g1_q = []
 
@@ -338,17 +342,21 @@ def tile_list_dislocation_recurrent_backward_kernel(
         b0_woven = at(state(5), [P, 2 * PACK * HALF], BF16, "b0_woven")
         for b in range(GROUPS):
             b_woven[b, 0] = side(b0_woven, b)
-        weave_second_half(0)
-        gate(1, 0, 1, 4)
+        for u in range(2):
+            nc.scalar.copy(*quarter_views(0, u))
         for u in range(PACK):
-            summed_on_gpsimd(0, 0, u, u, term_tile(term_place(u), f"term00{u}"))
-            if 0 < u < PACK - 1:
-                gate(1, u, 1, u - 1)
-            if u == PACK - 2:
-                gate(1, PACK - 1, 1, u)
-                weave_second_half(1)
-        for u in range(PACK):
-            with_repeated_product(1, 0, u, [5, 6, 7, 4][u])
+            woven = None if u < 2 else g1_woven[1][:, PASS * u : PASS * (u + 1)]
+            column_gate(1, u, 4 + u, woven)
+            if u == 1:
+                nc.scalar.copy(*quarter_views(1, 0))
+            if u < PACK - 1:
+                summed_on_gpsimd(0, 0, u, u, term_tile(term_place(u), f"term00{u}"))
+        for u in range(PACK - 1):
+            with_repeated_product(1, 0, u, 4 + u)
+        last_term = term_tile(term_place(3), "term003")
+        term_into(last_term[:], 0, 0, 3, 3)
+        with_repeated_product(1, 0, 3, 7)
+        nc.vector.tensor_tensor(words_of(0, 0, lane(3)), by_lane(last_term[:]), by_lane(g32[0, 0][:, :, lane(3)]), ADD)
         wo_woven = at(LATE_WOVEN, [P, 2 * PACK * HALF], BF16, "wo_woven")
         for pair in (1, 0):
             for a in range(GROUPS):
@@ -360,7 +368,7 @@ def tile_list_dislocation_recurrent_backward_kernel(
         for u in range(2):
             (codes,), calls = quantize(
                 g1_woven[u], at(G_CODES + 4 * KB + 2 * KB * u, [P, HALF], U32, f"g1_codes{u}"), f"g1{u}",
-                scales=at(term_place(3) + HALF * u, [P, HALF], U8, f"g1_scales{u}"),
+                scales=at(term_place(2) + HALF * u, [P, HALF], U8, f"g1_scales{u}"),
             )
             calls[0]()
             g1_q.append(codes)
@@ -368,7 +376,7 @@ def tile_list_dislocation_recurrent_backward_kernel(
         calls[0]()
         wo_q, calls = quantize(
             wo_woven, at(term_place(0), [P, S], U32, "wo_codes"), "wo",
-            scales=at(term_place(3) + KB, [P, S], U8, "wo_scales"),
+            scales=at(term_place(2) + KB, [P, S], U8, "wo_scales"),
         )
         calls[0]()
 
@@ -415,13 +423,13 @@ def tile_list_dislocation_recurrent_backward_kernel(
         def place_first(u):
             nc.vector.tensor_copy(pages[page_order[u]][:].indirect(entries(scatter_list, half(0))), weighted[u][:])
 
-        term_banks = [[0], [1], [2, 3], [5], [6]]
-        empty(staged[0][:], page_order[0], 0, 4)
+        term_banks = [[0], [1], [2, 3], [4], [5]]
+        empty(staged[0][:], page_order[0], 0, 7)
         for n, run in enumerate(summed):
             for i, (b, u) in enumerate(run):
                 term_into(terms[n][:, :, lane(i)], b, 1, u, term_banks[n][i])
         for u in range(2, PACK):
-            with_repeated_product(1, 1, u, [7, 4][u - 2])
+            with_repeated_product(1, 1, u, 4 + u)
         for u in range(1, PACK - 1):
             empty(staged[u][:], page_order[u], 0, u - 1)
         add_gradient(0)
@@ -435,7 +443,7 @@ def tile_list_dislocation_recurrent_backward_kernel(
         place_first(2)
         add_gradient(3)
         add_gradient(4)
-        empty(staged[3][:], page_order[3], 0, 4)
+        empty(staged[3][:], page_order[3], 0, 7)
         b1_q, calls = quantize(b1_woven, at(state(0), [P, S], U32, "b1_codes"), "b1")
         calls[0]()
         b_q.append(b1_q)

@@ -27,17 +27,17 @@ GROUPS = H // PASS
 KB = 1024
 DERIV = 0
 PAGES = DERIV + 32 * KB
-STATES = PAGES + 32 * KB
+STATES = PAGES + 24 * KB
 TABLE = STATES + 64 * KB
-W1_RAW = TABLE + 8 * KB
-WR_RAW = W1_RAW + 16 * KB
-RING = WR_RAW + 8 * KB
-WOVEN = RING + 13 * KB
-G_CODES = WOVEN + 11 * KB
+WR_RAW = TABLE + 8 * KB
+W1_RAW = WR_RAW + 8 * KB
+RING = W1_RAW + 21 * KB
+WOVEN = RING + 12 * KB
+G_CODES = WOVEN + 12 * KB
 TERMS = G_CODES + 8 * KB
 WR_SCALES = TERMS + 9 * KB
-STAGED = W1_RAW + 9 * KB
-LATE_WOVEN = W1_RAW + 12 * KB
+LAST_REST = W1_RAW + 19 * KB // 2
+LATE_WOVEN = W1_RAW + 21 * KB // 2
 
 
 def tile_list_dislocation_recurrent_backward_kernel(
@@ -88,14 +88,6 @@ def tile_list_dislocation_recurrent_backward_kernel(
                 )
             return [(codes[:, half(u)], scales[:, half(u)]) for u in range(width // HALF)], calls
 
-        def weave_weight(copy, raw, dst, parts=1):
-            width = P // parts
-            for u in range(parts):
-                copy(
-                    out=dst.rearrange("p (t m i) -> p m i t", t=PACK, i=PACK)[:, width * u : width * (u + 1)],
-                    in_=raw[:].rearrange("p i (m t) -> p m i t", t=PACK)[:, width * u : width * (u + 1)],
-                )
-
         def by_word(dst):
             return dst.rearrange("p (c i t) -> p c t i", t=PACK, i=4)
 
@@ -112,16 +104,18 @@ def tile_list_dislocation_recurrent_backward_kernel(
         scatter_list = keep.tile([P, S // 16], U16, name="scatter_list")
         tab_s = keep.tile([P, T], U8, name="tab_s", align_bytes=64)
         y_scales = keep.tile([P, T2], U8, name="y_scales", align_bytes=64)
-        v_w = [keep.tile([P, HALF], U32, name="v_w0", align_bytes=64)]
-        deriv = [at(DERIV + 16 * KB * a, [P, PACK, S], F32, f"d{a}") for a in range(GROUPS)]
+        v_w = keep.tile([P, S], U32, name="v_w", align_bytes=64)
+        v_s = keep.tile([P, S], U8, name="v_s", align_bytes=64)
+        deriv_rows = [at(DERIV + 16 * KB * a, [P, PACK * S], F32, f"d{a}") for a in range(GROUPS)]
+        deriv = [rows[:].rearrange("p (t c) -> p t c", t=PACK) for rows in deriv_rows]
         weights = [keep.tile([P, PACK, HALF], F32, name=f"weights{j}", align_bytes=64) for j in range(HALVES)]
         page_order = [2, 0, 1, 3]
-        pages = {t: at(PAGES + 8 * KB * u, [P, T2], F32, f"page{t}") for u, t in enumerate(page_order)}
+        pages = {t: at(PAGES + 8 * KB * u, [P, T2], F32, f"page{t}") for u, t in enumerate(page_order[:-1])}
         wr_s_raw = at(WR_SCALES, [P, PASS], U8, "wr_s_raw")
+        nc.vector.memset(tab_s[:].bitcast(I32), 0)
         nc.vector.memset(wr_s_raw[:].bitcast(I32), 0)
         for page in pages.values():
             nc.vector.memset(page[:], 0.0)
-        nc.vector.memset(tab_s[:].bitcast(I32), 0)
 
         s_rows = sT.rearrange("(a p t) c -> a t p c", p=P, t=PACK)
         s_tiles = {}
@@ -129,11 +123,6 @@ def tile_list_dislocation_recurrent_backward_kernel(
         def load_state(k):
             s_tiles[k] = at(state(k), [P, T], F32, f"s{k}")
             nc.sync.dma_start(out=s_tiles[k][:], in_=s_rows[k // PACK, k % PACK])
-
-        def load_weight(tag, name, rows):
-            raw = at(tag, [P, PACK, HALF], F32, name)
-            nc.sync.dma_start(out=raw[:], in_=rows.rearrange("(p i) c -> p i c", i=PACK))
-            return raw
 
         def load_scale_rows(a):
             for q in range(4):
@@ -150,22 +139,26 @@ def tile_list_dislocation_recurrent_backward_kernel(
 
         load_state(0)
         nc.sync.dma_start(gather_list[:], offs)
-        for k in range(1, 7):
-            load_state(k)
+        load_state(1)
         tab_w = at(TABLE, [P, T], U32, "tab_w")
         nc.sync.dma_start(out=tab_w[:].bitcast(I32), in_=tab_words[0].rearrange("p t i -> p (t i)").bitcast(I32))
-        load_state(7)
-        for q in range(4):
-            nc.sync.dma_start(
-                out=tab_s[32 * q : 32 * q + 4, :].bitcast(I32), in_=tab_scales[0, 4 * q : 4 * q + 4, :].bitcast(I32)
-            )
+        for r in range(4):
+            nc.sync.dma_start(out=tab_s[r:P:32, :].bitcast(I32), in_=tab_scales[0, r:16:4, :].bitcast(I32))
         w1_parts = [load_w1_part(u) for u in range(2)]
-        w1b_raw = load_weight(W1_RAW + 8 * KB, "w1b_raw", w1[:, PASS : 2 * PASS])
+        for k in range(2, 7):
+            load_state(k)
+        load_state(7)
+        w1_parts.extend(load_w1_part(u) for u in range(2, 4))
         load_scale_rows(0)
         wr_w_raw = at(WR_RAW, [P, GROUPS, H], I32, "wr_w_raw")
         nc.sync.dma_start(out=wr_w_raw[:], in_=wr_words.rearrange("a p c i -> p a (c i)").bitcast(I32))
         load_scale_rows(1)
-        wo_raw = [load_weight(state(1 + a), f"wo_raw{a}", wo[PASS * a : PASS * (a + 1), :]) for a in range(GROUPS)]
+        wo_parts = []
+        for u in range(2 * GROUPS):
+            raw = at(state(1) + 4 * KB * u, [P, PACK, N // 2], F32, f"wo_part{u}")
+            rows = wo[PASS * (u // 2) : PASS * (u // 2 + 1), N // 2 * (u % 2) : N // 2 * (u % 2 + 1)]
+            nc.sync.dma_start(out=raw[:], in_=rows.rearrange("(p i) c -> p i c", i=PACK))
+            wo_parts.append(raw)
         nc.sync.dma_start(scatter_list[:], offs2)
         for j in range(HALVES):
             for q in range(4):
@@ -179,18 +172,22 @@ def tile_list_dislocation_recurrent_backward_kernel(
         g32 = {}
         w1_q = {}
 
-        def gather_state(k):
-            nc.vector.tensor_copy(deriv[k // PACK][:, k % PACK, :], s_tiles[k][:].indirect(gather_list[:]))
+        def gather_state(k, cols, picked=None):
+            picked = deriv[k // PACK][:, k % PACK, cols] if picked is None else picked[:]
+            nc.vector.tensor_copy(picked, s_tiles[k][:].indirect(entries(gather_list, cols)))
+            return picked
 
-        def derivative(k, cols, rest):
-            d = deriv[k // PACK][:, k % PACK, cols]
-            nc.scalar.activation(out=rest[:], in_=d, func=COPY, scale=-1.0, bias=1.0)
-            nc.gpsimd.tensor_tensor(d, d, rest[:], MULT)
+        def derivative(k, cols, picked, rest):
+            nc.scalar.activation(out=rest[:], in_=picked, func=COPY, scale=-1.0, bias=1.0)
+            nc.gpsimd.tensor_tensor(deriv[k // PACK][:, k % PACK, cols], picked, rest[:], MULT)
+
+        def whole(k):
+            derivative(k, slice(0, S), gather_state(k, slice(0, S)), ring(k, [P, S], F32, f"rest{k}"))
 
         def first_product(out, a, t, cols, start, stop):
             nc.tensor.matmul_mx(
                 out=out, lhsT=w1_q[a][0][:, lane(t)].bitcast(E4M3), lhsT_scale=w1_q[a][1][:, lane(t)],
-                rhs=v_w[cols.start // HALF][:, cols.start % HALF : cols.start % HALF + cols.stop - cols.start].bitcast(E5M2), rhs_scale=v_s[:, cols], start=start, stop=stop,
+                rhs=v_w[:, cols].bitcast(E5M2), rhs_scale=v_s[:, cols], start=start, stop=stop,
             )
 
         def gate(a, t, j, k, staged=None):
@@ -202,85 +199,97 @@ def tile_list_dislocation_recurrent_backward_kernel(
             else:
                 nc.vector.tensor_tensor(g32[a, j][:, t, :], h[:], deriv[a][:, t, half(j)], MULT)
 
-        def gradient(a, j, tag):
-            g32[a, j] = at(tag, [P, PACK, HALF], F32, f"g{a}{j}")
+        def column_gate(a, j, u, k, woven=None):
+            h = bank(k, [P, PACK, P], f"h{a}{j}c{u}")
+            cols = slice(HALF * j + P * u, HALF * j + P * (u + 1))
+            for t in range(PACK):
+                first_product(h[:, t, :], a, t, cols, t == 0, t == PACK - 1)
+            if woven is None:
+                nc.vector.tensor_tensor(g32[a, j][:, :, lane(u)], h[:], deriv[a][:, :, cols], MULT)
+            else:
+                nc.vector.tensor_tensor(by_word(woven), by_lane(h[:]), by_lane(deriv[a][:, :, cols]), MULT)
 
-        for k in range(7):
-            gather_state(k)
-            derivative(k, slice(0, S), ring(k, [P, S], F32, f"rest{k}"))
-        nc.vector.tensor_copy(v_w[0][:], tab_w[:].indirect(entries(gather_list, half(0))))
-        gather_state(7)
-        v_s = keep.tile([P, S], U8, name="v_s", align_bytes=64)
+        def weave_w1(a, woven):
+            for u in range(2):
+                nc.scalar.copy(
+                    out=woven.rearrange("p (t m i) -> p m i t", t=PACK, i=PACK)[:, P // 2 * u : P // 2 * (u + 1)],
+                    in_=w1_parts[2 * a + u][:].rearrange("p i (m t) -> p m i t", t=PACK),
+                )
+
+        whole(0)
+        pages[page_order[-1]] = at(state(0), [P, T2], F32, "page_last")
+        nc.gpsimd.memset(pages[page_order[-1]][:], 0.0)
+        whole(1)
+        nc.vector.tensor_copy(v_w[:], tab_w[:].indirect(gather_list[:]))
         nc.vector.tensor_copy(v_s[:], tab_s[:].indirect(gather_list[:]))
         w1_woven = at(WOVEN, [P, PACK * HALF], BF16, "w1_woven0")
-        for u, raw in enumerate(w1_parts):
-            nc.scalar.copy(
-                out=w1_woven[:].rearrange("p (t m i) -> p m i t", t=PACK, i=PACK)[:, P // 2 * u : P // 2 * (u + 1)],
-                in_=raw[:].rearrange("p i (m t) -> p m i t", t=PACK),
-            )
-        (w1_q[0],), calls = quantize(w1_woven, ring(6, [P, HALF], U32, "w1a_codes"), "w1a")
+        weave_w1(0, w1_woven[:])
+        (w1_q[0],), calls = quantize(w1_woven, keep.tile([P, HALF], U32, name="w1a_codes", align_bytes=64), "w1a")
         calls[0]()
-        v_w.append(at(WOVEN + KB // 2, [P, HALF], U32, "v_w1"))
-        nc.vector.tensor_copy(v_w[1][:], tab_w[:].indirect(entries(gather_list, half(1))))
-        rest7 = at(WOVEN - 7 * KB // 2, [P, S], F32, "rest7")
-        for j in range(HALVES):
-            derivative(7, half(j), rest7[:, half(j)])
-        w1_woven = at(WOVEN + 5 * KB // 2, [P, PACK * HALF], BF16, "w1_woven1")
-        weave_weight(nc.scalar.copy, w1b_raw, w1_woven[:], parts=4)
-        gradient(0, 0, state(4))
-        for t in range(PACK):
-            gate(0, t, 0, t)
-        (w1_q[1],), calls = quantize(w1_woven, at(WOVEN - 7 * KB // 2, [P, HALF], U32, "w1b_codes"), "w1b")
-        calls[0]()
-        gradient(0, 1, WOVEN + 5 * KB // 2)
+        g32[0, 1] = at(TABLE, [P, PACK, HALF], F32, "g01")
         for t in range(2):
-            gate(0, t, 1, 4 + t, staged=at([WOVEN - 3 * KB // 2, STAGED][t], [P, HALF], F32, f"h0{t}1_staged"))
-        for t in range(2, PACK):
-            gate(0, t, 1, 4 + t)
-        g00_woven = at(LATE_WOVEN, [P, PACK * HALF], BF16, "g00_woven")
-        for cols in pieces(HALF, 4):
-            weave(g32[0, 0], g00_woven, cols)
+            gate(0, t, 1, 4 + t, staged=at([RING + 8 * KB, G_CODES + 4 * KB][t], [P, HALF], F32, f"h0{t}1_staged"))
+        for k in range(2, 6):
+            whole(k)
+        picked60 = gather_state(6, half(0))
+        picked61 = gather_state(6, half(1), at(WOVEN, [P, HALF], F32, "picked61"))
+        derivative(6, half(0), picked60, at(RING, [P, HALF], F32, "rest60"))
+        w1_woven = deriv[1][:, 3, :].bitcast(BF16)
+        weave_w1(1, w1_woven)
+        g32[0, 0] = at(state(6), [P, PACK, HALF - P], F32, "g00")
+        for u in range(PACK - 1):
+            column_gate(0, 0, u, u)
+        picked70 = gather_state(7, half(0), deriv[1][:, 2, half(1)])
+        (w1_q[1],), calls = quantize(
+            w1_woven, keep.tile([P, HALF], U32, name="w1b_codes", align_bytes=64), "w1b",
+            scales=at(RING, [P, HALF], U8, "w1b_scales"),
+        )
+        calls[0]()
+        g00_woven = at(W1_RAW + 15 * KB, [P, PACK * HALF], BF16, "g00_woven")
+        column_gate(0, 0, 3, 3, g00_woven[:, 3 * PASS : 4 * PASS])
+        picked71 = gather_state(7, half(1), at(W1_RAW + 13 * KB, [P, HALF], F32, "picked71"))
+        derivative(7, half(0), picked70, at(W1_RAW + 11 * KB, [P, HALF], F32, "rest70"))
+        derivative(6, half(1), picked61, at(W1_RAW + 4 * KB, [P, HALF], F32, "rest61"))
+        for u in range(2):
+            weave(g32[0, 0], g00_woven, lane(u))
+        derivative(7, half(1), picked71, at(LAST_REST, [P, HALF], F32, "rest71"))
+        weave(g32[0, 0], g00_woven, lane(2))
 
-        wr_w = at(W1_RAW + KB, [P, GROUPS, GROUPS, PASS], U32, "wr_w")
-        for b in range(GROUPS):
+        wr_w = {}
+
+        def deal_wr(b, place):
+            wr_w[b] = at(place, [P, GROUPS, PASS], U32, f"wr_w{b}")
             for a in range(GROUPS):
                 nc.scalar.copy(
-                    out=wr_w[:, a, b, :].rearrange("p (t q) -> p q t", t=PACK),
+                    out=wr_w[b][:, a, :].rearrange("p (t q) -> p q t", t=PACK),
                     in_=wr_w_raw[:].bitcast(U32)[:, a, PASS * b : PASS * (b + 1)].rearrange("p (q t) -> p q t", t=PACK),
                 )
 
-        g10_woven = at(state(7), [P, PACK * HALF], BF16, "g10_woven")
+        for b in range(GROUPS):
+            deal_wr(b, W1_RAW + 4 * KB * b)
+        g10_woven = at(WOVEN + 4 * KB, [P, PACK * HALF], BF16, "g10_woven")
 
-        def column_gate(j, u, k, woven=None):
-            h = bank(k, [P, PACK, P], f"h1{j}c{u}")
-            cols = slice(HALF * j + P * u, HALF * j + P * (u + 1))
-            for t in range(PACK):
-                first_product(h[:, t, :], 1, t, cols, t == 0, t == PACK - 1)
-            if woven is None:
-                nc.vector.tensor_tensor(g32[1, j][:, :, lane(u)], h[:], deriv[1][:, :, cols], MULT)
-            else:
-                nc.vector.tensor_tensor(by_word(woven), by_lane(h[:]), by_lane(deriv[1][:, :, cols]), MULT)
-
-        for u in range(PACK):
-            column_gate(0, u, u, g10_woven[:, PASS * u : PASS * (u + 1)])
-        wr_s = at(STAGED, [P, PASS], U8, "wr_s")
+        for u in range(PACK - 1):
+            column_gate(1, 0, u, u, g10_woven[:, PASS * u : PASS * (u + 1)])
+        gate(0, 3, 1, 0)
+        wr_s = at(LAST_REST, [P, PASS], U8, "wr_s")
         nc.vector.tensor_copy(
             out=wr_s[:].rearrange("p (t q) -> p q t", t=PACK),
             in_=wr_s_raw[:].rearrange("p (q t) -> p q t", t=PACK),
         )
-        (g00_q,), calls = quantize(
-            g00_woven, at(G_CODES, [P, HALF], U32, "g00_codes"), "g00", scales=at(WR_SCALES - PASS // 2, [P, HALF], U8, "g00_scales")
-        )
+        column_gate(1, 0, 3, 3, g10_woven[:, 3 * PASS : 4 * PASS])
+        g0_scales = at(WR_SCALES + 64 - KB, [P, S], U8, "g0_scales")
+        (g00_q,), calls = quantize(g00_woven, at(G_CODES, [P, HALF], U32, "g00_codes"), "g00", scales=g0_scales[:, half(0)])
         calls[0]()
         (g10_q,), calls = quantize(
-            g10_woven, at(G_CODES + 2 * KB, [P, HALF], U32, "g10_codes"), "g10",
-            scales=at(WR_SCALES + PASS // 2, [P, HALF], U8, "g10_scales"),
+            g10_woven, at(G_CODES + 2 * KB, [P, HALF], U32, "g10_codes"), "g10", scales=g0_scales[:, half(1)]
         )
         calls[0]()
+        gate(0, 2, 1, 6, staged=at(W1_RAW + 37 * KB // 2, [P, HALF], F32, "h021_staged"))
         quarter = HALF // 2
-        g32[1, 1] = at(state(7) - 2 * KB, [P, PACK, quarter], F32, "g11")
+        g32[1, 1] = at(WR_SCALES + 64, [P, PACK, HALF], F32, "g11")
         g1_woven = [
-            at(place, [P, PACK * HALF], BF16, f"g1_woven{u}") for u, place in enumerate([state(0), state(7) + 2 * KB])
+            at(place, [P, PACK * HALF], BF16, f"g1_woven{u}") for u, place in enumerate([state(1), WOVEN + 8 * KB])
         ]
 
         def quarter_views(a, u):
@@ -300,7 +309,7 @@ def tile_list_dislocation_recurrent_backward_kernel(
         def recurrent_pass(out, a, b, t, j, cols, start, stop):
             codes, scales = moving(a, j, cols)
             nc.tensor.matmul_mx(
-                out=out, lhsT=wr_w[:, a, b, lane(t)].bitcast(E4M3),
+                out=out, lhsT=wr_w[b][:, a, lane(t)].bitcast(E4M3),
                 lhsT_scale=wr_s[4 * (GROUPS * a + b) : P, lane(t)],
                 rhs=codes.bitcast(E4M3), rhs_scale=scales, start=start, stop=stop,
             )
@@ -339,32 +348,38 @@ def tile_list_dislocation_recurrent_backward_kernel(
         def term_tile(place, name):
             return at(place, [P, PACK, P], F32, name)
 
-        b0_woven = at(state(5), [P, 2 * PACK * HALF], BF16, "b0_woven")
+        b0_woven = at(state(4), [P, 2 * PACK * HALF], BF16, "b0_woven")
         for b in range(GROUPS):
             b_woven[b, 0] = side(b0_woven, b)
+        wo_woven = at(LATE_WOVEN, [P, 2 * PACK * HALF], BF16, "wo_woven")
+
+        def weave_wo(u):
+            dst = wo_woven[:].rearrange("p (t a m i) -> p a m i t", t=PACK, a=GROUPS, i=PACK)
+            nc.scalar.copy(
+                out=dst[:, u // 2, P // 2 * (u % 2) : P // 2 * (u % 2 + 1)],
+                in_=wo_parts[u][:].rearrange("p i (m t) -> p m i t", t=PACK),
+            )
+
+        def first_sum(u):
+            summed_on_gpsimd(0, 0, u, [1, 0, 4, 5][u], term_tile(term_place(u), f"term00{u}"))
+
+        weave_wo(0)
+        column_gate(1, 1, 0, 4)
+        column_gate(1, 1, 1, 5)
+        nc.scalar.copy(*quarter_views(1, 0))
+        first_sum(0)
+        first_sum(1)
+        column_gate(1, 1, 3, 1)
+        nc.scalar.copy(out=by_word(g1_woven[1][:, 3 * PASS : 4 * PASS]), in_=by_lane(g32[1, 1][:, :, lane(3)]))
+        first_sum(2)
+        column_gate(1, 1, 2, 0, g1_woven[1][:, 2 * PASS : 3 * PASS])
         for u in range(2):
             nc.scalar.copy(*quarter_views(0, u))
         for u in range(PACK):
-            woven = None if u < 2 else g1_woven[1][:, PASS * u : PASS * (u + 1)]
-            column_gate(1, u, 4 + u, woven)
-            if u == 1:
-                nc.scalar.copy(*quarter_views(1, 0))
-            if u < PACK - 1:
-                summed_on_gpsimd(0, 0, u, u, term_tile(term_place(u), f"term00{u}"))
-        for u in range(PACK - 1):
-            with_repeated_product(1, 0, u, 4 + u)
-        last_term = term_tile(term_place(3), "term003")
-        term_into(last_term[:], 0, 0, 3, 3)
-        with_repeated_product(1, 0, 3, 7)
-        nc.vector.tensor_tensor(words_of(0, 0, lane(3)), by_lane(last_term[:]), by_lane(g32[0, 0][:, :, lane(3)]), ADD)
-        wo_woven = at(LATE_WOVEN, [P, 2 * PACK * HALF], BF16, "wo_woven")
-        for pair in (1, 0):
-            for a in range(GROUPS):
-                lanes = slice(2 * pair, 2 * pair + 2)
-                nc.scalar.copy(
-                    out=wo_woven[:].rearrange("p (t a m i) -> p a m i t", t=PACK, a=GROUPS, i=PACK)[:, a, :, :, lanes],
-                    in_=wo_raw[a][:].rearrange("p i (m t) -> p m i t", t=PACK)[:, :, :, lanes],
-                )
+            with_repeated_product(1, 0, u, [7, 2, 3, 6][u])
+        with_repeated_product(0, 0, 3, 5)
+        for u in range(1, 2 * GROUPS):
+            weave_wo(u)
         for u in range(2):
             (codes,), calls = quantize(
                 g1_woven[u], at(G_CODES + 4 * KB + 2 * KB * u, [P, HALF], U32, f"g1_codes{u}"), f"g1{u}",
@@ -396,19 +411,19 @@ def tile_list_dislocation_recurrent_backward_kernel(
         def empty(dst, t, j, k):
             nc.scalar.copy(out=dst, in_=output_product(t, j, k)[:])
 
-        summed = [[(0, 0)], [(0, 1)], [(1, 0), (1, 1)], [(0, 2)], [(0, 3)]]
-        term_places = [LATE_WOVEN, LATE_WOVEN + 2 * KB, state(4), state(4) + 4 * KB, state(4) + 6 * KB]
+        summed = [[(0, 0)], [(0, 1)], [(1, 0), (1, 1)], [(0, 2), (0, 3)], [(1, 3)]]
+        term_places = [state(4), LATE_WOVEN + 2 * KB, LATE_WOVEN + 4 * KB, state(6), state(6) + 4 * KB]
         terms = [
             at(place, [P, PACK, P * len(run)], F32, f"terms{n}") for n, (place, run) in enumerate(zip(term_places, summed))
         ]
-        staged_places = [state(1), state(1) + 2 * KB, state(1) + 6 * KB, state(1) + 6 * KB]
+        staged_places = [state(1), state(1) + 2 * KB, state(1) + 9 * KB, term_places[4] + KB]
         staged = [at(place, [P, HALF], F32, f"e_first{u}") for u, place in enumerate(staged_places)]
-        weighted_places = [state(1) + 10 * KB, term_places[1], term_places[2]]
+        weighted_places = [state(1) + 12 * KB, term_places[1], term_places[2]]
         weighted = [at(place, [P, HALF], F32, f"y_first{u}") for u, place in enumerate(weighted_places)]
-        sum_places = [state(1) + 12 * KB] + staged_places[:2] + [staged_places[2] - KB, staged_places[2] + KB]
-        b1_woven = at(state(3), [P, 2 * PACK * HALF], BF16, "b1_woven")
-        for b in range(GROUPS):
-            b_woven[b, 1] = side(b1_woven, b)
+        sum_places = [LATE_WOVEN] + staged_places[:2] + [staged_places[2] - 3 * KB]
+        b1_woven = at(state(3), [P, 2 * PACK * HALF - PASS], BF16, "b1_woven")
+        b_woven[0, 1] = side(b1_woven, 0)
+        b_woven[1, 1] = b1_woven[:, PACK * HALF :]
 
         def add_gradient(n):
             (b, u), count = summed[n][0], len(summed[n])
@@ -423,15 +438,14 @@ def tile_list_dislocation_recurrent_backward_kernel(
         def place_first(u):
             nc.vector.tensor_copy(pages[page_order[u]][:].indirect(entries(scatter_list, half(0))), weighted[u][:])
 
-        term_banks = [[0], [1], [2, 3], [4], [5]]
+        term_banks = [[0], [1], [4, 2], [3, 6], [5]]
         empty(staged[0][:], page_order[0], 0, 7)
         for n, run in enumerate(summed):
             for i, (b, u) in enumerate(run):
                 term_into(terms[n][:, :, lane(i)], b, 1, u, term_banks[n][i])
-        for u in range(2, PACK):
-            with_repeated_product(1, 1, u, 4 + u)
+        with_repeated_product(1, 1, 2, 0)
         for u in range(1, PACK - 1):
-            empty(staged[u][:], page_order[u], 0, u - 1)
+            empty(staged[u][:], page_order[u], 0, [1, 4][u - 1])
         add_gradient(0)
         weigh(0)
         place_first(0)
@@ -442,11 +456,16 @@ def tile_list_dislocation_recurrent_backward_kernel(
         weigh(2)
         place_first(2)
         add_gradient(3)
-        add_gradient(4)
+        b1_last = at(staged_places[2] + KB, [P, PASS], BF16, "b1_last")
+        nc.gpsimd.tensor_tensor(by_word(b1_last[:]), by_lane(terms[4][:]), by_lane(g32[1, 1][:, :, lane(3)]), ADD)
         empty(staged[3][:], page_order[3], 0, 7)
-        b1_q, calls = quantize(b1_woven, at(state(0), [P, S], U32, "b1_codes"), "b1")
-        calls[0]()
-        b_q.append(b1_q)
+        b1_codes = at(DERIV + 6 * KB, [P, S], U32, "b1_codes")
+        b1_scales = at(term_places[4], [P, S], U8, "b1_scales")
+        for cols, src in (
+            (half(0), b_woven[0, 1]), (slice(HALF, S - P), b_woven[1, 1]), (slice(S - P, S), b1_last[:])
+        ):
+            nc.vector.quantize_mx(out=b1_codes[:, cols].bitcast(E4M3), scales=b1_scales[:, cols], in_=src)
+        b_q.append([(b1_codes[:, half(b)], b1_scales[:, half(b)]) for b in range(GROUPS)])
 
         def place_weighing(t, src, j):
             nc.vector.tensor_tensor(pages[t][:].indirect(entries(scatter_list, half(j))), src, weights[j][:, t, :], MULT)
@@ -502,14 +521,12 @@ def tile_list_dislocation_recurrent_backward_kernel(
             join_pairs(n, nc.scalar.copy, U32)
 
         words_out = out_1[0].rearrange("p m t -> p (m t)").bitcast(I32)
-        y_codes = at(state(6), [P, T2], U32, "y_codes")
+        y_codes = at(state(5), [P, T2], U32, "y_codes")
         stored = 0
         for n, cols in enumerate(chunks):
             nc.vector.quantize_mx(out=y_codes[:, cols].bitcast(E4M3), scales=y_scales[:, cols], in_=y_woven[n][:])
             if cols.stop != 1536:
                 nc.sync.dma_start(out=words_out[:, stored : cols.stop], in_=y_codes[:, stored : cols.stop].bitcast(I32))
                 stored = cols.stop
-        for q in range(4):
-            nc.scalar.dma_start(
-                out=out_2[0, 4 * q : 4 * q + 4, :].bitcast(I32), in_=y_scales[32 * q : 32 * q + 4, :].bitcast(I32)
-            )
+        for r in range(4):
+            nc.scalar.dma_start(out=out_2[0, r:16:4, :].bitcast(I32), in_=y_scales[r:P:32, :].bitcast(I32))

@@ -26,15 +26,15 @@ GROUPS = H // PASS
 
 KB = 1024
 DERIV = 0
-PAGES = DERIV + 32 * KB
-STATES = PAGES + 24 * KB
+PAGES = DERIV + 34 * KB
+STATES = PAGES + 32 * KB
 TABLE = STATES + 64 * KB
 WR_RAW = TABLE + 8 * KB
 W1_RAW = WR_RAW + 8 * KB
 RING = W1_RAW + 21 * KB
 WOVEN = RING + 12 * KB
-G_CODES = WOVEN + 12 * KB
-TERMS = G_CODES + 8 * KB
+G_CODES = STATES
+TERMS = WOVEN + 10 * KB
 WR_SCALES = TERMS + 9 * KB
 LAST_REST = W1_RAW + 19 * KB // 2
 LATE_WOVEN = W1_RAW + 21 * KB // 2
@@ -106,11 +106,19 @@ def tile_list_dislocation_recurrent_backward_kernel(
         y_scales = keep.tile([P, T2], U8, name="y_scales", align_bytes=64)
         v_w = keep.tile([P, S], U32, name="v_w", align_bytes=64)
         v_s = keep.tile([P, S], U8, name="v_s", align_bytes=64)
-        deriv_rows = [at(DERIV + 16 * KB * a, [P, PACK * S], F32, f"d{a}") for a in range(GROUPS)]
-        deriv = [rows[:].rearrange("p (t c) -> p t c", t=PACK) for rows in deriv_rows]
+        deriv0 = at(DERIV, [P, PACK, S], F32, "d0")
+        deriv1 = [at(DERIV + 16 * KB, [P, (PACK + 1) * HALF], F32, "d10"), at(DERIV + 26 * KB, [P, PACK * HALF], F32, "d11")]
+
+        def deriv(a, cols):
+            if a == 0:
+                return deriv0[:, :, cols]
+            j, first = divmod(cols.start, HALF)
+            rows = deriv1[j][:, 0 : PACK * HALF].rearrange("p (t c) -> p t c", t=PACK)
+            return rows[:, :, first : first + cols.stop - cols.start]
+
         weights = [keep.tile([P, PACK, HALF], F32, name=f"weights{j}", align_bytes=64) for j in range(HALVES)]
         page_order = [2, 0, 1, 3]
-        pages = {t: at(PAGES + 8 * KB * u, [P, T2], F32, f"page{t}") for u, t in enumerate(page_order[:-1])}
+        pages = {t: at(PAGES + 8 * KB * u, [P, T2], F32, f"page{t}") for u, t in enumerate(page_order)}
         wr_s_raw = at(WR_SCALES, [P, PASS], U8, "wr_s_raw")
         nc.vector.memset(tab_s[:].bitcast(I32), 0)
         nc.vector.memset(wr_s_raw[:].bitcast(I32), 0)
@@ -154,17 +162,24 @@ def tile_list_dislocation_recurrent_backward_kernel(
         nc.sync.dma_start(out=wr_w_raw[:], in_=wr_words.rearrange("a p c i -> p a (c i)").bitcast(I32))
         load_scale_rows(1)
         wo_parts = []
-        for u in range(2 * GROUPS):
+
+        def load_wo_part(u):
             raw = at(state(1) + 4 * KB * u, [P, PACK, N // 2], F32, f"wo_part{u}")
             rows = wo[PASS * (u // 2) : PASS * (u // 2 + 1), N // 2 * (u % 2) : N // 2 * (u % 2 + 1)]
             nc.sync.dma_start(out=raw[:], in_=rows.rearrange("(p i) c -> p i c", i=PACK))
             wo_parts.append(raw)
-        nc.sync.dma_start(scatter_list[:], offs2)
-        for j in range(HALVES):
+
+        def load_weights(j):
             for q in range(4):
                 nc.sync.dma_start(
                     out=weights[j][32 * q : 32 * q + 32], in_=wgo.rearrange("(q t) j -> q t j", t=PACK)[:, :, half(j)]
                 )
+
+        for u in range(2 * GROUPS):
+            load_wo_part(u)
+        nc.sync.dma_start(scatter_list[:], offs2)
+        for j in range(HALVES):
+            load_weights(j)
 
         def entries(lst, cols):
             return lst[:, cols.start // 16 : cols.stop // 16]
@@ -173,13 +188,13 @@ def tile_list_dislocation_recurrent_backward_kernel(
         w1_q = {}
 
         def gather_state(k, cols, picked=None):
-            picked = deriv[k // PACK][:, k % PACK, cols] if picked is None else picked[:]
+            picked = deriv(k // PACK, cols)[:, k % PACK, :] if picked is None else picked[:]
             nc.vector.tensor_copy(picked, s_tiles[k][:].indirect(entries(gather_list, cols)))
             return picked
 
         def derivative(k, cols, picked, rest):
             nc.scalar.activation(out=rest[:], in_=picked, func=COPY, scale=-1.0, bias=1.0)
-            nc.gpsimd.tensor_tensor(deriv[k // PACK][:, k % PACK, cols], picked, rest[:], MULT)
+            nc.gpsimd.tensor_tensor(deriv(k // PACK, cols)[:, k % PACK, :], picked, rest[:], MULT)
 
         def whole(k):
             derivative(k, slice(0, S), gather_state(k, slice(0, S)), ring(k, [P, S], F32, f"rest{k}"))
@@ -195,9 +210,9 @@ def tile_list_dislocation_recurrent_backward_kernel(
             first_product(h[:], a, t, half(j), True, True)
             if staged is not None:
                 nc.scalar.copy(out=staged[:], in_=h[:])
-                nc.gpsimd.tensor_tensor(g32[a, j][:, t, :], staged[:], deriv[a][:, t, half(j)], MULT)
+                nc.gpsimd.tensor_tensor(g32[a, j][:, t, :], staged[:], deriv(a, half(j))[:, t, :], MULT)
             else:
-                nc.vector.tensor_tensor(g32[a, j][:, t, :], h[:], deriv[a][:, t, half(j)], MULT)
+                nc.vector.tensor_tensor(g32[a, j][:, t, :], h[:], deriv(a, half(j))[:, t, :], MULT)
 
         def column_gate(a, j, u, k, woven=None):
             h = bank(k, [P, PACK, P], f"h{a}{j}c{u}")
@@ -205,9 +220,9 @@ def tile_list_dislocation_recurrent_backward_kernel(
             for t in range(PACK):
                 first_product(h[:, t, :], a, t, cols, t == 0, t == PACK - 1)
             if woven is None:
-                nc.vector.tensor_tensor(g32[a, j][:, :, lane(u)], h[:], deriv[a][:, :, cols], MULT)
+                nc.vector.tensor_tensor(g32[a, j][:, :, lane(u)], h[:], deriv(a, cols), MULT)
             else:
-                nc.vector.tensor_tensor(by_word(woven), by_lane(h[:]), by_lane(deriv[a][:, :, cols]), MULT)
+                nc.vector.tensor_tensor(by_word(woven), by_lane(h[:]), by_lane(deriv(a, cols)), MULT)
 
         def weave_w1(a, woven):
             for u in range(2):
@@ -217,8 +232,6 @@ def tile_list_dislocation_recurrent_backward_kernel(
                 )
 
         whole(0)
-        pages[page_order[-1]] = at(state(0), [P, T2], F32, "page_last")
-        nc.gpsimd.memset(pages[page_order[-1]][:], 0.0)
         whole(1)
         nc.vector.tensor_copy(v_w[:], tab_w[:].indirect(gather_list[:]))
         nc.vector.tensor_copy(v_s[:], tab_s[:].indirect(gather_list[:]))
@@ -227,19 +240,27 @@ def tile_list_dislocation_recurrent_backward_kernel(
         (w1_q[0],), calls = quantize(w1_woven, keep.tile([P, HALF], U32, name="w1a_codes", align_bytes=64), "w1a")
         calls[0]()
         g32[0, 1] = at(TABLE, [P, PACK, HALF], F32, "g01")
-        for t in range(2):
-            gate(0, t, 1, 4 + t, staged=at([RING + 8 * KB, G_CODES + 4 * KB][t], [P, HALF], F32, f"h0{t}1_staged"))
-        for k in range(2, 6):
-            whole(k)
+        gate(0, 0, 1, 4, staged=at(G_CODES + 4 * KB, [P, HALF], F32, "h001_staged"))
+
+        def by_halves(k):
+            rest = ring(k, [P, S], F32, f"rest{k}")
+            for j in range(HALVES):
+                derivative(k, half(j), gather_state(k, half(j)), rest[:, half(j)])
+
+        by_halves(2)
+        whole(3)
+        by_halves(4)
+        by_halves(5)
         picked60 = gather_state(6, half(0))
         picked61 = gather_state(6, half(1), at(WOVEN, [P, HALF], F32, "picked61"))
         derivative(6, half(0), picked60, at(RING, [P, HALF], F32, "rest60"))
-        w1_woven = deriv[1][:, 3, :].bitcast(BF16)
+        w1_woven = deriv1[0][:, 3 * HALF : 5 * HALF].bitcast(BF16)
         weave_w1(1, w1_woven)
         g32[0, 0] = at(state(6), [P, PACK, HALF - P], F32, "g00")
         for u in range(PACK - 1):
             column_gate(0, 0, u, u)
-        picked70 = gather_state(7, half(0), deriv[1][:, 2, half(1)])
+        gate(0, 1, 1, 0)
+        picked70 = gather_state(7, half(0), deriv(1, half(1))[:, 2, :])
         (w1_q[1],), calls = quantize(
             w1_woven, keep.tile([P, HALF], U32, name="w1b_codes", align_bytes=64), "w1b",
             scales=at(RING, [P, HALF], U8, "w1b_scales"),
@@ -267,7 +288,7 @@ def tile_list_dislocation_recurrent_backward_kernel(
 
         for b in range(GROUPS):
             deal_wr(b, W1_RAW + 4 * KB * b)
-        g10_woven = at(WOVEN + 4 * KB, [P, PACK * HALF], BF16, "g10_woven")
+        g10_woven = at(WOVEN + 2 * KB, [P, PACK * HALF], BF16, "g10_woven")
 
         for u in range(PACK - 1):
             column_gate(1, 0, u, u, g10_woven[:, PASS * u : PASS * (u + 1)])
@@ -289,7 +310,7 @@ def tile_list_dislocation_recurrent_backward_kernel(
         quarter = HALF // 2
         g32[1, 1] = at(WR_SCALES + 64, [P, PACK, HALF], F32, "g11")
         g1_woven = [
-            at(place, [P, PACK * HALF], BF16, f"g1_woven{u}") for u, place in enumerate([state(1), WOVEN + 8 * KB])
+            at(place, [P, PACK * HALF], BF16, f"g1_woven{u}") for u, place in enumerate([state(1), WOVEN + 6 * KB])
         ]
 
         def quarter_views(a, u):
@@ -326,7 +347,7 @@ def tile_list_dislocation_recurrent_backward_kernel(
                         rec[:, t, :], i, b, t, j, lane(u),
                         (i, t) == (0, 0) and not repeated, (i, t) == (GROUPS - 1, PACK - 1),
                     )
-            return rec, deriv[b][:, :, cols]
+            return rec, deriv(b, cols)
 
         b_woven = {}
 
@@ -375,14 +396,14 @@ def tile_list_dislocation_recurrent_backward_kernel(
         column_gate(1, 1, 2, 0, g1_woven[1][:, 2 * PASS : 3 * PASS])
         for u in range(2):
             nc.scalar.copy(*quarter_views(0, u))
+        with_repeated_product(0, 0, 3, 5)
         for u in range(PACK):
             with_repeated_product(1, 0, u, [7, 2, 3, 6][u])
-        with_repeated_product(0, 0, 3, 5)
         for u in range(1, 2 * GROUPS):
             weave_wo(u)
         for u in range(2):
             (codes,), calls = quantize(
-                g1_woven[u], at(G_CODES + 4 * KB + 2 * KB * u, [P, HALF], U32, f"g1_codes{u}"), f"g1{u}",
+                g1_woven[u], at(DERIV + 16 * KB + 2 * KB * u, [P, HALF], U32, f"g1_codes{u}"), f"g1{u}",
                 scales=at(term_place(2) + HALF * u, [P, HALF], U8, f"g1_scales{u}"),
             )
             calls[0]()
@@ -417,7 +438,7 @@ def tile_list_dislocation_recurrent_backward_kernel(
             at(place, [P, PACK, P * len(run)], F32, f"terms{n}") for n, (place, run) in enumerate(zip(term_places, summed))
         ]
         staged_places = [state(1), state(1) + 2 * KB, state(1) + 9 * KB, term_places[4] + KB]
-        staged = [at(place, [P, HALF], F32, f"e_first{u}") for u, place in enumerate(staged_places)]
+        staged = {u: at(staged_places[u], [P, HALF], F32, f"e_first{u}") for u in range(PACK)}
         weighted_places = [state(1) + 12 * KB, term_places[1], term_places[2]]
         weighted = [at(place, [P, HALF], F32, f"y_first{u}") for u, place in enumerate(weighted_places)]
         sum_places = [LATE_WOVEN] + staged_places[:2] + [staged_places[2] - 3 * KB]
@@ -438,14 +459,14 @@ def tile_list_dislocation_recurrent_backward_kernel(
         def place_first(u):
             nc.vector.tensor_copy(pages[page_order[u]][:].indirect(entries(scatter_list, half(0))), weighted[u][:])
 
-        term_banks = [[0], [1], [4, 2], [3, 6], [5]]
+        term_banks = [[0], [1], [4, 2], [1, 4], [2]]
         empty(staged[0][:], page_order[0], 0, 7)
         for n, run in enumerate(summed):
             for i, (b, u) in enumerate(run):
                 term_into(terms[n][:, :, lane(i)], b, 1, u, term_banks[n][i])
-        with_repeated_product(1, 1, 2, 0)
+        with_repeated_product(1, 1, 2, 7)
         for u in range(1, PACK - 1):
-            empty(staged[u][:], page_order[u], 0, [1, 4][u - 1])
+            empty(staged[u][:], page_order[u], 0, [3, 2][u - 1])
         add_gradient(0)
         weigh(0)
         place_first(0)
@@ -458,7 +479,7 @@ def tile_list_dislocation_recurrent_backward_kernel(
         add_gradient(3)
         b1_last = at(staged_places[2] + KB, [P, PASS], BF16, "b1_last")
         nc.gpsimd.tensor_tensor(by_word(b1_last[:]), by_lane(terms[4][:]), by_lane(g32[1, 1][:, :, lane(3)]), ADD)
-        empty(staged[3][:], page_order[3], 0, 7)
+        empty(staged[3][:], page_order[3], 0, 4)
         b1_codes = at(DERIV + 6 * KB, [P, S], U32, "b1_codes")
         b1_scales = at(term_places[4], [P, S], U8, "b1_scales")
         for cols, src in (

@@ -24,6 +24,8 @@ HALF = 512
 HALVES = S // HALF
 GROUPS = H // PASS
 
+SPLIT = 1280
+
 KB = 1024
 DERIV = 0
 PAGES = DERIV + 34 * KB
@@ -96,9 +98,6 @@ def tile_list_dislocation_recurrent_backward_kernel(
 
         def weave(src, dst, cols):
             nc.scalar.copy(out=by_word(dst[:, PACK * cols.start : PACK * cols.stop]), in_=by_lane(src[:, :, cols]))
-
-        def pieces(total, parts):
-            return [slice(total // parts * u, total // parts * (u + 1)) for u in range(parts)]
 
         gather_list = keep.tile([P, S // 16], U16, name="gather_list")
         scatter_list = keep.tile([P, S // 16], U16, name="scatter_list")
@@ -480,7 +479,7 @@ def tile_list_dislocation_recurrent_backward_kernel(
         b1_last = at(staged_places[2] + KB, [P, PASS], BF16, "b1_last")
         nc.gpsimd.tensor_tensor(by_word(b1_last[:]), by_lane(terms[4][:]), by_lane(g32[1, 1][:, :, lane(3)]), ADD)
         empty(staged[3][:], page_order[3], 0, 4)
-        b1_codes = at(DERIV + 6 * KB, [P, S], U32, "b1_codes")
+        b1_codes = at(DERIV + 8 * KB, [P, S], U32, "b1_codes")
         b1_scales = at(term_places[4], [P, S], U8, "b1_scales")
         for cols, src in (
             (half(0), b_woven[0, 1]), (slice(HALF, S - P), b_woven[1, 1]), (slice(S - P, S), b1_last[:])
@@ -495,10 +494,18 @@ def tile_list_dislocation_recurrent_backward_kernel(
 
         first, second, third, last = page_order
         y_rows = out_0.rearrange("(p t) m -> t p m", t=PACK)
-        pairs = [at(DERIV + 8 * KB * u, [P, 2, T2], BF16, f"y_pairs{u}") for u in range(2)]
+        shares = [slice(0, SPLIT), slice(SPLIT, T2)]
+        pairs = [
+            at(DERIV + 8 * cols.start, [P, 2, 2 * (cols.stop - cols.start)], BF16, f"y_pairs{u}")
+            for u, cols in enumerate(shares)
+        ]
+
+        def share_of(cols):
+            u = int(cols.start >= SPLIT)
+            return u, cols.start - shares[u].start
 
         def pair_page(t, cols, copy):
-            u, c0 = divmod(cols.start, T2 // 2)
+            u, c0 = share_of(cols)
             dst = pairs[u][:, t // 2, :].rearrange("p (m l) -> p m l", l=2)
             copy(out=dst[:, c0 : c0 + cols.stop - cols.start, t % 2], in_=pages[t][:, cols])
 
@@ -514,40 +521,40 @@ def tile_list_dislocation_recurrent_backward_kernel(
             place_weighing(t, e32[t], 1)
             nc.sync.dma_start(out=y_rows[t], in_=pages[t][:])
             if t != last:
-                for cols in pieces(T2, 2):
+                for cols in shares:
                     pair_page(t, cols, nc.scalar.copy)
             if t == first:
                 nc.scalar.copy(out=e32[last][:, 0:P], in_=held[:, 0:P])
 
-        chunks = [slice(0, 512), slice(512, 1024), slice(1024, 1536), slice(1536, 1792), slice(1792, 2048)]
-        y_woven = [
-            at(DERIV + 16 * KB + 8 * cols.start, [P, PACK * (cols.stop - cols.start)], BF16, f"y_woven{n}")
-            for n, cols in enumerate(chunks)
-        ]
+        chunks = [slice(HALF * n, HALF * (n + 1)) for n in range(T2 // HALF)]
+        y_woven = [at(DERIV + 16 * KB + 4 * KB * n, [P, PACK * HALF], BF16, f"y_woven{n}") for n in range(len(chunks))]
 
-        def join_pairs(n, copy, word):
-            u, c0 = divmod(chunks[n].start, T2 // 2)
-            src = pairs[u][:].bitcast(word)[:, :, c0 : c0 + chunks[n].stop - chunks[n].start]
+        def join_pairs(cols, copy, word):
+            u, c0 = share_of(cols)
+            n, first_col = divmod(cols.start, HALF)
+            width = cols.stop - cols.start
             copy(
-                out=y_woven[n][:].bitcast(word).rearrange("p (c i u) -> p c u i", u=2, i=4),
-                in_=src.rearrange("p u (c i) -> p c u i", i=4),
+                out=y_woven[n][:, PACK * first_col : PACK * (first_col + width)].bitcast(word).rearrange(
+                    "p (c i u) -> p c u i", u=2, i=4
+                ),
+                in_=pairs[u][:].bitcast(word)[:, :, c0 : c0 + width].rearrange("p u (c i) -> p c u i", i=4),
             )
 
-        for n in range(2):
-            pair_page(last, chunks[n], nc.vector.tensor_copy)
-        for n in range(2):
-            join_pairs(n, nc.vector.tensor_copy, I32)
-        for n in range(2, len(chunks)):
-            pair_page(last, chunks[n], nc.scalar.copy)
-            join_pairs(n, nc.scalar.copy, U32)
+        on_vector = [chunks[0], chunks[1], slice(chunks[2].start, SPLIT)]
+        on_scalar = [chunks[3], slice(SPLIT, chunks[2].stop)]
+        for cols in on_vector:
+            pair_page(last, cols, nc.vector.tensor_copy)
+        for cols in on_vector:
+            join_pairs(cols, nc.vector.tensor_copy, I32)
+        for cols in on_scalar:
+            pair_page(last, cols, nc.scalar.copy)
+            join_pairs(cols, nc.scalar.copy, U32)
 
         words_out = out_1[0].rearrange("p m t -> p (m t)").bitcast(I32)
         y_codes = at(state(5), [P, T2], U32, "y_codes")
-        stored = 0
-        for n, cols in enumerate(chunks):
+        for n in (0, 1, 3, 2):
+            cols = chunks[n]
             nc.vector.quantize_mx(out=y_codes[:, cols].bitcast(E4M3), scales=y_scales[:, cols], in_=y_woven[n][:])
-            if cols.stop != 1536:
-                nc.sync.dma_start(out=words_out[:, stored : cols.stop], in_=y_codes[:, stored : cols.stop].bitcast(I32))
-                stored = cols.stop
+            nc.sync.dma_start(out=words_out[:, cols], in_=y_codes[:, cols].bitcast(I32))
         for r in range(4):
             nc.scalar.dma_start(out=out_2[0, r:16:4, :].bitcast(I32), in_=y_scales[r:P:32, :].bitcast(I32))

from contextlib import ExitStack

import concourse.mybir as mybir

K, H, N, T, S, T2 = 512, 1024, 512, 2048, 1024, 2048
FLOPS = 2 * S * (K * H + H * H + H * N)

F32 = mybir.dt.float32
BF16 = mybir.dt.bfloat16
I32 = mybir.dt.int32
U32 = mybir.dt.uint32
U16 = mybir.dt.uint16
U8 = mybir.dt.uint8
E4M3 = mybir.dt.float8_e4m3fn_x4
E5M2 = mybir.dt.float8_e5m2_x4
MULT = mybir.AluOpType.mult
ADD = mybir.AluOpType.add
COPY = mybir.ActivationFunctionType.Copy

P = 128
PACK = 4
PASS = P * PACK
HALF = 512
HALVES = S // HALF
GROUPS = H // PASS

SPLIT = 1280

KB = 1024
DERIV = 0
PAGES = DERIV + 34 * KB
STATES = PAGES + 32 * KB
TABLE = STATES + 64 * KB
WR_RAW = TABLE + 8 * KB
W1_RAW = WR_RAW + 8 * KB
RING = W1_RAW + 21 * KB
WOVEN = RING + 12 * KB
G_CODES = STATES
TERMS = WOVEN + 10 * KB
WR_SCALES = TERMS + 9 * KB
LAST_REST = W1_RAW + 19 * KB // 2
LATE_WOVEN = W1_RAW + 21 * KB // 2


def tile_list_dislocation_recurrent_backward_kernel(
    tc, tab_words, tab_scales, offs, offs2, sT, w1, wr_words, wr_scales, wo, wgo, out_0, out_1, out_2
):
    nc = tc.nc
    with ExitStack() as ctx:
        keep = ctx.enter_context(tc.tile_pool(name="keep", bufs=1))
        mem = ctx.enter_context(tc.tile_pool(name="mem", bufs=1))
        psum = ctx.enter_context(tc.psum_pool(name="psum", bufs=1))

        def at(place, shape, dtype, name):
            return mem.tile(shape, dtype, name=name, align_bytes=64, offset=place)

        def ring(k, shape, dtype, name):
            return at(RING + 4 * KB * (k % 3), shape, dtype, name)

        def state(k):
            return STATES + 8 * KB * k

        def term_place(k):
            return TERMS + 2 * KB * k

        def bank(k, shape, name):
            return psum.tile(shape, F32, name=name, tag=f"bank{k % 8}", bufs=1)

        def half(j):
            return slice(HALF * j, HALF * (j + 1))

        def lane(t):
            return slice(P * t, P * (t + 1))

        def side(tile, u):
            return tile[:, PACK * HALF * u : PACK * HALF * (u + 1)]

        def quantize(src, codes, name, parts=1, scales=None):
            width = codes.shape[1]
            if scales is None:
                scales = keep.tile([P, width], U8, name=name + "_scales", align_bytes=64)
            calls = []
            for u in range(parts):
                cols = slice(width // parts * u, width // parts * (u + 1))
                calls.append(
                    lambda cols=cols: nc.vector.quantize_mx(
                        out=codes[:, cols].bitcast(E4M3), scales=scales[:, cols],
                        in_=src[:, PACK * cols.start : PACK * cols.stop],
                    )
                )
            return [(codes[:, half(u)], scales[:, half(u)]) for u in range(width // HALF)], calls

        def by_word(dst):
            return dst.rearrange("p (c i t) -> p c t i", t=PACK, i=4)

        def by_lane(src):
            return src.rearrange("p t (c i) -> p c t i", i=4)

        def weave(src, dst, cols):
            nc.scalar.copy(out=by_word(dst[:, PACK * cols.start : PACK * cols.stop]), in_=by_lane(src[:, :, cols]))

        gather_list = keep.tile([P, S // 16], U16, name="gather_list")
        scatter_list = keep.tile([P, S // 16], U16, name="scatter_list")
        tab_s = keep.tile([P, T], U8, name="tab_s", align_bytes=64)
        y_scales = keep.tile([P, T2], U8, name="y_scales", align_bytes=64)
        v_w = keep.tile([P, S], U32, name="v_w", align_bytes=64)
        v_s = keep.tile([P, S], U8, name="v_s", align_bytes=64)
        deriv0 = at(DERIV, [P, PACK, S], F32, "d0")
        deriv1 = [at(DERIV + 16 * KB, [P, (PACK + 1) * HALF], F32, "d10"), at(DERIV + 26 * KB, [P, PACK * HALF], F32, "d11")]

        def deriv(a, cols):
            if a == 0:
                return deriv0[:, :, cols]
            j, first = divmod(cols.start, HALF)
            rows = deriv1[j][:, 0 : PACK * HALF].rearrange("p (t c) -> p t c", t=PACK)
            return rows[:, :, first : first + cols.stop - cols.start]

        weights = [keep.tile([P, PACK, HALF], F32, name=f"weights{j}", align_bytes=64) for j in range(HALVES)]
        page_order = [2, 0, 1, 3]
        pages = {t: at(PAGES + 8 * KB * u, [P, T2], F32, f"page{t}") for u, t in enumerate(page_order)}
        wr_s_raw = at(WR_SCALES, [P, PASS], U8, "wr_s_raw")
        nc.vector.memset(tab_s[:].bitcast(I32), 0)
        nc.vector.memset(wr_s_raw[:].bitcast(I32), 0)
        for page in pages.values():
            nc.vector.memset(page[:], 0.0)

        s_rows = sT.rearrange("(a p t) c -> a t p c", p=P, t=PACK)
        s_tiles = {}

        def load_state(k):
            s_tiles[k] = at(state(k), [P, T], F32, f"s{k}")
            nc.sync.dma_start(out=s_tiles[k][:], in_=s_rows[k // PACK, k % PACK])

        def load_scale_rows(a):
            for q in range(4):
                nc.sync.dma_start(
                    out=wr_s_raw[32 * q + 8 * a : 32 * q + 8 * a + 8, :].bitcast(I32),
                    in_=wr_scales[a, 4 * q : 4 * q + 4, :].bitcast(I32).rearrange("r (b c) -> b r c", b=GROUPS),
                )

        def load_w1_part(u):
            raw = at(W1_RAW + 4 * KB * u, [P, PACK, HALF // 2], F32, f"w1_part{u}")
            cols = slice(HALF // 2 * u, HALF // 2 * (u + 1))
            nc.sync.dma_start(out=raw[:], in_=w1[:, cols].rearrange("(p i) c -> p i c", i=PACK))
            return raw

        load_state(0)
        nc.sync.dma_start(gather_list[:], offs)
        load_state(1)
        tab_w = at(TABLE, [P, T], U32, "tab_w")
        nc.sync.dma_start(out=tab_w[:].bitcast(I32), in_=tab_words[0].rearrange("p t i -> p (t i)").bitcast(I32))
        for r in range(4):
            nc.sync.dma_start(out=tab_s[r:P:32, :].bitcast(I32), in_=tab_scales[0, r:16:4, :].bitcast(I32))
        w1_parts = [load_w1_part(u) for u in range(2)]
        for k in range(2, 7):
            load_state(k)
        load_state(7)
        w1_parts.extend(load_w1_part(u) for u in range(2, 4))
        load_scale_rows(0)
        wr_w_raw = at(WR_RAW, [P, GROUPS, H], I32, "wr_w_raw")
        nc.sync.dma_start(out=wr_w_raw[:], in_=wr_words.rearrange("a p c i -> p a (c i)").bitcast(I32))
        load_scale_rows(1)
        wo_parts = []

        def load_wo_part(u):
            raw = at(state(1) + 4 * KB * u, [P, PACK, N // 2], F32, f"wo_part{u}")
            rows = wo[PASS * (u // 2) : PASS * (u // 2 + 1), N // 2 * (u % 2) : N // 2 * (u % 2 + 1)]
            nc.sync.dma_start(out=raw[:], in_=rows.rearrange("(p i) c -> p i c", i=PACK))
            wo_parts.append(raw)

        def load_weights(j):
            for q in range(4):
                nc.sync.dma_start(
                    out=weights[j][32 * q : 32 * q + 32], in_=wgo.rearrange("(q t) j -> q t j", t=PACK)[:, :, half(j)]
                )

        for u in range(2 * GROUPS):
            load_wo_part(u)
        nc.sync.dma_start(scatter_list[:], offs2)
        for j in range(HALVES):
            load_weights(j)

        def entries(lst, cols):
            return lst[:, cols.start // 16 : cols.stop // 16]

        g32 = {}
        w1_q = {}

        def gather_state(k, cols, picked=None):
            picked = deriv(k // PACK, cols)[:, k % PACK, :] if picked is None else picked[:]
            nc.vector.tensor_copy(picked, s_tiles[k][:].indirect(entries(gather_list, cols)))
            return picked

        def derivative(k, cols, picked, rest):
            nc.scalar.activation(out=rest[:], in_=picked, func=COPY, scale=-1.0, bias=1.0)
            nc.gpsimd.tensor_tensor(deriv(k // PACK, cols)[:, k % PACK, :], picked, rest[:], MULT)

        def whole(k):
            derivative(k, slice(0, S), gather_state(k, slice(0, S)), ring(k, [P, S], F32, f"rest{k}"))

        def first_product(out, a, t, cols, start, stop):
            nc.tensor.matmul_mx(
                out=out, lhsT=w1_q[a][0][:, lane(t)].bitcast(E4M3), lhsT_scale=w1_q[a][1][:, lane(t)],
                rhs=v_w[:, cols].bitcast(E5M2), rhs_scale=v_s[:, cols], start=start, stop=stop,
            )

        def gate(a, t, j, k, staged=None):
            h = bank(k, [P, HALF], f"h{a}{t}{j}")
            first_product(h[:], a, t, half(j), True, True)
            if staged is not None:
                nc.scalar.copy(out=staged[:], in_=h[:])
                nc.gpsimd.tensor_tensor(g32[a, j][:, t, :], staged[:], deriv(a, half(j))[:, t, :], MULT)
            else:
                nc.vector.tensor_tensor(g32[a, j][:, t, :], h[:], deriv(a, half(j))[:, t, :], MULT)

        def column_gate(a, j, u, k, woven=None):
            h = bank(k, [P, PACK, P], f"h{a}{j}c{u}")
            cols = slice(HALF * j + P * u, HALF * j + P * (u + 1))
            for t in range(PACK):
                first_product(h[:, t, :], a, t, cols, t == 0, t == PACK - 1)
            if woven is None:
                nc.vector.tensor_tensor(g32[a, j][:, :, lane(u)], h[:], deriv(a, cols), MULT)
            else:
                nc.vector.tensor_tensor(by_word(woven), by_lane(h[:]), by_lane(deriv(a, cols)), MULT)

        def weave_w1(a, woven):
            for u in range(2):
                nc.scalar.copy(
                    out=woven.rearrange("p (t m i) -> p m i t", t=PACK, i=PACK)[:, P // 2 * u : P // 2 * (u + 1)],
                    in_=w1_parts[2 * a + u][:].rearrange("p i (m t) -> p m i t", t=PACK),
                )

        whole(0)
        whole(1)
        nc.vector.tensor_copy(v_w[:], tab_w[:].indirect(gather_list[:]))
        nc.vector.tensor_copy(v_s[:], tab_s[:].indirect(gather_list[:]))
        w1_woven = at(WOVEN, [P, PACK * HALF], BF16, "w1_woven0")
        weave_w1(0, w1_woven[:])
        (w1_q[0],), calls = quantize(w1_woven, keep.tile([P, HALF], U32, name="w1a_codes", align_bytes=64), "w1a")
        calls[0]()
        g32[0, 1] = at(TABLE, [P, PACK, HALF], F32, "g01")
        gate(0, 0, 1, 4, staged=at(G_CODES + 4 * KB, [P, HALF], F32, "h001_staged"))

        def by_halves(k):
            rest = ring(k, [P, S], F32, f"rest{k}")
            for j in range(HALVES):
                derivative(k, half(j), gather_state(k, half(j)), rest[:, half(j)])

        by_halves(2)
        whole(3)
        by_halves(4)
        by_halves(5)
        picked60 = gather_state(6, half(0))
        picked61 = gather_state(6, half(1), at(WOVEN, [P, HALF], F32, "picked61"))
        derivative(6, half(0), picked60, at(RING, [P, HALF], F32, "rest60"))
        w1_woven = deriv1[0][:, 3 * HALF : 5 * HALF].bitcast(BF16)
        weave_w1(1, w1_woven)
        g32[0, 0] = at(state(6), [P, PACK, HALF - P], F32, "g00")
        for u in range(PACK - 1):
            column_gate(0, 0, u, u)
        gate(0, 1, 1, 0)
        picked70 = gather_state(7, half(0), deriv(1, half(1))[:, 2, :])
        (w1_q[1],), calls = quantize(
            w1_woven, keep.tile([P, HALF], U32, name="w1b_codes", align_bytes=64), "w1b",
            scales=at(RING, [P, HALF], U8, "w1b_scales"),
        )
        calls[0]()
        g00_woven = at(W1_RAW + 15 * KB, [P, PACK * HALF], BF16, "g00_woven")
        column_gate(0, 0, 3, 3, g00_woven[:, 3 * PASS : 4 * PASS])
        picked71 = gather_state(7, half(1), at(W1_RAW + 13 * KB, [P, HALF], F32, "picked71"))
        derivative(7, half(0), picked70, at(W1_RAW + 11 * KB, [P, HALF], F32, "rest70"))
        derivative(6, half(1), picked61, at(W1_RAW + 4 * KB, [P, HALF], F32, "rest61"))
        for u in range(2):
            weave(g32[0, 0], g00_woven, lane(u))
        derivative(7, half(1), picked71, at(LAST_REST, [P, HALF], F32, "rest71"))
        weave(g32[0, 0], g00_woven, lane(2))

        wr_w = {}

        def deal_wr(b, place):
            wr_w[b] = at(place, [P, GROUPS, PASS], U32, f"wr_w{b}")
            for a in range(GROUPS):
                nc.scalar.copy(
                    out=wr_w[b][:, a, :].rearrange("p (t q) -> p q t", t=PACK),
                    in_=wr_w_raw[:].bitcast(U32)[:, a, PASS * b : PASS * (b + 1)].rearrange("p (q t) -> p q t", t=PACK),
                )

        for b in range(GROUPS):
            deal_wr(b, W1_RAW + 4 * KB * b)
        g10_woven = at(WOVEN + 2 * KB, [P, PACK * HALF], BF16, "g10_woven")

        for u in range(PACK - 1):
            column_gate(1, 0, u, u, g10_woven[:, PASS * u : PASS * (u + 1)])
        gate(0, 3, 1, 0)
        wr_s = at(LAST_REST, [P, PASS], U8, "wr_s")
        nc.vector.tensor_copy(
            out=wr_s[:].rearrange("p (t q) -> p q t", t=PACK),
            in_=wr_s_raw[:].rearrange("p (q t) -> p q t", t=PACK),
        )
        column_gate(1, 0, 3, 3, g10_woven[:, 3 * PASS : 4 * PASS])
        g0_scales = at(WR_SCALES + 64 - KB, [P, S], U8, "g0_scales")
        (g00_q,), calls = quantize(g00_woven, at(G_CODES, [P, HALF], U32, "g00_codes"), "g00", scales=g0_scales[:, half(0)])
        calls[0]()
        (g10_q,), calls = quantize(
            g10_woven, at(G_CODES + 2 * KB, [P, HALF], U32, "g10_codes"), "g10", scales=g0_scales[:, half(1)]
        )
        calls[0]()
        gate(0, 2, 1, 6, staged=at(W1_RAW + 37 * KB // 2, [P, HALF], F32, "h021_staged"))
        quarter = HALF // 2
        g32[1, 1] = at(WR_SCALES + 64, [P, PACK, HALF], F32, "g11")
        g1_woven = [
            at(place, [P, PACK * HALF], BF16, f"g1_woven{u}") for u, place in enumerate([state(1), WOVEN + 6 * KB])
        ]

        def quarter_views(a, u):
            dst = by_word(g1_woven[u][:, PACK * quarter * a : PACK * quarter * (a + 1)])
            return dst, by_lane(g32[a, 1][:, :, quarter * u : quarter * (u + 1)])

        g1_q = []

        def moving(a, j, cols):
            if j == 0:
                codes, scales = (g00_q, g10_q)[a]
                return codes[:, cols], scales[:, cols]
            codes, scales = g1_q[cols.start // quarter]
            c0 = quarter * a + cols.start % quarter
            return codes[:, c0 : c0 + P], scales[:, c0 : c0 + P]

        def recurrent_pass(out, a, b, t, j, cols, start, stop):
            codes, scales = moving(a, j, cols)
            nc.tensor.matmul_mx(
                out=out, lhsT=wr_w[b][:, a, lane(t)].bitcast(E4M3),
                lhsT_scale=wr_s[4 * (GROUPS * a + b) : P, lane(t)],
                rhs=codes.bitcast(E4M3), rhs_scale=scales, start=start, stop=stop,
            )

        def recurrent_sum(b, j, u, k, repeated):
            rec = bank(k, [P, PACK, P], f"rec{b}{j}c{u}")
            cols = slice(HALF * j + P * u, HALF * j + P * (u + 1))
            if repeated:
                for t in range(PACK):
                    first_product(rec[:, t, :], b, t, cols, t == 0, False)
            for i in range(GROUPS):
                for t in range(PACK):
                    recurrent_pass(
                        rec[:, t, :], i, b, t, j, lane(u),
                        (i, t) == (0, 0) and not repeated, (i, t) == (GROUPS - 1, PACK - 1),
                    )
            return rec, deriv(b, cols)

        b_woven = {}

        def words_of(b, j, cols):
            return by_word(b_woven[b, j][:, PACK * cols.start : PACK * cols.stop])

        def with_repeated_product(b, j, u, k):
            rec, d = recurrent_sum(b, j, u, k, True)
            nc.vector.tensor_tensor(words_of(b, j, lane(u)), by_lane(rec[:]), by_lane(d), MULT)

        def term_into(term, b, j, u, k):
            rec, d = recurrent_sum(b, j, u, k, False)
            nc.vector.tensor_tensor(term, rec[:], d, MULT)

        def summed_on_gpsimd(b, j, u, k, term):
            term_into(term[:], b, j, u, k)
            nc.gpsimd.tensor_tensor(words_of(b, j, lane(u)), by_lane(term[:]), by_lane(g32[b, j][:, :, lane(u)]), ADD)

        def term_tile(place, name):
            return at(place, [P, PACK, P], F32, name)

        b0_woven = at(state(4), [P, 2 * PACK * HALF], BF16, "b0_woven")
        for b in range(GROUPS):
            b_woven[b, 0] = side(b0_woven, b)
        wo_woven = at(LATE_WOVEN, [P, 2 * PACK * HALF], BF16, "wo_woven")

        def weave_wo(u):
            dst = wo_woven[:].rearrange("p (t a m i) -> p a m i t", t=PACK, a=GROUPS, i=PACK)
            nc.scalar.copy(
                out=dst[:, u // 2, P // 2 * (u % 2) : P // 2 * (u % 2 + 1)],
                in_=wo_parts[u][:].rearrange("p i (m t) -> p m i t", t=PACK),
            )

        def first_sum(u):
            summed_on_gpsimd(0, 0, u, [1, 0, 4, 5][u], term_tile(term_place(u), f"term00{u}"))

        weave_wo(0)
        column_gate(1, 1, 0, 4)
        column_gate(1, 1, 1, 5)
        nc.scalar.copy(*quarter_views(1, 0))
        first_sum(0)
        first_sum(1)
        column_gate(1, 1, 3, 1)
        nc.scalar.copy(out=by_word(g1_woven[1][:, 3 * PASS : 4 * PASS]), in_=by_lane(g32[1, 1][:, :, lane(3)]))
        first_sum(2)
        column_gate(1, 1, 2, 0, g1_woven[1][:, 2 * PASS : 3 * PASS])
        for u in range(2):
            nc.scalar.copy(*quarter_views(0, u))
        with_repeated_product(0, 0, 3, 5)
        for u in range(PACK):
            with_repeated_product(1, 0, u, [7, 2, 3, 6][u])
        for u in range(1, 2 * GROUPS):
            weave_wo(u)
        for u in range(2):
            (codes,), calls = quantize(
                g1_woven[u], at(DERIV + 16 * KB + 2 * KB * u, [P, HALF], U32, f"g1_codes{u}"), f"g1{u}",
                scales=at(term_place(2) + HALF * u, [P, HALF], U8, f"g1_scales{u}"),
            )
            calls[0]()
            g1_q.append(codes)
        b0_q, calls = quantize(b0_woven, ring(1, [P, S], U32, "b0_codes"), "b0")
        calls[0]()
        wo_q, calls = quantize(
            wo_woven, at(term_place(0), [P, S], U32, "wo_codes"), "wo",
            scales=at(term_place(2) + KB, [P, S], U8, "wo_scales"),
        )
        calls[0]()

        b_q = [b0_q]

        def output_product(t, j, k):
            e = bank(k, [P, HALF], f"e{t}{j}")
            for b in range(GROUPS):
                nc.tensor.matmul_mx(
                    out=e[:], lhsT=wo_q[t // 2][0][:, lane(2 * (t % 2) + b)].bitcast(E4M3),
                    lhsT_scale=wo_q[t // 2][1][:, lane(2 * (t % 2) + b)],
                    rhs=b_q[j][b][0].bitcast(E4M3), rhs_scale=b_q[j][b][1],
                    start=(b == 0), stop=(b == GROUPS - 1),
                )
            return e

        def empty(dst, t, j, k):
            nc.scalar.copy(out=dst, in_=output_product(t, j, k)[:])

        summed = [[(0, 0)], [(0, 1)], [(1, 0), (1, 1)], [(0, 2), (0, 3)], [(1, 3)]]
        term_places = [state(4), LATE_WOVEN + 2 * KB, LATE_WOVEN + 4 * KB, state(6), state(6) + 4 * KB]
        terms = [
            at(place, [P, PACK, P * len(run)], F32, f"terms{n}") for n, (place, run) in enumerate(zip(term_places, summed))
        ]
        staged_places = [state(1), state(1) + 2 * KB, state(1) + 9 * KB, term_places[4] + KB]
        staged = {u: at(staged_places[u], [P, HALF], F32, f"e_first{u}") for u in range(PACK)}
        weighted_places = [state(1) + 12 * KB, term_places[1], term_places[2]]
        weighted = [at(place, [P, HALF], F32, f"y_first{u}") for u, place in enumerate(weighted_places)]
        sum_places = [LATE_WOVEN] + staged_places[:2] + [staged_places[2] - 3 * KB]
        b1_woven = at(state(3), [P, 2 * PACK * HALF - PASS], BF16, "b1_woven")
        b_woven[0, 1] = side(b1_woven, 0)
        b_woven[1, 1] = b1_woven[:, PACK * HALF :]

        def add_gradient(n):
            (b, u), count = summed[n][0], len(summed[n])
            total = at(sum_places[n], [P, PACK, P * count], F32, f"b32_{n}")
            nc.gpsimd.tensor_tensor(total[:], terms[n][:], g32[b, 1][:, :, P * u : P * (u + count)], ADD)
            for i in range(count):
                nc.scalar.copy(out=words_of(b, 1, lane(u + i)), in_=by_lane(total[:, :, lane(i)]))

        def weigh(u):
            nc.gpsimd.tensor_tensor(weighted[u][:], staged[u][:], weights[0][:, page_order[u], :], MULT)

        def place_first(u):
            nc.vector.tensor_copy(pages[page_order[u]][:].indirect(entries(scatter_list, half(0))), weighted[u][:])

        term_banks = [[0], [1], [4, 2], [1, 4], [2]]
        empty(staged[0][:], page_order[0], 0, 7)
        for n, run in enumerate(summed):
            for i, (b, u) in enumerate(run):
                term_into(terms[n][:, :, lane(i)], b, 1, u, term_banks[n][i])
        with_repeated_product(1, 1, 2, 7)
        for u in range(1, PACK - 1):
            empty(staged[u][:], page_order[u], 0, [3, 2][u - 1])
        add_gradient(0)
        weigh(0)
        place_first(0)
        add_gradient(1)
        weigh(1)
        place_first(1)
        add_gradient(2)
        weigh(2)
        place_first(2)
        add_gradient(3)
        b1_last = at(staged_places[2] + KB, [P, PASS], BF16, "b1_last")
        nc.gpsimd.tensor_tensor(by_word(b1_last[:]), by_lane(terms[4][:]), by_lane(g32[1, 1][:, :, lane(3)]), ADD)
        empty(staged[3][:], page_order[3], 0, 4)
        b1_codes = at(DERIV + 8 * KB, [P, S], U32, "b1_codes")
        b1_scales = at(term_places[4], [P, S], U8, "b1_scales")
        for cols, src in (
            (half(0), b_woven[0, 1]), (slice(HALF, S - P), b_woven[1, 1]), (slice(S - P, S), b1_last[:])
        ):
            nc.vector.quantize_mx(out=b1_codes[:, cols].bitcast(E4M3), scales=b1_scales[:, cols], in_=src)
        b_q.append([(b1_codes[:, half(b)], b1_scales[:, half(b)]) for b in range(GROUPS)])

        def place_weighing(t, src, j):
            nc.vector.tensor_tensor(pages[t][:].indirect(entries(scatter_list, half(j))), src, weights[j][:, t, :], MULT)

        place_weighing(page_order[3], staged[3][:], 0)

        first, second, third, last = page_order
        y_rows = out_0.rearrange("(p t) m -> t p m", t=PACK)
        shares = [slice(0, SPLIT), slice(SPLIT, T2)]
        pairs = [
            at(DERIV + 8 * cols.start, [P, 2, 2 * (cols.stop - cols.start)], BF16, f"y_pairs{u}")
            for u, cols in enumerate(shares)
        ]

        def share_of(cols):
            u = int(cols.start >= SPLIT)
            return u, cols.start - shares[u].start

        def pair_page(t, cols, copy):
            u, c0 = share_of(cols)
            dst = pairs[u][:, t // 2, :].rearrange("p (m l) -> p m l", l=2)
            copy(out=dst[:, c0 : c0 + cols.stop - cols.start, t % 2], in_=pages[t][:, cols])

        chained = at(state(7), [P, 2 * HALF - P], F32, "e_chained")
        e32 = {first: chained[:, 0:HALF], last: chained[:, HALF - P : 2 * HALF - P]}
        empty(e32[first], first, 1, 0)
        for u, t in enumerate((second, third)):
            e32[t] = at(state(7) + 4 * KB + 2 * KB * u, [P, HALF], F32, f"e_second{t}")[:]
            empty(e32[t], t, 1, [6, 7][u])
        held = output_product(last, 1, 2)
        nc.scalar.copy(out=e32[last][:, P:HALF], in_=held[:, P:HALF])
        for t in page_order:
            place_weighing(t, e32[t], 1)
            nc.sync.dma_start(out=y_rows[t], in_=pages[t][:])
            if t != last:
                for cols in shares:
                    pair_page(t, cols, nc.scalar.copy)
            if t == first:
                nc.scalar.copy(out=e32[last][:, 0:P], in_=held[:, 0:P])

        chunks = [slice(HALF * n, HALF * (n + 1)) for n in range(T2 // HALF)]
        y_woven = [at(DERIV + 16 * KB + 4 * KB * n, [P, PACK * HALF], BF16, f"y_woven{n}") for n in range(len(chunks))]

        def join_pairs(cols, copy, word):
            u, c0 = share_of(cols)
            n, first_col = divmod(cols.start, HALF)
            width = cols.stop - cols.start
            copy(
                out=y_woven[n][:, PACK * first_col : PACK * (first_col + width)].bitcast(word).rearrange(
                    "p (c i u) -> p c u i", u=2, i=4
                ),
                in_=pairs[u][:].bitcast(word)[:, :, c0 : c0 + width].rearrange("p u (c i) -> p c u i", i=4),
            )

        on_vector = [chunks[0], chunks[1], slice(chunks[2].start, SPLIT)]
        on_scalar = [chunks[3], slice(SPLIT, chunks[2].stop)]
        for cols in on_vector:
            pair_page(last, cols, nc.vector.tensor_copy)
        for cols in on_vector:
            join_pairs(cols, nc.vector.tensor_copy, I32)
        for cols in on_scalar:
            pair_page(last, cols, nc.scalar.copy)
            join_pairs(cols, nc.scalar.copy, U32)

        words_out = out_1[0].rearrange("p m t -> p (m t)").bitcast(I32)
        y_codes = at(state(5), [P, T2], U32, "y_codes")
        for n in (0, 1, 3, 2):
            cols = chunks[n]
            nc.vector.quantize_mx(out=y_codes[:, cols].bitcast(E4M3), scales=y_scales[:, cols], in_=y_woven[n][:])
            nc.sync.dma_start(out=words_out[:, cols], in_=y_codes[:, cols].bitcast(I32))
        for r in range(4):
            nc.scalar.dma_start(out=out_2[0, r:16:4, :].bitcast(I32), in_=y_scales[r:P:32, :].bitcast(I32))
